import numpy as np
import ml_dtypes


def mxq(x, axis, fmt="e4m3"):
    dtype, down = {"e4m3": (ml_dtypes.float8_e4m3fn, 7), "e5m2": (ml_dtypes.float8_e5m2, 14)}[fmt]
    v = np.moveaxis(np.asarray(x, np.float32).astype(ml_dtypes.bfloat16).astype(np.float64), axis, -1)
    blocks = v.reshape(v.shape[:-1] + (-1, 32))
    amax = np.abs(blocks).max(-1, keepdims=True)
    byte = np.maximum(np.where(amax > 0, np.frexp(amax)[1] - 1 + 127, 0) - down, 1)
    scale = np.exp2(byte - 127.0)
    codes = (blocks / scale).astype(np.float32).astype(dtype).astype(np.float64)
    return np.moveaxis((codes * scale).reshape(v.shape), -1, axis)


WIDE = False


def mx_kscale(k):
    if not WIDE:
        return np.ones(k)
    levels = np.array([10, -10, 5, -5, 0])
    if k % 512:
        return np.exp2(np.random.permutation(np.resize(levels, k // 32))).repeat(32)
    a = np.empty((k // 512, 16))
    for p in range(k // 512):
        a[p, :8] = np.random.permutation(np.resize(levels, 8))
        for g in range(8):
            far = levels[np.abs(levels - a[p, g]) >= 10]
            a[p, g + 8] = far[np.random.randint(len(far))]
    return np.exp2(a.ravel()).repeat(32)


def f64(x):
    return np.asarray(x).astype(np.float64)


def striped(idx):
    return np.tile(idx.reshape(-1, 16).T, (8, 1)).astype(np.uint16)


def unstriped(offs):
    return offs[:16].T.reshape(-1).astype(np.int64)


E2M1 = np.array([0.0, 0.5, 1.0, 1.5, 2.0, 3.0, 4.0, 6.0, -0.0, -0.5, -1.0, -1.5, -2.0, -3.0, -4.0, -6.0])


def pack_weight(w, fmt):
    k, n = w.shape
    w = f64(np.asarray(w, np.float32).astype(ml_dtypes.bfloat16)).reshape(k // 32, 32, n)
    amax = np.abs(w).max(1)
    if fmt == "e4m3":
        byte = np.frexp(amax)[1] - 1 + 127 - 7
    else:
        mant, ex = np.frexp(amax / 6.0)
        byte = np.where(mant > 0.5, ex, ex - 1) + 127
    byte = np.clip(np.where(amax > 0, byte, 1), 1, 254)
    scaled = (w * np.exp2(127.0 - byte)[:, None, :]).reshape(k, n).astype(np.float32)
    by_word = np.ascontiguousarray(scaled.reshape(k // 512, 128, 4, n).transpose(0, 1, 3, 2))
    if fmt == "e4m3":
        words = by_word.astype(ml_dtypes.float8_e4m3fn).view(np.uint8)
    else:
        c = by_word.astype(ml_dtypes.float4_e2m1fn).view(np.uint8) & 0xF
        words = (c[..., 0::2] | (c[..., 1::2] << 4)).reshape(k // 512, 128, 2 * n)
    return np.ascontiguousarray(words), np.ascontiguousarray(byte.astype(np.uint8).reshape(k // 512, 16, n))


def unpack_weight(words, scales, fmt):
    g, _, n = scales.shape
    words = np.ascontiguousarray(words).reshape(g, 128, n, -1)
    if fmt == "e4m3":
        vals = words.view(ml_dtypes.float8_e4m3fn).astype(np.float64)
    else:
        nib = np.empty((g, 128, n, 4), np.uint8)
        nib[..., 0::2] = words & 0xF
        nib[..., 1::2] = words >> 4
        vals = E2M1[nib]
    vals = vals * np.repeat(np.exp2(scales.astype(np.float64) - 127.0), 8, axis=1)[..., None]
    return vals.transpose(0, 1, 3, 2).reshape(g * 512, n)


def gelu(v):
    return 0.5 * v * (1.0 + np.tanh(np.sqrt(2.0 / np.pi) * (v + 0.044715 * v**3)))


K, T, S, H, N, T2, P = 1536, 4096, 1024, 512, 384, 2048, 1024

def setup_inputs():
    n = np.random.standard_normal
    s = mx_kscale(K)[:, None]
    u = mx_kscale(H)[:, None]
    tab_words, tab_scales = pack_weight(n((K, T)) * s, "e4m3")
    w1_words, w1_scales = pack_weight(n((K, H)) / np.sqrt(K) / s, "e2m1")
    w3_words, w3_scales = pack_weight(n((H, N)) / np.sqrt(H) / u, "e4m3")
    return {
        "tab_words": tab_words, "tab_scales": tab_scales,
        "offs": striped(np.random.permutation(T)[:S]),
        "w1_words": w1_words, "w1_scales": w1_scales,
        "w2": (n((K, H)) / np.sqrt(K) / s).astype(np.float32),
        "curve": (0.6 * n(H)).astype(np.float32),
        "gain": (np.random.uniform(0.8, 1.6, H) * u[:, 0]).astype(np.float32),
        "offs2": striped(np.random.permutation(T2)[:S]),
        "wgs": np.exp(0.3 * n((128, S))).astype(np.float32),
        "base": (n((H, T2)) * u).astype(np.float32),
        "w3_words": w3_words, "w3_scales": w3_scales,
        "offs3": striped(np.random.permutation(T2)[:P]),
        "limit": np.random.uniform(0.3, 1.2, N).astype(np.float32),
        "offs4": striped(np.random.permutation(T2)[:P]),
        "wgo": np.exp(0.3 * n((128, P))).astype(np.float32),
    }

def reference(tab_words, tab_scales, offs, w1_words, w1_scales, w2, curve, gain, offs2, wgs, base, w3_words, w3_scales, offs3, limit, offs4, wgo):
    v = unpack_weight(tab_words, tab_scales, "e4m3")[:, unstriped(offs)]
    a = unpack_weight(w1_words, w1_scales, "e2m1").T @ v
    b = mxq(f64(w2), 0, "e4m3").T @ v
    h = f64(gain)[:, None] * np.tanh(a + f64(curve)[:, None] * np.square(b))
    page = np.zeros((H, T2))
    page[:, unstriped(offs2)] = np.tile(f64(wgs), (H // 128, 1)) * h
    z = mxq(page + f64(base), 0, "e4m3")
    y = unpack_weight(w3_words, w3_scales, "e4m3").T @ z
    x = np.abs(y[:, unstriped(offs3)]) - f64(limit)[:, None]
    out = np.zeros((N, T2))
    out[:, unstriped(offs4)] = np.tile(f64(wgo), (N // 128, 1)) * x
    return out

@@ -1,0 +1,267 @@
+from contextlib import ExitStack
+
+import concourse.mybir as mybir
+from concourse.masks import make_identity
+
+K, T, S, H, N, T2 = 1536, 4096, 1024, 512, 384, 2048
+FLOPS = 2 * 2 * K * H * S + 2 * H * N * T2
+
+F32 = mybir.dt.float32
+BF16 = mybir.dt.bfloat16
+I32 = mybir.dt.int32
+U32 = mybir.dt.uint32
+U16 = mybir.dt.uint16
+U8 = mybir.dt.uint8
+FP8X4 = mybir.dt.float8_e4m3fn_x4
+FP4X4 = mybir.dt.float4_e2m1fn_x4
+ACT = mybir.ActivationFunctionType
+ALU = mybir.AluOpType
+
+P = 128
+PASSES = K // 512
+ROW_TILES = H // P
+OUT_TILES = N // P
+HALF = 512
+HALVES = S // HALF
+LIST_COLS = HALF // 16
+CHUNK = 512
+CHUNKS = T2 // CHUNK
+SUBS = CHUNK // P
+QUADS = 4
+SHIFT_ROWS = 112
+
+
+def tile_list_pump_dock_check_kernel(tc, tab_words, tab_scales, offs, w1_words, w1_scales, w2, curve, gain,
+                                               offs2, wgs, base, w3_words, w3_scales, offs3, limit, offs4, wgo, out):
+    nc = tc.nc
+    with ExitStack() as ctx:
+        lists = ctx.enter_context(tc.tile_pool(name="lists", bufs=1))
+        keep = ctx.enter_context(tc.tile_pool(name="keep", bufs=1))
+        ring = ctx.enter_context(tc.tile_pool(name="ring", bufs=2))
+        psum = ctx.enter_context(tc.psum_pool(name="psum", bufs=1))
+
+        def bank(i, name):
+            return psum.tile([P, 512], F32, name=name, tag="bank%d" % i)
+
+        def load_list(src, name):
+            tile = lists.tile([P, S // 16], U16, name=name)
+            nc.sync.dma_start(tile[:], src)
+            return tile
+
+        def half_of(tile, h):
+            return tile[:, h * LIST_COLS : (h + 1) * LIST_COLS]
+
+        def cols(i, width):
+            return slice(i * width, (i + 1) * width)
+
+        def load_table(a):
+            tile = keep.tile([P, T], U32, name="table%d" % a, tag="big%d" % a, align_bytes=64)
+            nc.sync.dma_start(tile[:].bitcast(I32), tab_words[a].rearrange("p t i -> p (t i)").bitcast(I32))
+            return tile
+
+        def load_w2(t):
+            tile = keep.tile([P, PASSES, 4, P], F32, name="w2_raw%d" % t, tag="raw%d" % t, align_bytes=64)
+            for a in range(PASSES):
+                nc.sync.dma_start(tile[:, a, :, :], w2[cols(a, 512), cols(t, P)].rearrange("(p j) c -> p j c", j=4))
+            return tile
+
+        tab_scale_rows = keep.tile([P, T], U8, name="tab_scale_rows", align_bytes=64)
+        nc.vector.memset(tab_scale_rows[:].bitcast(I32), 0)
+        vec_rows = keep.tile([P, P], F32, name="vec_rows")
+        nc.vector.memset(vec_rows[:], 0.0)
+        w1_sc = keep.tile([P, PASSES, H], U8, name="w1_sc", align_bytes=64)
+        nc.vector.memset(w1_sc[:].rearrange("p a c -> p (a c)").bitcast(I32), 0)
+        w3_sc = keep.tile([P, N], U8, name="w3_sc", align_bytes=64)
+        nc.vector.memset(w3_sc[:].bitcast(I32), 0)
+        v_sc = [keep.tile([P, S], U8, name="v_sc%d" % a, align_bytes=64) for a in range(PASSES)]
+        for a in range(1, PASSES):
+            nc.vector.memset(v_sc[a][:].bitcast(I32), 0)
+
+        ident = keep.tile([P, P], F32, name="ident")
+        make_identity(nc, ident[:])
+        warm = keep.tile([P, 1], F32, name="warm")
+        nc.scalar.activation(warm[:], ident[:, 0:1], ACT.Tanh)
+        for q in range(QUADS):
+            nc.gpsimd.dma_start(tab_scale_rows[32 * q : 32 * q + 4 * PASSES, :].bitcast(I32),
+                                tab_scales[:, 4 * q : 4 * q + 4, :].bitcast(I32))
+        for q in range(QUADS):
+            nc.gpsimd.dma_start(w1_sc[32 * q : 32 * q + 4, :, :].bitcast(I32),
+                                w1_scales[:, 4 * q : 4 * q + 4, :].rearrange("a r c -> r a c").bitcast(I32))
+        offs_sb = load_list(offs, "offs_sb")
+        table = [load_table(0)]
+        nc.sync.dma_start(vec_rows[0:4, :], curve.rearrange("(t p) -> t p", p=P))
+        nc.sync.dma_start(vec_rows[4:8, :], gain.rearrange("(t p) -> t p", p=P))
+        nc.sync.dma_start(vec_rows[8:11, :], limit.rearrange("(t p) -> t p", p=P))
+        table.append(load_table(1))
+        w2_raw = [load_w2(0)]
+        w1_sb = keep.tile([P, PASSES, 2 * H], U8, name="w1_sb", align_bytes=64)
+        nc.sync.dma_start(w1_sb[:].bitcast(I32), w1_words.rearrange("a p c -> p a c").bitcast(I32))
+        table.append(load_table(2))
+        wgs_sb = [keep.tile([P, HALF], F32, name="wgs_sb%d" % h) for h in range(HALVES)]
+        nc.sync.dma_start(wgs_sb[0][:], wgs[:, cols(0, HALF)])
+        offs2_sb = load_list(offs2, "offs2_sb")
+        w2_raw.append(load_w2(1))
+        nc.sync.dma_start(wgs_sb[1][:], wgs[:, cols(1, HALF)])
+        for t in range(2, ROW_TILES):
+            w2_raw.append(load_w2(t))
+        base_sb = []
+        for t in range(ROW_TILES):
+            tile = keep.tile([P, T2], F32, name="base%d" % t)
+            nc.sync.dma_start(tile[:], base[cols(t, P), :])
+            base_sb.append(tile)
+        w3_sb = keep.tile([P, N], U32, name="w3_sb", align_bytes=64)
+        nc.sync.dma_start(w3_sb[:].bitcast(I32), w3_words[0].rearrange("p c i -> p (c i)").bitcast(I32))
+        offs3_sb = load_list(offs3, "offs3_sb")
+        offs4_sb = load_list(offs4, "offs4_sb")
+        wgo_sb = keep.tile([P, S], F32, name="wgo_sb")
+        nc.sync.dma_start(wgo_sb[:], wgo)
+
+        vec_bank = bank(7, "vec_bank")
+        nc.tensor.transpose(vec_bank[:, 0:P], vec_rows[:], ident[:])
+        vecs = keep.tile([P, 8], F32, name="vecs")
+        nc.scalar.copy(vecs[:], vec_bank[:, 0:8])
+        neg_limit = keep.tile([P, OUT_TILES], F32, name="neg_limit")
+        nc.scalar.mul(neg_limit[:], vec_bank[:, 8:11], -1.0)
+
+        pages = [keep.tile([P, T2], F32, name="page%d" % t, tag="page%d" % t) for t in range(ROW_TILES)]
+        nc.vector.memset(pages[0][:], 0.0)
+
+        nc.vector.tensor_copy(v_sc[0][:], tab_scale_rows[:].indirect(offs_sb[:]))
+        for a in range(1, PASSES):
+            nc.gpsimd.dma_start(v_sc[a][0:SHIFT_ROWS, :].bitcast(I32),
+                                v_sc[0][4 * a : 4 * a + SHIFT_ROWS, :].bitcast(I32))
+        for t in range(1, ROW_TILES):
+            nc.gpsimd.memset(pages[t][:], 0.0)
+        for q in range(QUADS):
+            nc.gpsimd.dma_start(w3_sc[32 * q : 32 * q + 4, :].bitcast(I32), w3_scales[0, 4 * q : 4 * q + 4, :].bitcast(I32))
+
+        def quantize_w2(t):
+            grouped = ring.tile([P, PASSES, P, 4], BF16, name="w2_grouped", align_bytes=64)
+            nc.scalar.copy(grouped[:], w2_raw[t][:].rearrange("p a j c -> p a c j"))
+            codes = keep.tile([P, PASSES * P], U32, name="w2_codes%d" % t, align_bytes=64)
+            scales = keep.tile([P, PASSES * P], U8, name="w2_scales%d" % t, align_bytes=64)
+            flat = grouped[:].rearrange("p a c j -> p (a c j)")
+            for lo, hi in ((0, 2 * P), (2 * P, 3 * P)):
+                nc.vector.quantize_mx(out=codes[:, lo:hi].bitcast(FP8X4), scales=scales[:, lo:hi], in_=flat[:, 4 * lo : 4 * hi])
+            return codes, scales
+
+        v = []
+        w2_q = []
+        for a in range(PASSES):
+            v.append([])
+            for h in range(HALVES):
+                tile = keep.tile([P, HALF], U32, name="v%d_%d" % (a, h), tag="words%d" % (a * HALVES + h), align_bytes=64)
+                nc.vector.tensor_copy(tile[:], table[a][:].indirect(half_of(offs_sb, h)))
+                v[a].append(tile)
+            if a == 0:
+                w2_q.append(quantize_w2(0))
+
+        def weight_tile(t, h):
+            later = t + 1 < ROW_TILES and h == (1 if t == 0 else 0)
+            if later:
+                tile = keep.tile([P, HALF], F32, name="gw%d_%d" % (t, h), tag="raw%d" % (t + 1), align_bytes=64)
+            else:
+                tile = ring.tile([P, HALF], F32, name="gw")
+            nc.scalar.mul(tile[:], wgs_sb[h][:], vecs[:, 4 + t : 5 + t])
+            return tile
+
+        z_t = []
+
+        def stage_one(t):
+            codes, scales = w2_q[t]
+            hs = []
+            for h in range(HALVES):
+                b_bank = bank(4 * (t % 2) + 2 * h, "b_bank")
+                a_bank = bank(4 * (t % 2) + 2 * h + 1, "a_bank")
+                for a in range(PASSES):
+                    nc.tensor.matmul_mx(out=b_bank[:], lhsT=codes[:, cols(a, P)].bitcast(FP8X4), lhsT_scale=scales[:, cols(a, P)],
+                                        rhs=v[a][h][:].bitcast(FP8X4), rhs_scale=v_sc[a][:, cols(h, HALF)],
+                                        start=(a == 0), stop=(a == PASSES - 1))
+                for a in range(PASSES):
+                    nc.tensor.matmul_mx(out=a_bank[:], lhsT=w1_sb[:, a, cols(t, 2 * P)].bitcast(FP4X4), lhsT_scale=w1_sc[:, a, cols(t, P)],
+                                        rhs=v[a][h][:].bitcast(FP8X4), rhs_scale=v_sc[a][:, cols(h, HALF)],
+                                        start=(a == 0), stop=(a == PASSES - 1))
+                sq = ring.tile([P, HALF], F32, name="sq", tag="s0")
+                nc.scalar.activation(sq[:], b_bank[:], ACT.Square)
+                u = ring.tile([P, HALF], F32, name="u", tag="s1")
+                nc.vector.scalar_tensor_tensor(u[:], sq[:], vecs[:, t : t + 1], a_bank[:], ALU.mult, ALU.add)
+                th = ring.tile([P, HALF], F32, name="th", tag="s2")
+                nc.scalar.activation(th[:], u[:], ACT.Tanh)
+                hs.append(th)
+            for h in range(HALVES):
+                if t + 1 < ROW_TILES and h == (1 if t == 0 else 0):
+                    w2_q.append(quantize_w2(t + 1))
+                gw = weight_tile(t, h)
+                nc.vector.tensor_tensor(pages[t][:].indirect(half_of(offs2_sb, h)), hs[h][:], gw[:], ALU.mult)
+
+        def add_base(t, first_bank):
+            banks = [bank(first_bank + c, "sum_bank") for c in range(CHUNKS)]
+            for src, is_page in ((base_sb[t], False), (pages[t], True)):
+                for c in range(CHUNKS):
+                    for s in range(SUBS):
+                        nc.tensor.matmul(banks[c][:, cols(s, P)], src[:, cols(c * SUBS + s, P)], ident[:], is_transpose=True,
+                                         start=(s == 0 and not is_page), stop=(s == SUBS - 1 and is_page))
+            for c in range(CHUNKS):
+                nc.scalar.copy(z_t[c][:, :, :, cols(t, 32), :],
+                               banks[c][:].rearrange("q (s p u e) -> q s u p e", s=SUBS, u=2, e=2))
+
+        for c in range(CHUNKS):
+            z_t.append(keep.tile([P, SUBS, 2, P, 2], BF16, name="z_t%d" % c, align_bytes=64))
+        for t in range(ROW_TILES):
+            stage_one(t)
+            if t >= 2:
+                add_base(t - 2, 4 * ((t - 1) % 2))
+        for t in range(ROW_TILES - 2, ROW_TILES):
+            add_base(t, 4 * ((t + 1) % 2))
+
+        outs = []
+        for n in range(OUT_TILES):
+            tile = keep.tile([P, T2], F32, name="out_page%d" % n, tag="page%d" % n)
+            nc.gpsimd.memset(tile[:], 0.0)
+            outs.append(tile)
+
+        y = [keep.tile([P, T2], F32, name="y%d" % n, tag="big%d" % n, align_bytes=64) for n in range(OUT_TILES)]
+        z_q = []
+
+        def product(n, c, bank_no):
+            codes, scales = z_q[c]
+            y_bank = bank(bank_no, "y_bank")
+            nc.tensor.matmul_mx(out=y_bank[:], lhsT=w3_sb[:, cols(n, P)].bitcast(FP8X4), lhsT_scale=w3_sc[:, cols(n, P)],
+                                rhs=codes[:].bitcast(FP8X4), rhs_scale=scales[:], start=True, stop=True)
+            nc.scalar.copy(y[n][:, cols(c, CHUNK)], y_bank[:])
+
+        for c in range(CHUNKS):
+            words = z_t[c][:].rearrange("q s u p e -> q (s u p e)").bitcast(F32)
+            codes = keep.tile([P, CHUNK], U32, name="z_codes%d" % c, tag="words%d" % c, align_bytes=64)
+            scales = keep.tile([P, CHUNK], U8, name="z_scales%d" % c, align_bytes=64)
+            for h in range(2):
+                back = bank(4 + (2 * c + h) % 4, "back_bank")
+                for i in range(4):
+                    nc.tensor.transpose(back[:, cols(i, P)], words[:, cols(4 * h + i, P)], ident[:])
+                z = ring.tile([P, 2 * P * 4], BF16, name="z", tag="z%d" % h, align_bytes=64)
+                z_words = z[:].bitcast(F32).rearrange("p (s q u) -> p s q u", s=2, u=2)
+                src = back[:].rearrange("p (s u q) -> p s q u", s=2, u=2)
+                if h == 0 or c % 2 == 1:
+                    nc.vector.tensor_copy(z_words, src)
+                else:
+                    nc.scalar.copy(z_words, src)
+                nc.vector.quantize_mx(out=codes[:, cols(h, 2 * P)].bitcast(FP8X4), scales=scales[:, cols(h, 2 * P)], in_=z[:])
+            z_q.append((codes, scales))
+            product(0, c, c)
+
+        for n in range(OUT_TILES):
+            xs = []
+            for h in range(HALVES):
+                picked = ring.tile([P, HALF], F32, name="picked", tag="s0")
+                nc.vector.tensor_copy(picked[:], y[n][:].indirect(half_of(offs3_sb, h)))
+                size = ring.tile([P, HALF], F32, name="size", tag="s1")
+                nc.scalar.activation(size[:], picked[:], ACT.Abs)
+                x = ring.tile([P, HALF], F32, name="x", tag="s2")
+                nc.scalar.activation(x[:], size[:], ACT.Identity, bias=neg_limit[:, n : n + 1])
+                xs.append(x)
+            if n + 1 < OUT_TILES:
+                for c in range(CHUNKS):
+                    product(n + 1, c, 4 + c)
+            for h in range(HALVES):
+                nc.vector.tensor_tensor(outs[n][:].indirect(half_of(offs4_sb, h)), xs[h][:], wgo_sb[:, cols(h, HALF)], ALU.mult)
+            nc.sync.dma_start(out[cols(n, P), :], outs[n][:])

@@ -29,6 +29,7 @@ CHUNKS = T2 // CHUNK
 SUBS = CHUNK // P
 QUADS = 4
 SHIFT_ROWS = 112
+GW_SLOTS = {1: "raw1", 2: "raw3", 3: "codes2", 4: "codes3", 5: "raw2", 6: "codes1", 7: "codes0"}
 
 
 def tile_list_pump_dock_check_kernel(tc, tab_words, tab_scales, offs, w1_words, w1_scales, w2, curve, gain,
@@ -65,14 +66,10 @@ def tile_list_pump_dock_check_kernel(tc, tab_words, tab_scales, offs, w1_words, 
                 nc.sync.dma_start(tile[:, a, :, :], w2[cols(a, 512), cols(t, P)].rearrange("(p j) c -> p j c", j=4))
             return tile
 
-        tab_scale_rows = keep.tile([P, T], U8, name="tab_scale_rows", align_bytes=64)
+        tab_scale_rows = keep.tile([P, T], U8, name="tab_scale_rows", tag="big2", align_bytes=64)
         nc.vector.memset(tab_scale_rows[:].bitcast(I32), 0)
         vec_rows = keep.tile([P, P], F32, name="vec_rows")
         nc.vector.memset(vec_rows[:], 0.0)
-        w1_sc = keep.tile([P, PASSES, H], U8, name="w1_sc", align_bytes=64)
-        nc.vector.memset(w1_sc[:].rearrange("p a c -> p (a c)").bitcast(I32), 0)
-        w3_sc = keep.tile([P, N], U8, name="w3_sc", align_bytes=64)
-        nc.vector.memset(w3_sc[:].bitcast(I32), 0)
         v_sc = [keep.tile([P, S], U8, name="v_sc%d" % a, align_bytes=64) for a in range(PASSES)]
         for a in range(1, PASSES):
             nc.vector.memset(v_sc[a][:].bitcast(I32), 0)
@@ -81,25 +78,31 @@ def tile_list_pump_dock_check_kernel(tc, tab_words, tab_scales, offs, w1_words, 
         make_identity(nc, ident[:])
         warm = keep.tile([P, 1], F32, name="warm")
         nc.scalar.activation(warm[:], ident[:, 0:1], ACT.Tanh)
-        for q in range(QUADS):
-            nc.gpsimd.dma_start(tab_scale_rows[32 * q : 32 * q + 4 * PASSES, :].bitcast(I32),
-                                tab_scales[:, 4 * q : 4 * q + 4, :].bitcast(I32))
-        for q in range(QUADS):
-            nc.gpsimd.dma_start(w1_sc[32 * q : 32 * q + 4, :, :].bitcast(I32),
-                                w1_scales[:, 4 * q : 4 * q + 4, :].rearrange("a r c -> r a c").bitcast(I32))
+        w1_sc = keep.tile([P, PASSES, H], U8, name="w1_sc", align_bytes=64)
+        nc.gpsimd.memset(w1_sc[:].rearrange("p a c -> p (a c)").bitcast(I32), 0)
+
         offs_sb = load_list(offs, "offs_sb")
         table = [load_table(0)]
+        for q in range(QUADS):
+            nc.sync.dma_start(tab_scale_rows[32 * q : 32 * q + 4 * PASSES, :].bitcast(I32),
+                              tab_scales[:, 4 * q : 4 * q + 4, :].bitcast(I32))
+        table.append(load_table(1))
         nc.sync.dma_start(vec_rows[0:4, :], curve.rearrange("(t p) -> t p", p=P))
         nc.sync.dma_start(vec_rows[4:8, :], gain.rearrange("(t p) -> t p", p=P))
-        nc.sync.dma_start(vec_rows[8:11, :], limit.rearrange("(t p) -> t p", p=P))
-        table.append(load_table(1))
         w2_raw = [load_w2(0)]
         w1_sb = keep.tile([P, PASSES, 2 * H], U8, name="w1_sb", align_bytes=64)
         nc.sync.dma_start(w1_sb[:].bitcast(I32), w1_words.rearrange("a p c -> p a c").bitcast(I32))
+        nc.vector.tensor_copy(v_sc[0][:], tab_scale_rows[:].indirect(offs_sb[:]))
+        for a in range(1, PASSES):
+            nc.sync.dma_start(v_sc[a][0:SHIFT_ROWS, :].bitcast(I32),
+                              v_sc[0][4 * a : 4 * a + SHIFT_ROWS, :].bitcast(I32))
         table.append(load_table(2))
+        offs2_sb = load_list(offs2, "offs2_sb")
+        for q in range(QUADS):
+            nc.sync.dma_start(w1_sc[32 * q : 32 * q + 4, :, :].bitcast(I32),
+                              w1_scales[:, 4 * q : 4 * q + 4, :].rearrange("a r c -> r a c").bitcast(I32))
         wgs_sb = [keep.tile([P, HALF], F32, name="wgs_sb%d" % h) for h in range(HALVES)]
         nc.sync.dma_start(wgs_sb[0][:], wgs[:, cols(0, HALF)])
-        offs2_sb = load_list(offs2, "offs2_sb")
         w2_raw.append(load_w2(1))
         nc.sync.dma_start(wgs_sb[1][:], wgs[:, cols(1, HALF)])
         for t in range(2, ROW_TILES):
@@ -115,30 +118,29 @@ def tile_list_pump_dock_check_kernel(tc, tab_words, tab_scales, offs, w1_words, 
         offs4_sb = load_list(offs4, "offs4_sb")
         wgo_sb = keep.tile([P, S], F32, name="wgo_sb")
         nc.sync.dma_start(wgo_sb[:], wgo)
+        limit_sb = keep.tile([P, OUT_TILES], F32, name="limit_sb")
+        with nc.allow_non_contiguous_dma(reason="one value a partition"):
+            nc.sync.dma_start(limit_sb[:], limit.rearrange("(n p) -> p n", p=P))
+        neg_limit = keep.tile([P, OUT_TILES], F32, name="neg_limit")
 
         vec_bank = bank(7, "vec_bank")
         nc.tensor.transpose(vec_bank[:, 0:P], vec_rows[:], ident[:])
         vecs = keep.tile([P, 8], F32, name="vecs")
         nc.scalar.copy(vecs[:], vec_bank[:, 0:8])
-        neg_limit = keep.tile([P, OUT_TILES], F32, name="neg_limit")
-        nc.scalar.mul(neg_limit[:], vec_bank[:, 8:11], -1.0)
 
         pages = [keep.tile([P, T2], F32, name="page%d" % t, tag="page%d" % t) for t in range(ROW_TILES)]
         nc.vector.memset(pages[0][:], 0.0)
-
-        nc.vector.tensor_copy(v_sc[0][:], tab_scale_rows[:].indirect(offs_sb[:]))
-        for a in range(1, PASSES):
-            nc.gpsimd.dma_start(v_sc[a][0:SHIFT_ROWS, :].bitcast(I32),
-                                v_sc[0][4 * a : 4 * a + SHIFT_ROWS, :].bitcast(I32))
         for t in range(1, ROW_TILES):
             nc.gpsimd.memset(pages[t][:], 0.0)
+        w3_sc = keep.tile([P, N], U8, name="w3_sc", align_bytes=64)
+        nc.gpsimd.memset(w3_sc[:].bitcast(I32), 0)
         for q in range(QUADS):
             nc.gpsimd.dma_start(w3_sc[32 * q : 32 * q + 4, :].bitcast(I32), w3_scales[0, 4 * q : 4 * q + 4, :].bitcast(I32))
 
         def quantize_w2(t):
-            grouped = ring.tile([P, PASSES, P, 4], BF16, name="w2_grouped", align_bytes=64)
+            grouped = keep.tile([P, PASSES, P, 4], BF16, name="w2_grouped%d" % t, tag="grouped%d" % t, align_bytes=64)
             nc.scalar.copy(grouped[:], w2_raw[t][:].rearrange("p a j c -> p a c j"))
-            codes = keep.tile([P, PASSES * P], U32, name="w2_codes%d" % t, align_bytes=64)
+            codes = keep.tile([P, PASSES * P], U32, name="w2_codes%d" % t, tag="codes%d" % t, align_bytes=64)
             scales = keep.tile([P, PASSES * P], U8, name="w2_scales%d" % t, align_bytes=64)
             flat = grouped[:].rearrange("p a c j -> p (a c j)")
             for lo, hi in ((0, 2 * P), (2 * P, 3 * P)):
@@ -156,43 +158,49 @@ def tile_list_pump_dock_check_kernel(tc, tab_words, tab_scales, offs, w1_words, 
             if a == 0:
                 w2_q.append(quantize_w2(0))
 
-        def weight_tile(t, h):
-            later = t + 1 < ROW_TILES and h == (1 if t == 0 else 0)
-            if later:
-                tile = keep.tile([P, HALF], F32, name="gw%d_%d" % (t, h), tag="raw%d" % (t + 1), align_bytes=64)
-            else:
-                tile = ring.tile([P, HALF], F32, name="gw")
-            nc.scalar.mul(tile[:], wgs_sb[h][:], vecs[:, 4 + t : 5 + t])
-            return tile
-
+        th = keep.tile([P, ROW_TILES * HALVES, HALF], F32, name="th", tag="big0", align_bytes=64)
         z_t = []
 
         def stage_one(t):
             codes, scales = w2_q[t]
-            hs = []
+            b_banks = [bank(4 * (t % 2) + h, "b_bank") for h in range(HALVES)]
+            a_banks = [bank(4 * (t % 2) + HALVES + h, "a_bank") for h in range(HALVES)]
+
+            def product_b(h):
+                for a in range(PASSES):
+                    nc.tensor.matmul_mx(out=b_banks[h][:], lhsT=codes[:, cols(a, P)].bitcast(FP8X4), lhsT_scale=scales[:, cols(a, P)],
+                                        rhs=v[a][h][:].bitcast(FP8X4), rhs_scale=v_sc[a][:, cols(h, HALF)],
+                                        start=(a == 0), stop=(a == PASSES - 1))
+
+            def product_a(h):
+                for a in range(PASSES):
+                    nc.tensor.matmul_mx(out=a_banks[h][:], lhsT=w1_sb[:, a, cols(t, 2 * P)].bitcast(FP4X4), lhsT_scale=w1_sc[:, a, cols(t, P)],
+                                        rhs=v[a][h][:].bitcast(FP8X4), rhs_scale=v_sc[a][:, cols(h, HALF)],
+                                        start=(a == 0), stop=(a == PASSES - 1))
+
+            order = [(product_b, 0), (product_a, 0), (product_b, 1), (product_a, 1)]
+            if t > 0:
+                order = [order[0], order[2], order[1], order[3]]
+            for product, h in order:
+                product(h)
+            squares = []
             for h in range(HALVES):
-                b_bank = bank(4 * (t % 2) + 2 * h, "b_bank")
-                a_bank = bank(4 * (t % 2) + 2 * h + 1, "a_bank")
-                for a in range(PASSES):
-                    nc.tensor.matmul_mx(out=b_bank[:], lhsT=codes[:, cols(a, P)].bitcast(FP8X4), lhsT_scale=scales[:, cols(a, P)],
-                                        rhs=v[a][h][:].bitcast(FP8X4), rhs_scale=v_sc[a][:, cols(h, HALF)],
-                                        start=(a == 0), stop=(a == PASSES - 1))
-                for a in range(PASSES):
-                    nc.tensor.matmul_mx(out=a_bank[:], lhsT=w1_sb[:, a, cols(t, 2 * P)].bitcast(FP4X4), lhsT_scale=w1_sc[:, a, cols(t, P)],
-                                        rhs=v[a][h][:].bitcast(FP8X4), rhs_scale=v_sc[a][:, cols(h, HALF)],
-                                        start=(a == 0), stop=(a == PASSES - 1))
                 sq = ring.tile([P, HALF], F32, name="sq", tag="s0")
-                nc.scalar.activation(sq[:], b_bank[:], ACT.Square)
-                u = ring.tile([P, HALF], F32, name="u", tag="s1")
-                nc.vector.scalar_tensor_tensor(u[:], sq[:], vecs[:, t : t + 1], a_bank[:], ALU.mult, ALU.add)
-                th = ring.tile([P, HALF], F32, name="th", tag="s2")
-                nc.scalar.activation(th[:], u[:], ACT.Tanh)
-                hs.append(th)
+                nc.scalar.activation(sq[:], b_banks[h][:], ACT.Square)
+                squares.append(sq)
             for h in range(HALVES):
-                if t + 1 < ROW_TILES and h == (1 if t == 0 else 0):
-                    w2_q.append(quantize_w2(t + 1))
-                gw = weight_tile(t, h)
-                nc.vector.tensor_tensor(pages[t][:].indirect(half_of(offs2_sb, h)), hs[h][:], gw[:], ALU.mult)
+                if t == 0 and h == 0:
+                    u = keep.tile([P, HALF], F32, name="u_first", tag="grouped1", align_bytes=64)
+                else:
+                    u = ring.tile([P, HALF], F32, name="u", tag="s1")
+                nc.vector.scalar_tensor_tensor(u[:], squares[h][:], vecs[:, t : t + 1], a_banks[h][:], ALU.mult, ALU.add)
+                nc.scalar.activation(th[:, t * HALVES + h, :], u[:], ACT.Tanh)
+
+        def place(step):
+            t, h = divmod(step, HALVES)
+            gw = keep.tile([P, HALF], F32, name="gw%d" % step, tag=GW_SLOTS.get(step, "gw%d" % step), align_bytes=64)
+            nc.scalar.mul(gw[:], wgs_sb[h][:], vecs[:, 4 + t : 5 + t])
+            nc.vector.tensor_tensor(pages[t][:].indirect(half_of(offs2_sb, h)), th[:, step, :], gw[:], ALU.mult)
 
         def add_base(t, first_bank):
             banks = [bank(first_bank + c, "sum_bank") for c in range(CHUNKS)]
@@ -207,38 +215,50 @@ def tile_list_pump_dock_check_kernel(tc, tab_words, tab_scales, offs, w1_words, 
 
         for c in range(CHUNKS):
             z_t.append(keep.tile([P, SUBS, 2, P, 2], BF16, name="z_t%d" % c, align_bytes=64))
-        for t in range(ROW_TILES):
+        stage_one(0)
+        place(0)
+        w2_q.append(quantize_w2(1))
+        place(1)
+        w2_q.append(quantize_w2(2))
+        w2_q.append(quantize_w2(3))
+        for t in range(1, ROW_TILES):
             stage_one(t)
-            if t >= 2:
-                add_base(t - 2, 4 * ((t - 1) % 2))
-        for t in range(ROW_TILES - 2, ROW_TILES):
-            add_base(t, 4 * ((t + 1) % 2))
+            place(t + 1)
+        for step in range(ROW_TILES + 1, ROW_TILES * HALVES):
+            place(step)
+        for t in range(ROW_TILES):
+            add_base(t, 4 * (t % 2))
 
+        nc.scalar.mul(neg_limit[:], limit_sb[:], -1.0)
         outs = []
         for n in range(OUT_TILES):
             tile = keep.tile([P, T2], F32, name="out_page%d" % n, tag="page%d" % n)
             nc.gpsimd.memset(tile[:], 0.0)
             outs.append(tile)
 
-        y = [keep.tile([P, T2], F32, name="y%d" % n, tag="big%d" % n, align_bytes=64) for n in range(OUT_TILES)]
+        y = []
         z_q = []
 
-        def product(n, c, bank_no):
+        def product(n, c, bank_no, engine_copy):
             codes, scales = z_q[c]
             y_bank = bank(bank_no, "y_bank")
             nc.tensor.matmul_mx(out=y_bank[:], lhsT=w3_sb[:, cols(n, P)].bitcast(FP8X4), lhsT_scale=w3_sc[:, cols(n, P)],
                                 rhs=codes[:].bitcast(FP8X4), rhs_scale=scales[:], start=True, stop=True)
-            nc.scalar.copy(y[n][:, cols(c, CHUNK)], y_bank[:])
+            engine_copy(y[n][:, cols(c, CHUNK)], y_bank[:])
 
+        y.append(keep.tile([P, T2], F32, name="y0", tag="big0", align_bytes=64))
         for c in range(CHUNKS):
             words = z_t[c][:].rearrange("q s u p e -> q (s u p e)").bitcast(F32)
             codes = keep.tile([P, CHUNK], U32, name="z_codes%d" % c, tag="words%d" % c, align_bytes=64)
             scales = keep.tile([P, CHUNK], U8, name="z_scales%d" % c, align_bytes=64)
             for h in range(2):
-                back = bank(4 + (2 * c + h) % 4, "back_bank")
+                back = bank((2 * c + h) % 4, "back_bank")
                 for i in range(4):
                     nc.tensor.transpose(back[:, cols(i, P)], words[:, cols(4 * h + i, P)], ident[:])
-                z = ring.tile([P, 2 * P * 4], BF16, name="z", tag="z%d" % h, align_bytes=64)
+                if c == CHUNKS - 1:
+                    z = keep.tile([P, 2 * P * 4], BF16, name="z_last%d" % h, tag="big%d" % (2 - h), align_bytes=64)
+                else:
+                    z = ring.tile([P, 2 * P * 4], BF16, name="z", tag="z%d" % h, align_bytes=64)
                 z_words = z[:].bitcast(F32).rearrange("p (s q u) -> p s q u", s=2, u=2)
                 src = back[:].rearrange("p (s u q) -> p s q u", s=2, u=2)
                 if h == 0 or c % 2 == 1:
@@ -247,21 +267,23 @@ def tile_list_pump_dock_check_kernel(tc, tab_words, tab_scales, offs, w1_words, 
                     nc.scalar.copy(z_words, src)
                 nc.vector.quantize_mx(out=codes[:, cols(h, 2 * P)].bitcast(FP8X4), scales=scales[:, cols(h, 2 * P)], in_=z[:])
             z_q.append((codes, scales))
-            product(0, c, c)
+            product(0, c, 4 + c, nc.vector.tensor_copy if c == CHUNKS - 1 else nc.scalar.copy)
+        for n in range(1, OUT_TILES):
+            y.append(keep.tile([P, T2], F32, name="y%d" % n, tag="big%d" % n, align_bytes=64))
+            for c in range(CHUNKS):
+                product(n, c, c, nc.scalar.copy)
 
+        picked = []
         for n in range(OUT_TILES):
-            xs = []
             for h in range(HALVES):
-                picked = ring.tile([P, HALF], F32, name="picked", tag="s0")
-                nc.vector.tensor_copy(picked[:], y[n][:].indirect(half_of(offs3_sb, h)))
+                tile = keep.tile([P, HALF], F32, name="picked%d_%d" % (n, h), tag=GW_SLOTS[1 + n * HALVES + h], align_bytes=64)
+                nc.vector.tensor_copy(tile[:], y[n][:].indirect(half_of(offs3_sb, h)))
+                picked.append(tile)
+        for n in range(OUT_TILES):
+            for h in range(HALVES):
+                tile = picked[n * HALVES + h]
                 size = ring.tile([P, HALF], F32, name="size", tag="s1")
-                nc.scalar.activation(size[:], picked[:], ACT.Abs)
-                x = ring.tile([P, HALF], F32, name="x", tag="s2")
-                nc.scalar.activation(x[:], size[:], ACT.Identity, bias=neg_limit[:, n : n + 1])
-                xs.append(x)
-            if n + 1 < OUT_TILES:
-                for c in range(CHUNKS):
-                    product(n + 1, c, 4 + c)
-            for h in range(HALVES):
-                nc.vector.tensor_tensor(outs[n][:].indirect(half_of(offs4_sb, h)), xs[h][:], wgo_sb[:, cols(h, HALF)], ALU.mult)
+                nc.scalar.activation(size[:], tile[:], ACT.Abs)
+                nc.scalar.activation(tile[:], size[:], ACT.Identity, bias=neg_limit[:, n : n + 1])
+                nc.vector.tensor_tensor(outs[n][:].indirect(half_of(offs4_sb, h)), tile[:], wgo_sb[:, cols(h, HALF)], ALU.mult)
             nc.sync.dma_start(out[cols(n, P), :], outs[n][:])

@@ -66,7 +66,7 @@ def tile_list_pump_dock_check_kernel(tc, tab_words, tab_scales, offs, w1_words, 
                 nc.sync.dma_start(tile[:, a, :, :], w2[cols(a, 512), cols(t, P)].rearrange("(p j) c -> p j c", j=4))
             return tile
 
-        tab_scale_rows = keep.tile([P, T], U8, name="tab_scale_rows", tag="big2", align_bytes=64)
+        tab_scale_rows = keep.tile([P, T], U8, name="tab_scale_rows", align_bytes=64)
         nc.vector.memset(tab_scale_rows[:].bitcast(I32), 0)
         vec_rows = keep.tile([P, P], F32, name="vec_rows")
         nc.vector.memset(vec_rows[:], 0.0)
@@ -80,6 +80,11 @@ def tile_list_pump_dock_check_kernel(tc, tab_words, tab_scales, offs, w1_words, 
         nc.scalar.activation(warm[:], ident[:, 0:1], ACT.Tanh)
         w1_sc = keep.tile([P, PASSES, H], U8, name="w1_sc", align_bytes=64)
         nc.gpsimd.memset(w1_sc[:].rearrange("p a c -> p (a c)").bitcast(I32), 0)
+        for q in range(QUADS):
+            nc.gpsimd.dma_start(w1_sc[32 * q : 32 * q + 4, :, :].bitcast(I32),
+                                w1_scales[:, 4 * q : 4 * q + 4, :].rearrange("a r c -> r a c").bitcast(I32))
+        w3_sc = keep.tile([P, N], U8, name="w3_sc", align_bytes=64)
+        nc.vector.memset(w3_sc[:].bitcast(I32), 0)
 
         offs_sb = load_list(offs, "offs_sb")
         table = [load_table(0)]
@@ -92,28 +97,22 @@ def tile_list_pump_dock_check_kernel(tc, tab_words, tab_scales, offs, w1_words, 
         w2_raw = [load_w2(0)]
         w1_sb = keep.tile([P, PASSES, 2 * H], U8, name="w1_sb", align_bytes=64)
         nc.sync.dma_start(w1_sb[:].bitcast(I32), w1_words.rearrange("a p c -> p a c").bitcast(I32))
+        table.append(load_table(2))
         nc.vector.tensor_copy(v_sc[0][:], tab_scale_rows[:].indirect(offs_sb[:]))
         for a in range(1, PASSES):
             nc.sync.dma_start(v_sc[a][0:SHIFT_ROWS, :].bitcast(I32),
                               v_sc[0][4 * a : 4 * a + SHIFT_ROWS, :].bitcast(I32))
-        table.append(load_table(2))
-        offs2_sb = load_list(offs2, "offs2_sb")
-        for q in range(QUADS):
-            nc.sync.dma_start(w1_sc[32 * q : 32 * q + 4, :, :].bitcast(I32),
-                              w1_scales[:, 4 * q : 4 * q + 4, :].rearrange("a r c -> r a c").bitcast(I32))
         wgs_sb = [keep.tile([P, HALF], F32, name="wgs_sb%d" % h) for h in range(HALVES)]
         nc.sync.dma_start(wgs_sb[0][:], wgs[:, cols(0, HALF)])
+        offs2_sb = load_list(offs2, "offs2_sb")
         w2_raw.append(load_w2(1))
         nc.sync.dma_start(wgs_sb[1][:], wgs[:, cols(1, HALF)])
         for t in range(2, ROW_TILES):
             w2_raw.append(load_w2(t))
-        base_sb = []
-        for t in range(ROW_TILES):
-            tile = keep.tile([P, T2], F32, name="base%d" % t)
-            nc.sync.dma_start(tile[:], base[cols(t, P), :])
-            base_sb.append(tile)
         w3_sb = keep.tile([P, N], U32, name="w3_sb", align_bytes=64)
         nc.sync.dma_start(w3_sb[:].bitcast(I32), w3_words[0].rearrange("p c i -> p (c i)").bitcast(I32))
+        for q in range(QUADS):
+            nc.sync.dma_start(w3_sc[32 * q : 32 * q + 4, :].bitcast(I32), w3_scales[0, 4 * q : 4 * q + 4, :].bitcast(I32))
         offs3_sb = load_list(offs3, "offs3_sb")
         offs4_sb = load_list(offs4, "offs4_sb")
         wgo_sb = keep.tile([P, S], F32, name="wgo_sb")
@@ -121,6 +120,11 @@ def tile_list_pump_dock_check_kernel(tc, tab_words, tab_scales, offs, w1_words, 
         limit_sb = keep.tile([P, OUT_TILES], F32, name="limit_sb")
         with nc.allow_non_contiguous_dma(reason="one value a partition"):
             nc.sync.dma_start(limit_sb[:], limit.rearrange("(n p) -> p n", p=P))
+        base_sb = []
+        for t in range(ROW_TILES):
+            tile = ring.tile([P, T2], F32, name="base_sb")
+            nc.sync.dma_start(tile[:], base[cols(t, P), :])
+            base_sb.append(tile)
         neg_limit = keep.tile([P, OUT_TILES], F32, name="neg_limit")
 
         vec_bank = bank(7, "vec_bank")
@@ -128,14 +132,6 @@ def tile_list_pump_dock_check_kernel(tc, tab_words, tab_scales, offs, w1_words, 
         vecs = keep.tile([P, 8], F32, name="vecs")
         nc.scalar.copy(vecs[:], vec_bank[:, 0:8])
 
-        pages = [keep.tile([P, T2], F32, name="page%d" % t, tag="page%d" % t) for t in range(ROW_TILES)]
-        nc.vector.memset(pages[0][:], 0.0)
-        for t in range(1, ROW_TILES):
-            nc.gpsimd.memset(pages[t][:], 0.0)
-        w3_sc = keep.tile([P, N], U8, name="w3_sc", align_bytes=64)
-        nc.gpsimd.memset(w3_sc[:].bitcast(I32), 0)
-        for q in range(QUADS):
-            nc.gpsimd.dma_start(w3_sc[32 * q : 32 * q + 4, :].bitcast(I32), w3_scales[0, 4 * q : 4 * q + 4, :].bitcast(I32))
 
         def quantize_w2(t):
             grouped = keep.tile([P, PASSES, P, 4], BF16, name="w2_grouped%d" % t, tag="grouped%d" % t, align_bytes=64)
@@ -157,6 +153,11 @@ def tile_list_pump_dock_check_kernel(tc, tab_words, tab_scales, offs, w1_words, 
                 v[a].append(tile)
             if a == 0:
                 w2_q.append(quantize_w2(0))
+
+        pages = [keep.tile([P, T2], F32, name="page%d" % t) for t in range(ROW_TILES)]
+        last_out = keep.tile([P, T2], F32, name="last_out")
+        for tile in pages + [last_out]:
+            nc.vector.memset(tile[:], 0.0)
 
         th = keep.tile([P, ROW_TILES * HALVES, HALF], F32, name="th", tag="big0", align_bytes=64)
         z_t = []
@@ -213,8 +214,6 @@ def tile_list_pump_dock_check_kernel(tc, tab_words, tab_scales, offs, w1_words, 
                 nc.scalar.copy(z_t[c][:, :, :, cols(t, 32), :],
                                banks[c][:].rearrange("q (s p u e) -> q s u p e", s=SUBS, u=2, e=2))
 
-        for c in range(CHUNKS):
-            z_t.append(keep.tile([P, SUBS, 2, P, 2], BF16, name="z_t%d" % c, align_bytes=64))
         stage_one(0)
         place(0)
         w2_q.append(quantize_w2(1))
@@ -226,15 +225,19 @@ def tile_list_pump_dock_check_kernel(tc, tab_words, tab_scales, offs, w1_words, 
             place(t + 1)
         for step in range(ROW_TILES + 1, ROW_TILES * HALVES):
             place(step)
+        for c in range(CHUNKS):
+            z_t.append(keep.tile([P, SUBS, 2, P, 2], BF16, name="z_t%d" % c, tag="grouped%d" % c, align_bytes=64))
         for t in range(ROW_TILES):
             add_base(t, 4 * (t % 2))
 
         nc.scalar.mul(neg_limit[:], limit_sb[:], -1.0)
+
         outs = []
-        for n in range(OUT_TILES):
-            tile = keep.tile([P, T2], F32, name="out_page%d" % n, tag="page%d" % n)
-            nc.gpsimd.memset(tile[:], 0.0)
+        for n, slot in enumerate(("big0", GW_SLOTS[ROW_TILES * HALVES - 1])):
+            tile = keep.tile([P, T2], F32, name="out_page%d" % n, tag=slot, align_bytes=64)
+            nc.vector.memset(tile[:], 0.0)
             outs.append(tile)
+        outs.append(last_out)
 
         y = []
         z_q = []
@@ -246,7 +249,7 @@ def tile_list_pump_dock_check_kernel(tc, tab_words, tab_scales, offs, w1_words, 
                                 rhs=codes[:].bitcast(FP8X4), rhs_scale=scales[:], start=True, stop=True)
             engine_copy(y[n][:, cols(c, CHUNK)], y_bank[:])
 
-        y.append(keep.tile([P, T2], F32, name="y0", tag="big0", align_bytes=64))
+        y.append(keep.tile([P, T2], F32, name="y0", tag="big2", align_bytes=64))
         for c in range(CHUNKS):
             words = z_t[c][:].rearrange("q s u p e -> q (s u p e)").bitcast(F32)
             codes = keep.tile([P, CHUNK], U32, name="z_codes%d" % c, tag="words%d" % c, align_bytes=64)
@@ -255,13 +258,13 @@ def tile_list_pump_dock_check_kernel(tc, tab_words, tab_scales, offs, w1_words, 
                 back = bank((2 * c + h) % 4, "back_bank")
                 for i in range(4):
                     nc.tensor.transpose(back[:, cols(i, P)], words[:, cols(4 * h + i, P)], ident[:])
-                if c == CHUNKS - 1:
-                    z = keep.tile([P, 2 * P * 4], BF16, name="z_last%d" % h, tag="big%d" % (2 - h), align_bytes=64)
+                if c == CHUNKS - 1 and h == 1:
+                    z = keep.tile([P, 2 * P * 4], BF16, name="z_last", tag="big1", align_bytes=64)
                 else:
                     z = ring.tile([P, 2 * P * 4], BF16, name="z", tag="z%d" % h, align_bytes=64)
                 z_words = z[:].bitcast(F32).rearrange("p (s q u) -> p s q u", s=2, u=2)
                 src = back[:].rearrange("p (s u q) -> p s q u", s=2, u=2)
-                if h == 0 or c % 2 == 1:
+                if h == 0:
                     nc.vector.tensor_copy(z_words, src)
                 else:
                     nc.scalar.copy(z_words, src)
@@ -269,7 +272,10 @@ def tile_list_pump_dock_check_kernel(tc, tab_words, tab_scales, offs, w1_words, 
             z_q.append((codes, scales))
             product(0, c, 4 + c, nc.vector.tensor_copy if c == CHUNKS - 1 else nc.scalar.copy)
         for n in range(1, OUT_TILES):
-            y.append(keep.tile([P, T2], F32, name="y%d" % n, tag="big%d" % n, align_bytes=64))
+            if n == 1:
+                y.append(keep.tile([P, T2], F32, name="y1", tag="big1", align_bytes=64))
+            else:
+                y.append(ring.tile([P, T2], F32, name="y2", tag="base_sb"))
             for c in range(CHUNKS):
                 product(n, c, c, nc.scalar.copy)
 

@@ -29,7 +29,6 @@ CHUNKS = T2 // CHUNK
 SUBS = CHUNK // P
 QUADS = 4
 SHIFT_ROWS = 112
-GW_SLOTS = {1: "raw1", 2: "raw3", 3: "codes2", 4: "codes3", 5: "raw2", 6: "codes1", 7: "codes0"}
 
 
 def tile_list_pump_dock_check_kernel(tc, tab_words, tab_scales, offs, w1_words, w1_scales, w2, curve, gain,
@@ -60,13 +59,12 @@ def tile_list_pump_dock_check_kernel(tc, tab_words, tab_scales, offs, w1_words, 
             nc.sync.dma_start(tile[:].bitcast(I32), tab_words[a].rearrange("p t i -> p (t i)").bitcast(I32))
             return tile
 
-        def load_w2(t):
-            tile = keep.tile([P, PASSES, 4, P], F32, name="w2_raw%d" % t, tag="raw%d" % t, align_bytes=64)
-            for a in range(PASSES):
-                nc.sync.dma_start(tile[:, a, :, :], w2[cols(a, 512), cols(t, P)].rearrange("(p j) c -> p j c", j=4))
+        def load_w2(a):
+            tile = keep.tile([P, 4, H], F32, name="w2_raw%d" % a, tag="raw%d" % a, align_bytes=64)
+            nc.sync.dma_start(tile[:], w2[cols(a, 512), :].rearrange("(p j) c -> p j c", j=4))
             return tile
 
-        tab_scale_rows = keep.tile([P, T], U8, name="tab_scale_rows", align_bytes=64)
+        tab_scale_rows = keep.tile([P, T], U8, name="tab_scale_rows", tag="tab_scale_rows", align_bytes=64)
         nc.vector.memset(tab_scale_rows[:].bitcast(I32), 0)
         vec_rows = keep.tile([P, P], F32, name="vec_rows")
         nc.vector.memset(vec_rows[:], 0.0)
@@ -87,14 +85,16 @@ def tile_list_pump_dock_check_kernel(tc, tab_words, tab_scales, offs, w1_words, 
         nc.vector.memset(w3_sc[:].bitcast(I32), 0)
 
         offs_sb = load_list(offs, "offs_sb")
-        table = [load_table(0)]
+        w2_raw = [load_w2(0)]
         for q in range(QUADS):
             nc.sync.dma_start(tab_scale_rows[32 * q : 32 * q + 4 * PASSES, :].bitcast(I32),
                               tab_scales[:, 4 * q : 4 * q + 4, :].bitcast(I32))
-        table.append(load_table(1))
+        w2_raw.append(load_w2(1))
         nc.sync.dma_start(vec_rows[0:4, :], curve.rearrange("(t p) -> t p", p=P))
         nc.sync.dma_start(vec_rows[4:8, :], gain.rearrange("(t p) -> t p", p=P))
-        w2_raw = [load_w2(0)]
+        nc.sync.dma_start(vec_rows[8:11, :], limit.rearrange("(t p) -> t p", p=P))
+        w2_raw.append(load_w2(2))
+        table = [load_table(0), load_table(1)]
         w1_sb = keep.tile([P, PASSES, 2 * H], U8, name="w1_sb", align_bytes=64)
         nc.sync.dma_start(w1_sb[:].bitcast(I32), w1_words.rearrange("a p c -> p a c").bitcast(I32))
         table.append(load_table(2))
@@ -102,13 +102,10 @@ def tile_list_pump_dock_check_kernel(tc, tab_words, tab_scales, offs, w1_words, 
         for a in range(1, PASSES):
             nc.sync.dma_start(v_sc[a][0:SHIFT_ROWS, :].bitcast(I32),
                               v_sc[0][4 * a : 4 * a + SHIFT_ROWS, :].bitcast(I32))
-        wgs_sb = [keep.tile([P, HALF], F32, name="wgs_sb%d" % h) for h in range(HALVES)]
-        nc.sync.dma_start(wgs_sb[0][:], wgs[:, cols(0, HALF)])
+        wgs_sb = keep.tile([P, S], F32, name="wgs_sb")
+        for h in range(HALVES):
+            nc.sync.dma_start(wgs_sb[:, cols(h, HALF)], wgs[:, cols(h, HALF)])
         offs2_sb = load_list(offs2, "offs2_sb")
-        w2_raw.append(load_w2(1))
-        nc.sync.dma_start(wgs_sb[1][:], wgs[:, cols(1, HALF)])
-        for t in range(2, ROW_TILES):
-            w2_raw.append(load_w2(t))
         w3_sb = keep.tile([P, N], U32, name="w3_sb", align_bytes=64)
         nc.sync.dma_start(w3_sb[:].bitcast(I32), w3_words[0].rearrange("p c i -> p (c i)").bitcast(I32))
         for q in range(QUADS):
@@ -117,91 +114,81 @@ def tile_list_pump_dock_check_kernel(tc, tab_words, tab_scales, offs, w1_words, 
         offs4_sb = load_list(offs4, "offs4_sb")
         wgo_sb = keep.tile([P, S], F32, name="wgo_sb")
         nc.sync.dma_start(wgo_sb[:], wgo)
-        limit_sb = keep.tile([P, OUT_TILES], F32, name="limit_sb")
-        with nc.allow_non_contiguous_dma(reason="one value a partition"):
-            nc.sync.dma_start(limit_sb[:], limit.rearrange("(n p) -> p n", p=P))
         base_sb = []
         for t in range(ROW_TILES):
             tile = ring.tile([P, T2], F32, name="base_sb")
             nc.sync.dma_start(tile[:], base[cols(t, P), :])
             base_sb.append(tile)
-        neg_limit = keep.tile([P, OUT_TILES], F32, name="neg_limit")
 
         vec_bank = bank(7, "vec_bank")
         nc.tensor.transpose(vec_bank[:, 0:P], vec_rows[:], ident[:])
         vecs = keep.tile([P, 8], F32, name="vecs")
         nc.scalar.copy(vecs[:], vec_bank[:, 0:8])
+        neg_limit = keep.tile([P, OUT_TILES], F32, name="neg_limit")
+        nc.scalar.mul(neg_limit[:], vec_bank[:, 8:11], -1.0)
 
+
+        w2_grouped = keep.tile([P, ROW_TILES, PASSES, P, 4], BF16, name="w2_grouped", tag="w2_grouped", align_bytes=64)
 
         def quantize_w2(t):
-            grouped = keep.tile([P, PASSES, P, 4], BF16, name="w2_grouped%d" % t, tag="grouped%d" % t, align_bytes=64)
-            nc.scalar.copy(grouped[:], w2_raw[t][:].rearrange("p a j c -> p a c j"))
             codes = keep.tile([P, PASSES * P], U32, name="w2_codes%d" % t, tag="codes%d" % t, align_bytes=64)
-            scales = keep.tile([P, PASSES * P], U8, name="w2_scales%d" % t, align_bytes=64)
-            flat = grouped[:].rearrange("p a c j -> p (a c j)")
+            scales = keep.tile([P, PASSES * P], U8, name="w2_scales%d" % t, tag="scales%d" % t, align_bytes=64)
+            flat = w2_grouped[:, t, :, :, :].rearrange("p a c j -> p (a c j)")
             for lo, hi in ((0, 2 * P), (2 * P, 3 * P)):
                 nc.vector.quantize_mx(out=codes[:, lo:hi].bitcast(FP8X4), scales=scales[:, lo:hi], in_=flat[:, 4 * lo : 4 * hi])
             return codes, scales
 
-        v = []
-        w2_q = []
         for a in range(PASSES):
-            v.append([])
-            for h in range(HALVES):
-                tile = keep.tile([P, HALF], U32, name="v%d_%d" % (a, h), tag="words%d" % (a * HALVES + h), align_bytes=64)
-                nc.vector.tensor_copy(tile[:], table[a][:].indirect(half_of(offs_sb, h)))
-                v[a].append(tile)
-            if a == 0:
-                w2_q.append(quantize_w2(0))
+            nc.scalar.copy(w2_grouped[:, :, a, :, :], w2_raw[a][:].rearrange("p j (t c) -> p t c j", t=ROW_TILES))
+        w2_q = [quantize_w2(t) for t in range(ROW_TILES)]
+
+        v = []
+        for a in range(PASSES):
+            tile = keep.tile([P, S], U32, name="v%d" % a, tag="words%d" % a, align_bytes=64)
+            if a + 1 < PASSES:
+                nc.vector.tensor_copy(tile[:], table[a][:].indirect(offs_sb[:]))
+            else:
+                for h in range(HALVES):
+                    nc.vector.tensor_copy(tile[:, cols(h, HALF)], table[a][:].indirect(half_of(offs_sb, h)))
+            v.append(tile)
 
         pages = [keep.tile([P, T2], F32, name="page%d" % t) for t in range(ROW_TILES)]
         last_out = keep.tile([P, T2], F32, name="last_out")
         for tile in pages + [last_out]:
             nc.vector.memset(tile[:], 0.0)
 
-        th = keep.tile([P, ROW_TILES * HALVES, HALF], F32, name="th", tag="big0", align_bytes=64)
+        th = keep.tile([P, ROW_TILES, S], F32, name="th", tag="big0", align_bytes=64)
         z_t = []
 
-        def stage_one(t):
+        def product_a(t, h):
+            a_bank = bank(4 * (t % 2) + HALVES + h, "a_bank")
+            for a in range(PASSES):
+                nc.tensor.matmul_mx(out=a_bank[:], lhsT=w1_sb[:, a, cols(t, 2 * P)].bitcast(FP4X4), lhsT_scale=w1_sc[:, a, cols(t, P)],
+                                    rhs=v[a][:, cols(h, HALF)].bitcast(FP8X4), rhs_scale=v_sc[a][:, cols(h, HALF)],
+                                    start=(a == 0), stop=(a == PASSES - 1))
+            return a_bank
+
+        def square_of_b(t, h):
             codes, scales = w2_q[t]
-            b_banks = [bank(4 * (t % 2) + h, "b_bank") for h in range(HALVES)]
-            a_banks = [bank(4 * (t % 2) + HALVES + h, "a_bank") for h in range(HALVES)]
+            b_bank = bank(4 * (t % 2) + h, "b_bank")
+            for a in range(PASSES):
+                nc.tensor.matmul_mx(out=b_bank[:], lhsT=codes[:, cols(a, P)].bitcast(FP8X4), lhsT_scale=scales[:, cols(a, P)],
+                                    rhs=v[a][:, cols(h, HALF)].bitcast(FP8X4), rhs_scale=v_sc[a][:, cols(h, HALF)],
+                                    start=(a == 0), stop=(a == PASSES - 1))
+            sq = ring.tile([P, HALF], F32, name="sq")
+            nc.scalar.activation(sq[:], b_bank[:], ACT.Square)
+            return sq
 
-            def product_b(h):
-                for a in range(PASSES):
-                    nc.tensor.matmul_mx(out=b_banks[h][:], lhsT=codes[:, cols(a, P)].bitcast(FP8X4), lhsT_scale=scales[:, cols(a, P)],
-                                        rhs=v[a][h][:].bitcast(FP8X4), rhs_scale=v_sc[a][:, cols(h, HALF)],
-                                        start=(a == 0), stop=(a == PASSES - 1))
+        def tanh_of_sum(t, h, a_bank, sq):
+            u = ring.tile([P, HALF], F32, name="u")
+            nc.vector.scalar_tensor_tensor(u[:], sq[:], vecs[:, t : t + 1], a_bank[:], ALU.mult, ALU.add)
+            nc.scalar.activation(th[:, t, cols(h, HALF)], u[:], ACT.Tanh)
 
-            def product_a(h):
-                for a in range(PASSES):
-                    nc.tensor.matmul_mx(out=a_banks[h][:], lhsT=w1_sb[:, a, cols(t, 2 * P)].bitcast(FP4X4), lhsT_scale=w1_sc[:, a, cols(t, P)],
-                                        rhs=v[a][h][:].bitcast(FP8X4), rhs_scale=v_sc[a][:, cols(h, HALF)],
-                                        start=(a == 0), stop=(a == PASSES - 1))
-
-            order = [(product_b, 0), (product_a, 0), (product_b, 1), (product_a, 1)]
-            if t > 0:
-                order = [order[0], order[2], order[1], order[3]]
-            for product, h in order:
-                product(h)
-            squares = []
-            for h in range(HALVES):
-                sq = ring.tile([P, HALF], F32, name="sq", tag="s0")
-                nc.scalar.activation(sq[:], b_banks[h][:], ACT.Square)
-                squares.append(sq)
-            for h in range(HALVES):
-                if t == 0 and h == 0:
-                    u = keep.tile([P, HALF], F32, name="u_first", tag="grouped1", align_bytes=64)
-                else:
-                    u = ring.tile([P, HALF], F32, name="u", tag="s1")
-                nc.vector.scalar_tensor_tensor(u[:], squares[h][:], vecs[:, t : t + 1], a_banks[h][:], ALU.mult, ALU.add)
-                nc.scalar.activation(th[:, t * HALVES + h, :], u[:], ACT.Tanh)
-
-        def place(step):
-            t, h = divmod(step, HALVES)
-            gw = keep.tile([P, HALF], F32, name="gw%d" % step, tag=GW_SLOTS.get(step, "gw%d" % step), align_bytes=64)
-            nc.scalar.mul(gw[:], wgs_sb[h][:], vecs[:, 4 + t : 5 + t])
-            nc.vector.tensor_tensor(pages[t][:].indirect(half_of(offs2_sb, h)), th[:, step, :], gw[:], ALU.mult)
+        def place(t, lo, hi, slot):
+            entries = slice(lo * HALF, hi * HALF)
+            gw = keep.tile([P, (hi - lo) * HALF], F32, name="gw%d_%d" % (t, lo), tag=slot, align_bytes=64)
+            nc.scalar.mul(gw[:], wgs_sb[:, entries], vecs[:, 4 + t : 5 + t])
+            nc.vector.tensor_tensor(pages[t][:].indirect(offs2_sb[:, lo * LIST_COLS : hi * LIST_COLS]), th[:, t, entries], gw[:], ALU.mult)
 
         def add_base(t, first_bank):
             banks = [bank(first_bank + c, "sum_bank") for c in range(CHUNKS)]
@@ -214,26 +201,25 @@ def tile_list_pump_dock_check_kernel(tc, tab_words, tab_scales, offs, w1_words, 
                 nc.scalar.copy(z_t[c][:, :, :, cols(t, 32), :],
                                banks[c][:].rearrange("q (s p u e) -> q s u p e", s=SUBS, u=2, e=2))
 
-        stage_one(0)
-        place(0)
-        w2_q.append(quantize_w2(1))
-        place(1)
-        w2_q.append(quantize_w2(2))
-        w2_q.append(quantize_w2(3))
+        for h in range(HALVES):
+            sq = square_of_b(0, h)
+            tanh_of_sum(0, h, product_a(0, h), sq)
+        place(0, 0, 1, "raw0")
         for t in range(1, ROW_TILES):
-            stage_one(t)
-            place(t + 1)
-        for step in range(ROW_TILES + 1, ROW_TILES * HALVES):
-            place(step)
-        for c in range(CHUNKS):
-            z_t.append(keep.tile([P, SUBS, 2, P, 2], BF16, name="z_t%d" % c, tag="grouped%d" % c, align_bytes=64))
+            a_banks = [product_a(t, h) for h in range(HALVES)]
+            squares = [square_of_b(t, h) for h in range(HALVES)]
+            place(t - 1, 1 if t == 1 else 0, HALVES, "codes%d" % t)
+            for h in range(HALVES):
+                tanh_of_sum(t, h, a_banks[h], squares[h])
+        place(ROW_TILES - 1, 0, HALVES, "codes2")
+        for c, slot in enumerate(("raw1", "raw2", "w2_grouped", "tab_scale_rows")):
+            z_t.append(keep.tile([P, SUBS, 2, P, 2], BF16, name="z_t%d" % c, tag=slot, align_bytes=64))
         for t in range(ROW_TILES):
             add_base(t, 4 * (t % 2))
 
-        nc.scalar.mul(neg_limit[:], limit_sb[:], -1.0)
 
         outs = []
-        for n, slot in enumerate(("big0", GW_SLOTS[ROW_TILES * HALVES - 1])):
+        for n, slot in enumerate(("big0", "codes2")):
             tile = keep.tile([P, T2], F32, name="out_page%d" % n, tag=slot, align_bytes=64)
             nc.vector.memset(tile[:], 0.0)
             outs.append(tile)
@@ -242,17 +228,18 @@ def tile_list_pump_dock_check_kernel(tc, tab_words, tab_scales, offs, w1_words, 
         y = []
         z_q = []
 
-        def product(n, c, bank_no, engine_copy):
+        def product(n, lo, width, bank_no, engine_copy):
+            c, first = divmod(lo, CHUNK)
             codes, scales = z_q[c]
             y_bank = bank(bank_no, "y_bank")
-            nc.tensor.matmul_mx(out=y_bank[:], lhsT=w3_sb[:, cols(n, P)].bitcast(FP8X4), lhsT_scale=w3_sc[:, cols(n, P)],
-                                rhs=codes[:].bitcast(FP8X4), rhs_scale=scales[:], start=True, stop=True)
-            engine_copy(y[n][:, cols(c, CHUNK)], y_bank[:])
+            nc.tensor.matmul_mx(out=y_bank[:, 0:width], lhsT=w3_sb[:, cols(n, P)].bitcast(FP8X4), lhsT_scale=w3_sc[:, cols(n, P)],
+                                rhs=codes[:, first : first + width].bitcast(FP8X4), rhs_scale=scales[:, first : first + width],
+                                start=True, stop=True)
+            engine_copy(y[n][:, lo : lo + width], y_bank[:, 0:width])
 
-        y.append(keep.tile([P, T2], F32, name="y0", tag="big2", align_bytes=64))
         for c in range(CHUNKS):
             words = z_t[c][:].rearrange("q s u p e -> q (s u p e)").bitcast(F32)
-            codes = keep.tile([P, CHUNK], U32, name="z_codes%d" % c, tag="words%d" % c, align_bytes=64)
+            codes = keep.tile([P, CHUNK], U32, name="z_codes%d" % c, align_bytes=64)
             scales = keep.tile([P, CHUNK], U8, name="z_scales%d" % c, align_bytes=64)
             for h in range(2):
                 back = bank((2 * c + h) % 4, "back_bank")
@@ -270,26 +257,26 @@ def tile_list_pump_dock_check_kernel(tc, tab_words, tab_scales, offs, w1_words, 
                     nc.scalar.copy(z_words, src)
                 nc.vector.quantize_mx(out=codes[:, cols(h, 2 * P)].bitcast(FP8X4), scales=scales[:, cols(h, 2 * P)], in_=z[:])
             z_q.append((codes, scales))
-            product(0, c, 4 + c, nc.vector.tensor_copy if c == CHUNKS - 1 else nc.scalar.copy)
+
+        y.append(keep.tile([P, T2], F32, name="y0", tag="big2", align_bytes=64))
+        y.append(keep.tile([P, T2], F32, name="y1", tag="big1", align_bytes=64))
+        y.append(ring.tile([P, T2], F32, name="y2", tag="base_sb"))
+        for c in range(CHUNKS - 1):
+            product(0, c * CHUNK, CHUNK, c, nc.scalar.copy)
+        for h in range(2):
+            product(0, T2 - CHUNK + h * 2 * P, 2 * P, (3 + h) % 4, nc.vector.tensor_copy)
         for n in range(1, OUT_TILES):
-            if n == 1:
-                y.append(keep.tile([P, T2], F32, name="y1", tag="big1", align_bytes=64))
-            else:
-                y.append(ring.tile([P, T2], F32, name="y2", tag="base_sb"))
             for c in range(CHUNKS):
-                product(n, c, c, nc.scalar.copy)
+                product(n, c * CHUNK, CHUNK, 4 + c, nc.scalar.copy)
 
         picked = []
         for n in range(OUT_TILES):
-            for h in range(HALVES):
-                tile = keep.tile([P, HALF], F32, name="picked%d_%d" % (n, h), tag=GW_SLOTS[1 + n * HALVES + h], align_bytes=64)
-                nc.vector.tensor_copy(tile[:], y[n][:].indirect(half_of(offs3_sb, h)))
-                picked.append(tile)
+            tile = keep.tile([P, S], F32, name="picked%d" % n, tag="words%d" % n, align_bytes=64)
+            nc.vector.tensor_copy(tile[:], y[n][:].indirect(offs3_sb[:]))
+            picked.append(tile)
         for n in range(OUT_TILES):
-            for h in range(HALVES):
-                tile = picked[n * HALVES + h]
-                size = ring.tile([P, HALF], F32, name="size", tag="s1")
-                nc.scalar.activation(size[:], tile[:], ACT.Abs)
-                nc.scalar.activation(tile[:], size[:], ACT.Identity, bias=neg_limit[:, n : n + 1])
-                nc.vector.tensor_tensor(outs[n][:].indirect(half_of(offs4_sb, h)), tile[:], wgo_sb[:, cols(h, HALF)], ALU.mult)
+            size = keep.tile([P, S], F32, name="size", tag="size")
+            nc.scalar.activation(size[:], picked[n][:], ACT.Abs)
+            nc.scalar.activation(picked[n][:], size[:], ACT.Identity, bias=neg_limit[:, n : n + 1])
+            nc.vector.tensor_tensor(outs[n][:].indirect(offs4_sb[:]), picked[n][:], wgo_sb[:], ALU.mult)
             nc.sync.dma_start(out[cols(n, P), :], outs[n][:])

@@ -190,10 +190,20 @@ def tile_list_pump_dock_check_kernel(tc, tab_words, tab_scales, offs, w1_words, 
             nc.scalar.mul(gw[:], wgs_sb[:, entries], vecs[:, 4 + t : 5 + t])
             nc.vector.tensor_tensor(pages[t][:].indirect(offs2_sb[:, lo * LIST_COLS : hi * LIST_COLS]), th[:, t, entries], gw[:], ALU.mult)
 
+        def warm_tensor_engine(passes):
+            codes, scales = w2_q[0]
+            spare = bank(3, "spare_bank")
+            for i in range(passes):
+                nc.tensor.matmul_mx(out=spare[:], lhsT=codes[:, cols(0, P)].bitcast(FP8X4), lhsT_scale=scales[:, cols(0, P)],
+                                    rhs=v[0][:, cols(0, HALF)].bitcast(FP8X4), rhs_scale=v_sc[0][:, cols(0, HALF)],
+                                    start=True, stop=True)
+
         def add_base(t, first_bank):
             banks = [bank(first_bank + c, "sum_bank") for c in range(CHUNKS)]
             for src, is_page in ((base_sb[t], False), (pages[t], True)):
                 for c in range(CHUNKS):
+                    if is_page and t == ROW_TILES - 1 and c % 2 == 0:
+                        warm_tensor_engine(3 if c == 0 else 2)
                     for s in range(SUBS):
                         nc.tensor.matmul(banks[c][:, cols(s, P)], src[:, cols(c * SUBS + s, P)], ident[:], is_transpose=True,
                                          start=(s == 0 and not is_page), stop=(s == SUBS - 1 and is_page))

@@ -59,53 +59,74 @@ def tile_list_pump_dock_check_kernel(tc, tab_words, tab_scales, offs, w1_words, 
             nc.sync.dma_start(tile[:].bitcast(I32), tab_words[a].rearrange("p t i -> p (t i)").bitcast(I32))
             return tile
 
-        def load_w2(a):
-            tile = keep.tile([P, 4, H], F32, name="w2_raw%d" % a, tag="raw%d" % a, align_bytes=64)
-            nc.sync.dma_start(tile[:], w2[cols(a, 512), :].rearrange("(p j) c -> p j c", j=4))
+        def load_w2(t):
+            tiles = []
+            for a in range(PASSES):
+                tile = keep.tile([P, 4, P], F32, name="w2_raw%d_%d" % (t, a), tag="out1" if t + a == 0 else "raw%d_%d" % (t, a), align_bytes=64)
+                nc.sync.dma_start(tile[:], w2[cols(a, 512), cols(t, P)].rearrange("(p j) c -> p j c", j=4))
+                tiles.append(tile)
+            return tiles
+
+        def load_base(t):
+            tile = keep.tile([P, T2], F32, name="base%d" % t, tag="big%d" % t, align_bytes=64)
+            nc.sync.dma_start(tile[:], base[cols(t, P), :])
             return tile
 
-        tab_scale_rows = keep.tile([P, T], U8, name="tab_scale_rows", tag="tab_scale_rows", align_bytes=64)
+        tab_scale_rows = keep.tile([P, T], U8, name="tab_scale_rows", tag="out0", align_bytes=64)
         nc.vector.memset(tab_scale_rows[:].bitcast(I32), 0)
-        vec_rows = keep.tile([P, P], F32, name="vec_rows")
-        nc.vector.memset(vec_rows[:], 0.0)
         v_sc = [keep.tile([P, S], U8, name="v_sc%d" % a, align_bytes=64) for a in range(PASSES)]
         for a in range(1, PASSES):
             nc.vector.memset(v_sc[a][:].bitcast(I32), 0)
+        w3_sc = keep.tile([P, N], U8, name="w3_sc", align_bytes=64)
+        nc.vector.memset(w3_sc[:].bitcast(I32), 0)
 
         ident = keep.tile([P, P], F32, name="ident")
         make_identity(nc, ident[:])
         warm = keep.tile([P, 1], F32, name="warm")
         nc.scalar.activation(warm[:], ident[:, 0:1], ACT.Tanh)
+        vec_rows = keep.tile([P, P], F32, name="vec_rows")
+        nc.gpsimd.memset(vec_rows[:], 0.0)
+        nc.gpsimd.dma_start(vec_rows[0:4, :], curve.rearrange("(t p) -> t p", p=P))
+        nc.gpsimd.dma_start(vec_rows[4:8, :], gain.rearrange("(t p) -> t p", p=P))
+        nc.gpsimd.dma_start(vec_rows[8:11, :], limit.rearrange("(t p) -> t p", p=P))
         w1_sc = keep.tile([P, PASSES, H], U8, name="w1_sc", align_bytes=64)
-        nc.gpsimd.memset(w1_sc[:].rearrange("p a c -> p (a c)").bitcast(I32), 0)
-        for q in range(QUADS):
-            nc.gpsimd.dma_start(w1_sc[32 * q : 32 * q + 4, :, :].bitcast(I32),
-                                w1_scales[:, 4 * q : 4 * q + 4, :].rearrange("a r c -> r a c").bitcast(I32))
-        w3_sc = keep.tile([P, N], U8, name="w3_sc", align_bytes=64)
-        nc.vector.memset(w3_sc[:].bitcast(I32), 0)
+        nc.vector.memset(w1_sc[:].rearrange("p a c -> p (a c)").bitcast(I32), 0)
 
         offs_sb = load_list(offs, "offs_sb")
-        w2_raw = [load_w2(0)]
+        table = [load_table(0)]
         for q in range(QUADS):
             nc.sync.dma_start(tab_scale_rows[32 * q : 32 * q + 4 * PASSES, :].bitcast(I32),
                               tab_scales[:, 4 * q : 4 * q + 4, :].bitcast(I32))
-        w2_raw.append(load_w2(1))
-        nc.sync.dma_start(vec_rows[0:4, :], curve.rearrange("(t p) -> t p", p=P))
-        nc.sync.dma_start(vec_rows[4:8, :], gain.rearrange("(t p) -> t p", p=P))
-        nc.sync.dma_start(vec_rows[8:11, :], limit.rearrange("(t p) -> t p", p=P))
-        w2_raw.append(load_w2(2))
-        table = [load_table(0), load_table(1)]
-        w1_sb = keep.tile([P, PASSES, 2 * H], U8, name="w1_sb", align_bytes=64)
-        nc.sync.dma_start(w1_sb[:].bitcast(I32), w1_words.rearrange("a p c -> p a c").bitcast(I32))
+        table.append(load_table(1))
+        w2_raw = [load_w2(0)]
+        w1_view = w1_words.rearrange("a p c -> p a c")
+        w1_first = keep.tile([P, PASSES, 2 * P], U8, name="w1_first", align_bytes=64)
+        nc.sync.dma_start(w1_first[:].bitcast(I32), w1_view[:, :, 0 : 2 * P].bitcast(I32))
+        for q in range(QUADS):
+            nc.sync.dma_start(w1_sc[32 * q : 32 * q + 4, :, :].bitcast(I32),
+                              w1_scales[:, 4 * q : 4 * q + 4, :].rearrange("a r c -> r a c").bitcast(I32))
         table.append(load_table(2))
+
+        v = [keep.tile([P, S], U32, name="v%d" % a, tag="words%d" % a, align_bytes=64) for a in range(PASSES)]
+        nc.vector.tensor_copy(v[0][:], table[0][:].indirect(offs_sb[:]))
         nc.vector.tensor_copy(v_sc[0][:], tab_scale_rows[:].indirect(offs_sb[:]))
         for a in range(1, PASSES):
             nc.sync.dma_start(v_sc[a][0:SHIFT_ROWS, :].bitcast(I32),
                               v_sc[0][4 * a : 4 * a + SHIFT_ROWS, :].bitcast(I32))
+        nc.vector.tensor_copy(v[1][:], table[1][:].indirect(offs_sb[:]))
+
         wgs_sb = keep.tile([P, S], F32, name="wgs_sb")
-        for h in range(HALVES):
-            nc.sync.dma_start(wgs_sb[:, cols(h, HALF)], wgs[:, cols(h, HALF)])
+        nc.sync.dma_start(wgs_sb[:, cols(0, HALF)], wgs[:, cols(0, HALF)])
         offs2_sb = load_list(offs2, "offs2_sb")
+        w2_raw.append(load_w2(1))
+        w1_rest = keep.tile([P, PASSES, 2 * (H - P)], U8, name="w1_rest", align_bytes=64)
+        nc.sync.dma_start(w1_rest[:].bitcast(I32), w1_view[:, :, 2 * P : 2 * H].bitcast(I32))
+        nc.sync.dma_start(wgs_sb[:, cols(1, HALF)], wgs[:, cols(1, HALF)])
+        w2_raw.append(load_w2(2))
+        base_sb = [load_base(0)]
+        w2_raw.append(load_w2(3))
+        for t in range(1, ROW_TILES):
+            base_sb.append(load_base(t))
         w3_sb = keep.tile([P, N], U32, name="w3_sb", align_bytes=64)
         nc.sync.dma_start(w3_sb[:].bitcast(I32), w3_words[0].rearrange("p c i -> p (c i)").bitcast(I32))
         for q in range(QUADS):
@@ -114,11 +135,6 @@ def tile_list_pump_dock_check_kernel(tc, tab_words, tab_scales, offs, w1_words, 
         offs4_sb = load_list(offs4, "offs4_sb")
         wgo_sb = keep.tile([P, S], F32, name="wgo_sb")
         nc.sync.dma_start(wgo_sb[:], wgo)
-        base_sb = []
-        for t in range(ROW_TILES):
-            tile = ring.tile([P, T2], F32, name="base_sb")
-            nc.sync.dma_start(tile[:], base[cols(t, P), :])
-            base_sb.append(tile)
 
         vec_bank = bank(7, "vec_bank")
         nc.tensor.transpose(vec_bank[:, 0:P], vec_rows[:], ident[:])
@@ -127,115 +143,114 @@ def tile_list_pump_dock_check_kernel(tc, tab_words, tab_scales, offs, w1_words, 
         neg_limit = keep.tile([P, OUT_TILES], F32, name="neg_limit")
         nc.scalar.mul(neg_limit[:], vec_bank[:, 8:11], -1.0)
 
-
-        w2_grouped = keep.tile([P, ROW_TILES, PASSES, P, 4], BF16, name="w2_grouped", tag="w2_grouped", align_bytes=64)
-
-        def quantize_w2(t):
-            codes = keep.tile([P, PASSES * P], U32, name="w2_codes%d" % t, tag="codes%d" % t, align_bytes=64)
-            scales = keep.tile([P, PASSES * P], U8, name="w2_scales%d" % t, tag="scales%d" % t, align_bytes=64)
-            flat = w2_grouped[:, t, :, :, :].rearrange("p a c j -> p (a c j)")
-            for lo, hi in ((0, 2 * P), (2 * P, 3 * P)):
-                nc.vector.quantize_mx(out=codes[:, lo:hi].bitcast(FP8X4), scales=scales[:, lo:hi], in_=flat[:, 4 * lo : 4 * hi])
-            return codes, scales
-
-        for a in range(PASSES):
-            nc.scalar.copy(w2_grouped[:, :, a, :, :], w2_raw[a][:].rearrange("p j (t c) -> p t c j", t=ROW_TILES))
-        w2_q = [quantize_w2(t) for t in range(ROW_TILES)]
-
-        v = []
-        for a in range(PASSES):
-            tile = keep.tile([P, S], U32, name="v%d" % a, tag="words%d" % a, align_bytes=64)
-            if a + 1 < PASSES:
-                nc.vector.tensor_copy(tile[:], table[a][:].indirect(offs_sb[:]))
-            else:
-                for h in range(HALVES):
-                    nc.vector.tensor_copy(tile[:, cols(h, HALF)], table[a][:].indirect(half_of(offs_sb, h)))
-            v.append(tile)
-
-        pages = [keep.tile([P, T2], F32, name="page%d" % t) for t in range(ROW_TILES)]
-        last_out = keep.tile([P, T2], F32, name="last_out")
-        for tile in pages + [last_out]:
+        pages = [keep.tile([P, T2], F32, name="page%d" % i) for i in range(2)]
+        for tile in pages:
             nc.vector.memset(tile[:], 0.0)
 
-        th = keep.tile([P, ROW_TILES, S], F32, name="th", tag="big0", align_bytes=64)
-        z_t = []
+        w2_q = []
+
+        def quantize_w2(t, slot, codes_slot):
+            grouped = keep.tile([P, PASSES, P, 4], BF16, name="w2_grouped%d" % t, tag=slot, align_bytes=64)
+            for a in range(PASSES):
+                nc.scalar.copy(grouped[:, a, :, :], w2_raw[t][a][:].rearrange("p j c -> p c j"))
+            codes = keep.tile([P, PASSES * P], U32, name="w2_codes%d" % t, tag=codes_slot, align_bytes=64)
+            scales = keep.tile([P, PASSES * P], U8, name="w2_scales%d" % t, align_bytes=64)
+            flat = grouped[:].rearrange("p a c j -> p (a c j)")
+            for lo, hi in ((0, 2 * P), (2 * P, 3 * P)):
+                nc.vector.quantize_mx(out=codes[:, lo:hi].bitcast(FP8X4), scales=scales[:, lo:hi], in_=flat[:, 4 * lo : 4 * hi])
+            w2_q.append((codes, scales))
+
+        quantize_w2(0, "grouped0", "codes0")
+        outs = [keep.tile([P, T2], F32, name="out_page%d" % i, tag="out%d" % i, align_bytes=64) for i in range(2)]
+        for tile in outs:
+            nc.vector.memset(tile[:], 0.0)
+        for h in range(HALVES):
+            nc.vector.tensor_copy(v[2][:, cols(h, HALF)], table[2][:].indirect(half_of(offs_sb, h)))
+
+        z_t = [keep.tile([P, 2 * SUBS * 2, P], F32, name="z_t%d" % i, align_bytes=64) for i in range(2)]
+        th = [keep.tile([P, HALF], F32, name="th%d" % h) for h in range(HALVES)]
 
         def product_a(t, h):
-            a_bank = bank(4 * (t % 2) + HALVES + h, "a_bank")
+            a_bank = bank(HALVES * ((t + 1) % 2) + h, "a_bank")
             for a in range(PASSES):
-                nc.tensor.matmul_mx(out=a_bank[:], lhsT=w1_sb[:, a, cols(t, 2 * P)].bitcast(FP4X4), lhsT_scale=w1_sc[:, a, cols(t, P)],
+                w1_cols = w1_first[:, a, :] if t == 0 else w1_rest[:, a, cols(t - 1, 2 * P)]
+                nc.tensor.matmul_mx(out=a_bank[:], lhsT=w1_cols.bitcast(FP4X4), lhsT_scale=w1_sc[:, a, cols(t, P)],
                                     rhs=v[a][:, cols(h, HALF)].bitcast(FP8X4), rhs_scale=v_sc[a][:, cols(h, HALF)],
                                     start=(a == 0), stop=(a == PASSES - 1))
             return a_bank
 
         def square_of_b(t, h):
             codes, scales = w2_q[t]
-            b_bank = bank(4 * (t % 2) + h, "b_bank")
+            b_bank = bank(HALVES * (t % 2) + h, "b_bank")
             for a in range(PASSES):
                 nc.tensor.matmul_mx(out=b_bank[:], lhsT=codes[:, cols(a, P)].bitcast(FP8X4), lhsT_scale=scales[:, cols(a, P)],
-                                    rhs=v[a][:, cols(h, HALF)].bitcast(FP8X4), rhs_scale=v_sc[a][:, cols(h, HALF)],
+                                    rhs=v[a][:, cols(h, HALF)].bitcast(FP8X4), rhs_scale=v_sc[0][4 * a : P, cols(h, HALF)],
                                     start=(a == 0), stop=(a == PASSES - 1))
-            sq = ring.tile([P, HALF], F32, name="sq")
+            slot = "first%d" % (t % 3) if h == 0 else "second%d" % (t % 2)
+            sq = keep.tile([P, HALF], F32, name="sq%d_%d" % (t, h), tag=slot, align_bytes=64)
             nc.scalar.activation(sq[:], b_bank[:], ACT.Square)
             return sq
 
+        def runs(ap):
+            return ap.rearrange("p (g w) -> p g w", w=32)
+
         def tanh_of_sum(t, h, a_bank, sq):
-            u = ring.tile([P, HALF], F32, name="u")
-            nc.vector.scalar_tensor_tensor(u[:], sq[:], vecs[:, t : t + 1], a_bank[:], ALU.mult, ALU.add)
-            nc.scalar.activation(th[:, t, cols(h, HALF)], u[:], ACT.Tanh)
+            u = z_t[h][:, :, cols((t - 1) % ROW_TILES, 32)]
+            nc.vector.scalar_tensor_tensor(u, runs(sq[:]), vecs[:, t : t + 1], runs(a_bank[:]), ALU.mult, ALU.add)
+            nc.scalar.activation(runs(th[h][:]), u, ACT.Tanh)
 
-        def place(t, lo, hi, slot):
-            entries = slice(lo * HALF, hi * HALF)
+        def weigh(t, lo, hi, slot):
             gw = keep.tile([P, (hi - lo) * HALF], F32, name="gw%d_%d" % (t, lo), tag=slot, align_bytes=64)
-            nc.scalar.mul(gw[:], wgs_sb[:, entries], vecs[:, 4 + t : 5 + t])
-            nc.vector.tensor_tensor(pages[t][:].indirect(offs2_sb[:, lo * LIST_COLS : hi * LIST_COLS]), th[:, t, entries], gw[:], ALU.mult)
+            nc.scalar.mul(gw[:], wgs_sb[:, lo * HALF : hi * HALF], vecs[:, 4 + t : 5 + t])
+            return gw
 
-        def warm_tensor_engine(passes):
-            codes, scales = w2_q[0]
-            spare = bank(3, "spare_bank")
-            for i in range(passes):
-                nc.tensor.matmul_mx(out=spare[:], lhsT=codes[:, cols(0, P)].bitcast(FP8X4), lhsT_scale=scales[:, cols(0, P)],
-                                    rhs=v[0][:, cols(0, HALF)].bitcast(FP8X4), rhs_scale=v_sc[0][:, cols(0, HALF)],
-                                    start=True, stop=True)
+        def place(t, h, gw):
+            nc.vector.tensor_tensor(pages[t % 2][:].indirect(half_of(offs2_sb, h)), th[h][:], gw, ALU.mult)
 
-        def add_base(t, first_bank):
-            banks = [bank(first_bank + c, "sum_bank") for c in range(CHUNKS)]
-            for src, is_page in ((base_sb[t], False), (pages[t], True)):
-                for c in range(CHUNKS):
-                    if is_page and t == ROW_TILES - 1 and c % 2 == 0:
-                        warm_tensor_engine(3 if c == 0 else 2)
-                    for s in range(SUBS):
-                        nc.tensor.matmul(banks[c][:, cols(s, P)], src[:, cols(c * SUBS + s, P)], ident[:], is_transpose=True,
-                                         start=(s == 0 and not is_page), stop=(s == SUBS - 1 and is_page))
+        def add_transposed(banks, src, first):
             for c in range(CHUNKS):
-                nc.scalar.copy(z_t[c][:, :, :, cols(t, 32), :],
-                               banks[c][:].rearrange("q (s p u e) -> q s u p e", s=SUBS, u=2, e=2))
+                for s in range(SUBS):
+                    nc.tensor.matmul(banks[c][:, cols(s, P)], src[:, cols(c * SUBS + s, P)], ident[:], is_transpose=True,
+                                     start=(s == 0 and first), stop=(s == SUBS - 1 and not first))
 
-        for h in range(HALVES):
-            sq = square_of_b(0, h)
-            tanh_of_sum(0, h, product_a(0, h), sq)
-        place(0, 0, 1, "raw0")
+        def round_sum(t, c, sum_bank, engine_copy):
+            halves = z_t[c // 2][:].rearrange("q g w -> q (g w)").bitcast(BF16).rearrange(
+                "q (c s u p e) -> q c s u p e", c=2, s=SUBS, u=2, e=2)
+            engine_copy(halves[:, c % 2, :, :, cols(t, 32), :],
+                        sum_bank[:].rearrange("q (s p u e) -> q s u p e", s=SUBS, u=2, e=2))
+
+        def add_base(t):
+            banks = [bank(4 + c, "sum_bank") for c in range(CHUNKS)]
+            add_transposed(banks, base_sb[t], True)
+            add_transposed(banks, pages[t % 2], False)
+            return banks
+
+        sq = square_of_b(0, 0)
+        gw = weigh(0, 0, 1, "first2")
+        tanh_of_sum(0, 0, product_a(0, 0), sq)
+        sq = square_of_b(0, 1)
+        tanh_of_sum(0, 1, product_a(0, 1), sq)
+        place(0, 0, gw[:])
+        quantize_w2(1, "grouped1", "codes1")
+        place(0, 1, weigh(0, 1, 2, "grouped1")[:])
+        gw = weigh(1, 0, 2, "first0")
         for t in range(1, ROW_TILES):
             a_banks = [product_a(t, h) for h in range(HALVES)]
             squares = [square_of_b(t, h) for h in range(HALVES)]
-            place(t - 1, 1 if t == 1 else 0, HALVES, "codes%d" % t)
+            sum_banks = add_base(t - 1)
             for h in range(HALVES):
                 tanh_of_sum(t, h, a_banks[h], squares[h])
-        place(ROW_TILES - 1, 0, HALVES, "codes2")
-        for c, slot in enumerate(("raw1", "raw2", "w2_grouped", "tab_scale_rows")):
-            z_t.append(keep.tile([P, SUBS, 2, P, 2], BF16, name="z_t%d" % c, tag=slot, align_bytes=64))
-        for t in range(ROW_TILES):
-            add_base(t, 4 * (t % 2))
+            if t + 1 < ROW_TILES:
+                quantize_w2(t + 1, "grouped0", "second%d" % (t % 2))
+            for h in range(HALVES):
+                place(t, h, gw[:, cols(h, HALF)])
+            if t + 1 < ROW_TILES:
+                gw = weigh(t + 1, 0, 2, "first%d" % (t % 3))
+            for c in range(CHUNKS):
+                round_sum(t - 1, c, sum_banks[c], nc.scalar.copy)
+        sum_banks = add_base(ROW_TILES - 1)
 
-
-        outs = []
-        for n, slot in enumerate(("big0", "codes2")):
-            tile = keep.tile([P, T2], F32, name="out_page%d" % n, tag=slot, align_bytes=64)
-            nc.vector.memset(tile[:], 0.0)
-            outs.append(tile)
-        outs.append(last_out)
-
-        y = []
+        y = [keep.tile([P, T2], F32, name="y%d" % n, tag="big%d" % n, align_bytes=64) for n in range(OUT_TILES)]
         z_q = []
 
         def product(n, lo, width, bank_no, engine_copy):
@@ -248,17 +263,15 @@ def tile_list_pump_dock_check_kernel(tc, tab_words, tab_scales, offs, w1_words, 
             engine_copy(y[n][:, lo : lo + width], y_bank[:, 0:width])
 
         for c in range(CHUNKS):
-            words = z_t[c][:].rearrange("q s u p e -> q (s u p e)").bitcast(F32)
+            round_sum(ROW_TILES - 1, c, sum_banks[c], nc.vector.tensor_copy if c % 2 == 0 else nc.scalar.copy)
+        for c in range(CHUNKS):
             codes = keep.tile([P, CHUNK], U32, name="z_codes%d" % c, align_bytes=64)
             scales = keep.tile([P, CHUNK], U8, name="z_scales%d" % c, align_bytes=64)
             for h in range(2):
                 back = bank((2 * c + h) % 4, "back_bank")
                 for i in range(4):
-                    nc.tensor.transpose(back[:, cols(i, P)], words[:, cols(4 * h + i, P)], ident[:])
-                if c == CHUNKS - 1 and h == 1:
-                    z = keep.tile([P, 2 * P * 4], BF16, name="z_last", tag="big1", align_bytes=64)
-                else:
-                    z = ring.tile([P, 2 * P * 4], BF16, name="z", tag="z%d" % h, align_bytes=64)
+                    nc.tensor.transpose(back[:, cols(i, P)], z_t[c // 2][:, 8 * (c % 2) + 4 * h + i, :], ident[:])
+                z = ring.tile([P, 2 * P * 4], BF16, name="z", tag="z%d" % h, align_bytes=64)
                 z_words = z[:].bitcast(F32).rearrange("p (s q u) -> p s q u", s=2, u=2)
                 src = back[:].rearrange("p (s u q) -> p s q u", s=2, u=2)
                 if h == 0:
@@ -267,17 +280,13 @@ def tile_list_pump_dock_check_kernel(tc, tab_words, tab_scales, offs, w1_words, 
                     nc.scalar.copy(z_words, src)
                 nc.vector.quantize_mx(out=codes[:, cols(h, 2 * P)].bitcast(FP8X4), scales=scales[:, cols(h, 2 * P)], in_=z[:])
             z_q.append((codes, scales))
-
-        y.append(keep.tile([P, T2], F32, name="y0", tag="big2", align_bytes=64))
-        y.append(keep.tile([P, T2], F32, name="y1", tag="big1", align_bytes=64))
-        y.append(ring.tile([P, T2], F32, name="y2", tag="base_sb"))
-        for c in range(CHUNKS - 1):
-            product(0, c * CHUNK, CHUNK, c, nc.scalar.copy)
-        for h in range(2):
-            product(0, T2 - CHUNK + h * 2 * P, 2 * P, (3 + h) % 4, nc.vector.tensor_copy)
+            if c + 1 < CHUNKS:
+                product(0, c * CHUNK, CHUNK, 4 + c, nc.scalar.copy)
+        product(0, T2 - CHUNK, 2 * P, 7, nc.scalar.copy)
+        product(0, T2 - 2 * P, 2 * P, 4, nc.vector.tensor_copy)
         for n in range(1, OUT_TILES):
             for c in range(CHUNKS):
-                product(n, c * CHUNK, CHUNK, 4 + c, nc.scalar.copy)
+                product(n, c * CHUNK, CHUNK, c, nc.scalar.copy)
 
         picked = []
         for n in range(OUT_TILES):
@@ -288,5 +297,5 @@ def tile_list_pump_dock_check_kernel(tc, tab_words, tab_scales, offs, w1_words, 
             size = keep.tile([P, S], F32, name="size", tag="size")
             nc.scalar.activation(size[:], picked[n][:], ACT.Abs)
             nc.scalar.activation(picked[n][:], size[:], ACT.Identity, bias=neg_limit[:, n : n + 1])
-            nc.vector.tensor_tensor(outs[n][:].indirect(offs4_sb[:]), picked[n][:], wgo_sb[:], ALU.mult)
-            nc.sync.dma_start(out[cols(n, P), :], outs[n][:])
+            nc.vector.tensor_tensor(outs[n % 2][:].indirect(offs4_sb[:]), picked[n][:], wgo_sb[:], ALU.mult)
+            nc.sync.dma_start(out[cols(n, P), :], outs[n % 2][:])

@@ -29,6 +29,7 @@ CHUNKS = T2 // CHUNK
 SUBS = CHUNK // P
 QUADS = 4
 SHIFT_ROWS = 112
+WARM_PASSES = 6
 
 
 def tile_list_pump_dock_check_kernel(tc, tab_words, tab_scales, offs, w1_words, w1_scales, w2, curve, gain,
@@ -62,7 +63,7 @@ def tile_list_pump_dock_check_kernel(tc, tab_words, tab_scales, offs, w1_words, 
         def load_w2(t):
             tiles = []
             for a in range(PASSES):
-                tile = keep.tile([P, 4, P], F32, name="w2_raw%d_%d" % (t, a), tag="out1" if t + a == 0 else "raw%d_%d" % (t, a), align_bytes=64)
+                tile = keep.tile([P, 4, P], F32, name="w2_raw%d_%d" % (t, a), tag="out%d" % a if t == 0 and a < 2 else "raw%d_%d" % (t, a), align_bytes=64)
                 nc.sync.dma_start(tile[:], w2[cols(a, 512), cols(t, P)].rearrange("(p j) c -> p j c", j=4))
                 tiles.append(tile)
             return tiles
@@ -72,7 +73,7 @@ def tile_list_pump_dock_check_kernel(tc, tab_words, tab_scales, offs, w1_words, 
             nc.sync.dma_start(tile[:], base[cols(t, P), :])
             return tile
 
-        tab_scale_rows = keep.tile([P, T], U8, name="tab_scale_rows", tag="out0", align_bytes=64)
+        tab_scale_rows = keep.tile([P, T], U8, name="tab_scale_rows", tag="words1", align_bytes=64)
         nc.vector.memset(tab_scale_rows[:].bitcast(I32), 0)
         v_sc = [keep.tile([P, S], U8, name="v_sc%d" % a, align_bytes=64) for a in range(PASSES)]
         for a in range(1, PASSES):
@@ -82,13 +83,10 @@ def tile_list_pump_dock_check_kernel(tc, tab_words, tab_scales, offs, w1_words, 
 
         ident = keep.tile([P, P], F32, name="ident")
         make_identity(nc, ident[:])
-        warm = keep.tile([P, 1], F32, name="warm")
-        nc.scalar.activation(warm[:], ident[:, 0:1], ACT.Tanh)
         vec_rows = keep.tile([P, P], F32, name="vec_rows")
-        nc.gpsimd.memset(vec_rows[:], 0.0)
-        nc.gpsimd.dma_start(vec_rows[0:4, :], curve.rearrange("(t p) -> t p", p=P))
-        nc.gpsimd.dma_start(vec_rows[4:8, :], gain.rearrange("(t p) -> t p", p=P))
-        nc.gpsimd.dma_start(vec_rows[8:11, :], limit.rearrange("(t p) -> t p", p=P))
+        nc.vector.memset(vec_rows[:], 0.0)
+        limit_rows = keep.tile([P, P], F32, name="limit_rows")
+        nc.vector.memset(limit_rows[:], 0.0)
         w1_sc = keep.tile([P, PASSES, H], U8, name="w1_sc", align_bytes=64)
         nc.vector.memset(w1_sc[:].rearrange("p a c -> p (a c)").bitcast(I32), 0)
 
@@ -98,6 +96,8 @@ def tile_list_pump_dock_check_kernel(tc, tab_words, tab_scales, offs, w1_words, 
             nc.sync.dma_start(tab_scale_rows[32 * q : 32 * q + 4 * PASSES, :].bitcast(I32),
                               tab_scales[:, 4 * q : 4 * q + 4, :].bitcast(I32))
         table.append(load_table(1))
+        nc.sync.dma_start(vec_rows[0:4, :], curve.rearrange("(t p) -> t p", p=P))
+        nc.sync.dma_start(vec_rows[4:8, :], gain.rearrange("(t p) -> t p", p=P))
         w2_raw = [load_w2(0)]
         w1_view = w1_words.rearrange("a p c -> p a c")
         w1_first = keep.tile([P, PASSES, 2 * P], U8, name="w1_first", align_bytes=64)
@@ -107,12 +107,13 @@ def tile_list_pump_dock_check_kernel(tc, tab_words, tab_scales, offs, w1_words, 
                               w1_scales[:, 4 * q : 4 * q + 4, :].rearrange("a r c -> r a c").bitcast(I32))
         table.append(load_table(2))
 
-        v = [keep.tile([P, S], U32, name="v%d" % a, tag="words%d" % a, align_bytes=64) for a in range(PASSES)]
+        v = [keep.tile([P, S], U32, name="v0", tag="words0", align_bytes=64)]
         nc.vector.tensor_copy(v[0][:], table[0][:].indirect(offs_sb[:]))
         nc.vector.tensor_copy(v_sc[0][:], tab_scale_rows[:].indirect(offs_sb[:]))
         for a in range(1, PASSES):
             nc.sync.dma_start(v_sc[a][0:SHIFT_ROWS, :].bitcast(I32),
                               v_sc[0][4 * a : 4 * a + SHIFT_ROWS, :].bitcast(I32))
+        v.extend(keep.tile([P, S], U32, name="v%d" % a, tag="words%d" % a, align_bytes=64) for a in range(1, PASSES))
         nc.vector.tensor_copy(v[1][:], table[1][:].indirect(offs_sb[:]))
 
         wgs_sb = keep.tile([P, S], F32, name="wgs_sb")
@@ -131,6 +132,7 @@ def tile_list_pump_dock_check_kernel(tc, tab_words, tab_scales, offs, w1_words, 
         nc.sync.dma_start(w3_sb[:].bitcast(I32), w3_words[0].rearrange("p c i -> p (c i)").bitcast(I32))
         for q in range(QUADS):
             nc.sync.dma_start(w3_sc[32 * q : 32 * q + 4, :].bitcast(I32), w3_scales[0, 4 * q : 4 * q + 4, :].bitcast(I32))
+        nc.sync.dma_start(limit_rows[0:OUT_TILES, :], limit.rearrange("(t p) -> t p", p=P))
         offs3_sb = load_list(offs3, "offs3_sb")
         offs4_sb = load_list(offs4, "offs4_sb")
         wgo_sb = keep.tile([P, S], F32, name="wgo_sb")
@@ -140,12 +142,12 @@ def tile_list_pump_dock_check_kernel(tc, tab_words, tab_scales, offs, w1_words, 
         nc.tensor.transpose(vec_bank[:, 0:P], vec_rows[:], ident[:])
         vecs = keep.tile([P, 8], F32, name="vecs")
         nc.scalar.copy(vecs[:], vec_bank[:, 0:8])
-        neg_limit = keep.tile([P, OUT_TILES], F32, name="neg_limit")
-        nc.scalar.mul(neg_limit[:], vec_bank[:, 8:11], -1.0)
 
         pages = [keep.tile([P, T2], F32, name="page%d" % i) for i in range(2)]
         for tile in pages:
             nc.vector.memset(tile[:], 0.0)
+        warm = keep.tile([P, 1], F32, name="warm")
+        nc.scalar.activation(warm[:], pages[0][:, 0:1], ACT.Tanh)
 
         w2_q = []
 
@@ -168,7 +170,8 @@ def tile_list_pump_dock_check_kernel(tc, tab_words, tab_scales, offs, w1_words, 
             nc.vector.tensor_copy(v[2][:, cols(h, HALF)], table[2][:].indirect(half_of(offs_sb, h)))
 
         z_t = [keep.tile([P, 2 * SUBS * 2, P], F32, name="z_t%d" % i, align_bytes=64) for i in range(2)]
-        th = [keep.tile([P, HALF], F32, name="th%d" % h) for h in range(HALVES)]
+        th = {}
+        neg_limit = []
 
         def product_a(t, h):
             a_bank = bank(HALVES * ((t + 1) % 2) + h, "a_bank")
@@ -197,7 +200,9 @@ def tile_list_pump_dock_check_kernel(tc, tab_words, tab_scales, offs, w1_words, 
         def tanh_of_sum(t, h, a_bank, sq):
             u = z_t[h][:, :, cols((t - 1) % ROW_TILES, 32)]
             nc.vector.scalar_tensor_tensor(u, runs(sq[:]), vecs[:, t : t + 1], runs(a_bank[:]), ALU.mult, ALU.add)
-            nc.scalar.activation(runs(th[h][:]), u, ACT.Tanh)
+            tile = keep.tile([P, HALF], F32, name="th%d_%d" % (t, h), tag="th%d" % h)
+            nc.scalar.activation(runs(tile[:]), u, ACT.Tanh)
+            th[h] = tile
 
         def weigh(t, lo, hi, slot):
             gw = keep.tile([P, (hi - lo) * HALF], F32, name="gw%d_%d" % (t, lo), tag=slot, align_bytes=64)
@@ -206,6 +211,19 @@ def tile_list_pump_dock_check_kernel(tc, tab_words, tab_scales, offs, w1_words, 
 
         def place(t, h, gw):
             nc.vector.tensor_tensor(pages[t % 2][:].indirect(half_of(offs2_sb, h)), th[h][:], gw, ALU.mult)
+
+        def limits_and_warm_up():
+            limit_bank = bank(7, "limit_bank")
+            nc.tensor.transpose(limit_bank[:, 0:P], limit_rows[:], ident[:])
+            tile = keep.tile([P, OUT_TILES], F32, name="neg_limit")
+            nc.scalar.mul(tile[:], limit_bank[:, 0:OUT_TILES], -1.0)
+            neg_limit.append(tile)
+            codes, scales = w2_q[0]
+            spare = bank(7, "spare_bank")
+            for i in range(WARM_PASSES):
+                nc.tensor.matmul_mx(out=spare[:], lhsT=codes[:, cols(0, P)].bitcast(FP8X4), lhsT_scale=scales[:, cols(0, P)],
+                                    rhs=v[0][:, cols(0, HALF)].bitcast(FP8X4), rhs_scale=v_sc[0][:, cols(0, HALF)],
+                                    start=True, stop=True)
 
         def add_transposed(banks, src, first):
             for c in range(CHUNKS):
@@ -242,12 +260,14 @@ def tile_list_pump_dock_check_kernel(tc, tab_words, tab_scales, offs, w1_words, 
                 tanh_of_sum(t, h, a_banks[h], squares[h])
             if t + 1 < ROW_TILES:
                 quantize_w2(t + 1, "grouped0", "second%d" % (t % 2))
-            for h in range(HALVES):
-                place(t, h, gw[:, cols(h, HALF)])
+            place(t, 0, gw[:, cols(0, HALF)])
             if t + 1 < ROW_TILES:
+                place(t, 1, gw[:, cols(1, HALF)])
                 gw = weigh(t + 1, 0, 2, "first%d" % (t % 3))
             for c in range(CHUNKS):
                 round_sum(t - 1, c, sum_banks[c], nc.scalar.copy)
+        limits_and_warm_up()
+        place(ROW_TILES - 1, 1, gw[:, cols(1, HALF)])
         sum_banks = add_base(ROW_TILES - 1)
 
         y = [keep.tile([P, T2], F32, name="y%d" % n, tag="big%d" % n, align_bytes=64) for n in range(OUT_TILES)]
@@ -296,6 +316,6 @@ def tile_list_pump_dock_check_kernel(tc, tab_words, tab_scales, offs, w1_words, 
         for n in range(OUT_TILES):
             size = keep.tile([P, S], F32, name="size", tag="size")
             nc.scalar.activation(size[:], picked[n][:], ACT.Abs)
-            nc.scalar.activation(picked[n][:], size[:], ACT.Identity, bias=neg_limit[:, n : n + 1])
+            nc.scalar.activation(picked[n][:], size[:], ACT.Identity, bias=neg_limit[0][:, n : n + 1])
             nc.vector.tensor_tensor(outs[n % 2][:].indirect(offs4_sb[:]), picked[n][:], wgo_sb[:], ALU.mult)
             nc.sync.dma_start(out[cols(n, P), :], outs[n % 2][:])

@@ -30,6 +30,8 @@ SUBS = CHUNK // P
 QUADS = 4
 SHIFT_ROWS = 112
 WARM_PASSES = 6
+SQUARE_SLOTS = (("slot_a", "slot_b"), ("slot_c", "slot_d"), ("slot_e", "slot_f"), ("slot_a", "slot_b"))
+WEIGHT_SLOTS = ("slot_e", "slot_a", "slot_c", "slot_e")
 
 
 def tile_list_pump_dock_check_kernel(tc, tab_words, tab_scales, offs, w1_words, w1_scales, w2, curve, gain,
@@ -60,13 +62,13 @@ def tile_list_pump_dock_check_kernel(tc, tab_words, tab_scales, offs, w1_words, 
             nc.sync.dma_start(tile[:].bitcast(I32), tab_words[a].rearrange("p t i -> p (t i)").bitcast(I32))
             return tile
 
-        def load_w2(t):
+        def load_w2(first, count):
             tiles = []
             for a in range(PASSES):
-                tile = keep.tile([P, 4, P], F32, name="w2_raw%d_%d" % (t, a), tag="out%d" % a if t == 0 and a < 2 else "raw%d_%d" % (t, a), align_bytes=64)
-                nc.sync.dma_start(tile[:], w2[cols(a, 512), cols(t, P)].rearrange("(p j) c -> p j c", j=4))
+                tile = keep.tile([P, 4, count * P], F32, name="w2_raw%d_%d" % (first, a), align_bytes=64)
+                nc.sync.dma_start(tile[:], w2[cols(a, 512), first * P : (first + count) * P].rearrange("(p j) c -> p j c", j=4))
                 tiles.append(tile)
-            return tiles
+            return [[tile[:, :, cols(i, P)] for tile in tiles] for i in range(count)]
 
         def load_base(t):
             tile = keep.tile([P, T2], F32, name="base%d" % t, tag="big%d" % t, align_bytes=64)
@@ -98,7 +100,7 @@ def tile_list_pump_dock_check_kernel(tc, tab_words, tab_scales, offs, w1_words, 
         table.append(load_table(1))
         nc.sync.dma_start(vec_rows[0:4, :], curve.rearrange("(t p) -> t p", p=P))
         nc.sync.dma_start(vec_rows[4:8, :], gain.rearrange("(t p) -> t p", p=P))
-        w2_raw = [load_w2(0)]
+        w2_raw = load_w2(0, 2)
         w1_view = w1_words.rearrange("a p c -> p a c")
         w1_first = keep.tile([P, PASSES, 2 * P], U8, name="w1_first", align_bytes=64)
         nc.sync.dma_start(w1_first[:].bitcast(I32), w1_view[:, :, 0 : 2 * P].bitcast(I32))
@@ -119,15 +121,12 @@ def tile_list_pump_dock_check_kernel(tc, tab_words, tab_scales, offs, w1_words, 
         wgs_sb = keep.tile([P, S], F32, name="wgs_sb")
         nc.sync.dma_start(wgs_sb[:, cols(0, HALF)], wgs[:, cols(0, HALF)])
         offs2_sb = load_list(offs2, "offs2_sb")
-        w2_raw.append(load_w2(1))
+        w2_raw.extend(load_w2(2, 1))
         w1_rest = keep.tile([P, PASSES, 2 * (H - P)], U8, name="w1_rest", align_bytes=64)
         nc.sync.dma_start(w1_rest[:].bitcast(I32), w1_view[:, :, 2 * P : 2 * H].bitcast(I32))
         nc.sync.dma_start(wgs_sb[:, cols(1, HALF)], wgs[:, cols(1, HALF)])
-        w2_raw.append(load_w2(2))
-        base_sb = [load_base(0)]
-        w2_raw.append(load_w2(3))
-        for t in range(1, ROW_TILES):
-            base_sb.append(load_base(t))
+        w2_raw.extend(load_w2(3, 1))
+        base_sb = [load_base(t) for t in range(ROW_TILES)]
         w3_sb = keep.tile([P, N], U32, name="w3_sb", align_bytes=64)
         nc.sync.dma_start(w3_sb[:].bitcast(I32), w3_words[0].rearrange("p c i -> p (c i)").bitcast(I32))
         for q in range(QUADS):
@@ -150,20 +149,27 @@ def tile_list_pump_dock_check_kernel(tc, tab_words, tab_scales, offs, w1_words, 
         nc.scalar.activation(warm[:], pages[0][:, 0:1], ACT.Tanh)
 
         w2_q = []
+        w2_grouped = []
 
-        def quantize_w2(t, slot, codes_slot):
+        def round_w2(t, slot):
             grouped = keep.tile([P, PASSES, P, 4], BF16, name="w2_grouped%d" % t, tag=slot, align_bytes=64)
             for a in range(PASSES):
-                nc.scalar.copy(grouped[:, a, :, :], w2_raw[t][a][:].rearrange("p j c -> p c j"))
+                nc.scalar.copy(grouped[:, a, :, :].rearrange("p (c i) j -> p c j i", i=4),
+                               w2_raw[t][a].rearrange("p j (c i) -> p c j i", i=4))
+            w2_grouped.append(grouped)
+
+        def quantize_w2(t, codes_slot):
             codes = keep.tile([P, PASSES * P], U32, name="w2_codes%d" % t, tag=codes_slot, align_bytes=64)
             scales = keep.tile([P, PASSES * P], U8, name="w2_scales%d" % t, align_bytes=64)
-            flat = grouped[:].rearrange("p a c j -> p (a c j)")
+            flat = w2_grouped[t][:].rearrange("p a c j -> p (a c j)")
             for lo, hi in ((0, 2 * P), (2 * P, 3 * P)):
                 nc.vector.quantize_mx(out=codes[:, lo:hi].bitcast(FP8X4), scales=scales[:, lo:hi], in_=flat[:, 4 * lo : 4 * hi])
             w2_q.append((codes, scales))
 
-        quantize_w2(0, "grouped0", "codes0")
-        outs = [keep.tile([P, T2], F32, name="out_page%d" % i, tag="out%d" % i, align_bytes=64) for i in range(2)]
+        for t, slot in enumerate(("slot_f", "slot_d")):
+            round_w2(t, slot)
+            quantize_w2(t, "codes%d" % t)
+        outs = [keep.tile([P, T2], F32, name="out_page%d" % i) for i in range(2)]
         for tile in outs:
             nc.vector.memset(tile[:], 0.0)
         for h in range(HALVES):
@@ -189,7 +195,7 @@ def tile_list_pump_dock_check_kernel(tc, tab_words, tab_scales, offs, w1_words, 
                 nc.tensor.matmul_mx(out=b_bank[:], lhsT=codes[:, cols(a, P)].bitcast(FP8X4), lhsT_scale=scales[:, cols(a, P)],
                                     rhs=v[a][:, cols(h, HALF)].bitcast(FP8X4), rhs_scale=v_sc[0][4 * a : P, cols(h, HALF)],
                                     start=(a == 0), stop=(a == PASSES - 1))
-            slot = "first%d" % (t % 3) if h == 0 else "second%d" % (t % 2)
+            slot = SQUARE_SLOTS[t][h]
             sq = keep.tile([P, HALF], F32, name="sq%d_%d" % (t, h), tag=slot, align_bytes=64)
             nc.scalar.activation(sq[:], b_bank[:], ACT.Square)
             return sq
@@ -244,14 +250,15 @@ def tile_list_pump_dock_check_kernel(tc, tab_words, tab_scales, offs, w1_words, 
             return banks
 
         sq = square_of_b(0, 0)
-        gw = weigh(0, 0, 1, "first2")
+        gw = weigh(0, 0, 1, WEIGHT_SLOTS[0])
         tanh_of_sum(0, 0, product_a(0, 0), sq)
         sq = square_of_b(0, 1)
         tanh_of_sum(0, 1, product_a(0, 1), sq)
         place(0, 0, gw[:])
-        quantize_w2(1, "grouped1", "codes1")
-        place(0, 1, weigh(0, 1, 2, "grouped1")[:])
-        gw = weigh(1, 0, 2, "first0")
+        place(0, 1, weigh(0, 1, 2, "slot_g")[:])
+        round_w2(2, "slot_b")
+        gw = weigh(1, 0, 2, WEIGHT_SLOTS[1])
+        round_w2(3, "slot_h")
         for t in range(1, ROW_TILES):
             a_banks = [product_a(t, h) for h in range(HALVES)]
             squares = [square_of_b(t, h) for h in range(HALVES)]
@@ -259,11 +266,11 @@ def tile_list_pump_dock_check_kernel(tc, tab_words, tab_scales, offs, w1_words, 
             for h in range(HALVES):
                 tanh_of_sum(t, h, a_banks[h], squares[h])
             if t + 1 < ROW_TILES:
-                quantize_w2(t + 1, "grouped0", "second%d" % (t % 2))
+                quantize_w2(t + 1, SQUARE_SLOTS[t][1])
             place(t, 0, gw[:, cols(0, HALF)])
             if t + 1 < ROW_TILES:
                 place(t, 1, gw[:, cols(1, HALF)])
-                gw = weigh(t + 1, 0, 2, "first%d" % (t % 3))
+                gw = weigh(t + 1, 0, 2, WEIGHT_SLOTS[t + 1])
             for c in range(CHUNKS):
                 round_sum(t - 1, c, sum_banks[c], nc.scalar.copy)
         limits_and_warm_up()

@@ -76,7 +76,10 @@ def tile_list_pump_dock_check_kernel(tc, tab_words, tab_scales, offs, w1_words, 
             return tile
 
         tab_scale_rows = keep.tile([P, T], U8, name="tab_scale_rows", tag="words1", align_bytes=64)
-        nc.vector.memset(tab_scale_rows[:].bitcast(I32), 0)
+        nc.gpsimd.memset(tab_scale_rows[:].bitcast(I32), 0)
+        for q in range(QUADS):
+            nc.gpsimd.dma_start(tab_scale_rows[32 * q : 32 * q + 4 * PASSES, :].bitcast(I32),
+                                tab_scales[:, 4 * q : 4 * q + 4, :].bitcast(I32))
         v_sc = [keep.tile([P, S], U8, name="v_sc%d" % a, align_bytes=64) for a in range(PASSES)]
         for a in range(1, PASSES):
             nc.vector.memset(v_sc[a][:].bitcast(I32), 0)
@@ -94,9 +97,6 @@ def tile_list_pump_dock_check_kernel(tc, tab_words, tab_scales, offs, w1_words, 
 
         offs_sb = load_list(offs, "offs_sb")
         table = [load_table(0)]
-        for q in range(QUADS):
-            nc.sync.dma_start(tab_scale_rows[32 * q : 32 * q + 4 * PASSES, :].bitcast(I32),
-                              tab_scales[:, 4 * q : 4 * q + 4, :].bitcast(I32))
         table.append(load_table(1))
         nc.sync.dma_start(vec_rows[0:4, :], curve.rearrange("(t p) -> t p", p=P))
         nc.sync.dma_start(vec_rows[4:8, :], gain.rearrange("(t p) -> t p", p=P))
@@ -126,16 +126,6 @@ def tile_list_pump_dock_check_kernel(tc, tab_words, tab_scales, offs, w1_words, 
         nc.sync.dma_start(w1_rest[:].bitcast(I32), w1_view[:, :, 2 * P : 2 * H].bitcast(I32))
         nc.sync.dma_start(wgs_sb[:, cols(1, HALF)], wgs[:, cols(1, HALF)])
         w2_raw.extend(load_w2(3, 1))
-        base_sb = [load_base(t) for t in range(ROW_TILES)]
-        w3_sb = keep.tile([P, N], U32, name="w3_sb", align_bytes=64)
-        nc.sync.dma_start(w3_sb[:].bitcast(I32), w3_words[0].rearrange("p c i -> p (c i)").bitcast(I32))
-        for q in range(QUADS):
-            nc.sync.dma_start(w3_sc[32 * q : 32 * q + 4, :].bitcast(I32), w3_scales[0, 4 * q : 4 * q + 4, :].bitcast(I32))
-        nc.sync.dma_start(limit_rows[0:OUT_TILES, :], limit.rearrange("(t p) -> t p", p=P))
-        offs3_sb = load_list(offs3, "offs3_sb")
-        offs4_sb = load_list(offs4, "offs4_sb")
-        wgo_sb = keep.tile([P, S], F32, name="wgo_sb")
-        nc.sync.dma_start(wgo_sb[:], wgo)
 
         vec_bank = bank(7, "vec_bank")
         nc.tensor.transpose(vec_bank[:, 0:P], vec_rows[:], ident[:])
@@ -158,17 +148,28 @@ def tile_list_pump_dock_check_kernel(tc, tab_words, tab_scales, offs, w1_words, 
                                w2_raw[t][a].rearrange("p j (c i) -> p c j i", i=4))
             w2_grouped.append(grouped)
 
-        def quantize_w2(t, codes_slot):
-            codes = keep.tile([P, PASSES * P], U32, name="w2_codes%d" % t, tag=codes_slot, align_bytes=64)
+        def quantize_w2(t, codes):
             scales = keep.tile([P, PASSES * P], U8, name="w2_scales%d" % t, align_bytes=64)
             flat = w2_grouped[t][:].rearrange("p a c j -> p (a c j)")
             for lo, hi in ((0, 2 * P), (2 * P, 3 * P)):
                 nc.vector.quantize_mx(out=codes[:, lo:hi].bitcast(FP8X4), scales=scales[:, lo:hi], in_=flat[:, 4 * lo : 4 * hi])
             w2_q.append((codes, scales))
 
+        first_codes = keep.tile([P, 2 * PASSES * P], U32, name="first_codes", tag="big1", align_bytes=64)
         for t, slot in enumerate(("slot_f", "slot_d")):
             round_w2(t, slot)
-            quantize_w2(t, "codes%d" % t)
+            quantize_w2(t, first_codes[:, cols(t, PASSES * P)])
+        base_sb = [load_base(t) for t in range(ROW_TILES)]
+        w3_sb = keep.tile([P, N], U32, name="w3_sb", align_bytes=64)
+        nc.sync.dma_start(w3_sb[:].bitcast(I32), w3_words[0].rearrange("p c i -> p (c i)").bitcast(I32))
+        for q in range(QUADS):
+            nc.sync.dma_start(w3_sc[32 * q : 32 * q + 4, :].bitcast(I32), w3_scales[0, 4 * q : 4 * q + 4, :].bitcast(I32))
+        nc.sync.dma_start(limit_rows[0:OUT_TILES, :], limit.rearrange("(t p) -> t p", p=P))
+        offs3_sb = load_list(offs3, "offs3_sb")
+        offs4_sb = load_list(offs4, "offs4_sb")
+        wgo_sb = keep.tile([P, S], F32, name="wgo_sb")
+        nc.sync.dma_start(wgo_sb[:], wgo)
+
         outs = [keep.tile([P, T2], F32, name="out_page%d" % i) for i in range(2)]
         for tile in outs:
             nc.vector.memset(tile[:], 0.0)
@@ -224,7 +225,7 @@ def tile_list_pump_dock_check_kernel(tc, tab_words, tab_scales, offs, w1_words, 
             tile = keep.tile([P, OUT_TILES], F32, name="neg_limit")
             nc.scalar.mul(tile[:], limit_bank[:, 0:OUT_TILES], -1.0)
             neg_limit.append(tile)
-            codes, scales = w2_q[0]
+            codes, scales = w2_q[ROW_TILES - 1]
             spare = bank(7, "spare_bank")
             for i in range(WARM_PASSES):
                 nc.tensor.matmul_mx(out=spare[:], lhsT=codes[:, cols(0, P)].bitcast(FP8X4), lhsT_scale=scales[:, cols(0, P)],
@@ -266,7 +267,7 @@ def tile_list_pump_dock_check_kernel(tc, tab_words, tab_scales, offs, w1_words, 
             for h in range(HALVES):
                 tanh_of_sum(t, h, a_banks[h], squares[h])
             if t + 1 < ROW_TILES:
-                quantize_w2(t + 1, SQUARE_SLOTS[t][1])
+                quantize_w2(t + 1, keep.tile([P, PASSES * P], U32, name="w2_codes%d" % (t + 1), tag=SQUARE_SLOTS[t][1], align_bytes=64))
             place(t, 0, gw[:, cols(0, HALF)])
             if t + 1 < ROW_TILES:
                 place(t, 1, gw[:, cols(1, HALF)])

@@ -29,7 +29,6 @@ CHUNKS = T2 // CHUNK
 SUBS = CHUNK // P
 QUADS = 4
 SHIFT_ROWS = 112
-WARM_PASSES = 6
 SQUARE_SLOTS = (("slot_a", "slot_b"), ("slot_c", "slot_d"), ("slot_e", "slot_f"), ("slot_a", "slot_b"))
 WEIGHT_SLOTS = ("slot_e", "slot_a", "slot_c", "slot_e")
 
@@ -219,18 +218,12 @@ def tile_list_pump_dock_check_kernel(tc, tab_words, tab_scales, offs, w1_words, 
         def place(t, h, gw):
             nc.vector.tensor_tensor(pages[t % 2][:].indirect(half_of(offs2_sb, h)), th[h][:], gw, ALU.mult)
 
-        def limits_and_warm_up():
+        def negate_limits():
             limit_bank = bank(7, "limit_bank")
             nc.tensor.transpose(limit_bank[:, 0:P], limit_rows[:], ident[:])
             tile = keep.tile([P, OUT_TILES], F32, name="neg_limit")
             nc.scalar.mul(tile[:], limit_bank[:, 0:OUT_TILES], -1.0)
             neg_limit.append(tile)
-            codes, scales = w2_q[ROW_TILES - 1]
-            spare = bank(7, "spare_bank")
-            for i in range(WARM_PASSES):
-                nc.tensor.matmul_mx(out=spare[:], lhsT=codes[:, cols(0, P)].bitcast(FP8X4), lhsT_scale=scales[:, cols(0, P)],
-                                    rhs=v[0][:, cols(0, HALF)].bitcast(FP8X4), rhs_scale=v_sc[0][:, cols(0, HALF)],
-                                    start=True, stop=True)
 
         def add_transposed(banks, src, first):
             for c in range(CHUNKS):
@@ -274,7 +267,7 @@ def tile_list_pump_dock_check_kernel(tc, tab_words, tab_scales, offs, w1_words, 
                 gw = weigh(t + 1, 0, 2, WEIGHT_SLOTS[t + 1])
             for c in range(CHUNKS):
                 round_sum(t - 1, c, sum_banks[c], nc.scalar.copy)
-        limits_and_warm_up()
+        negate_limits()
         place(ROW_TILES - 1, 1, gw[:, cols(1, HALF)])
         sum_banks = add_base(ROW_TILES - 1)
 
@@ -291,30 +284,33 @@ def tile_list_pump_dock_check_kernel(tc, tab_words, tab_scales, offs, w1_words, 
             engine_copy(y[n][:, lo : lo + width], y_bank[:, 0:width])
 
         for c in range(CHUNKS):
-            round_sum(ROW_TILES - 1, c, sum_banks[c], nc.vector.tensor_copy if c % 2 == 0 else nc.scalar.copy)
+            round_sum(ROW_TILES - 1, c, sum_banks[c], nc.vector.tensor_copy if c % 2 == 1 else nc.scalar.copy)
         for c in range(CHUNKS):
             codes = keep.tile([P, CHUNK], U32, name="z_codes%d" % c, align_bytes=64)
             scales = keep.tile([P, CHUNK], U8, name="z_scales%d" % c, align_bytes=64)
-            for h in range(2):
-                back = bank((2 * c + h) % 4, "back_bank")
-                for i in range(4):
-                    nc.tensor.transpose(back[:, cols(i, P)], z_t[c // 2][:, 8 * (c % 2) + 4 * h + i, :], ident[:])
-                z = ring.tile([P, 2 * P * 4], BF16, name="z", tag="z%d" % h, align_bytes=64)
-                z_words = z[:].bitcast(F32).rearrange("p (s q u) -> p s q u", s=2, u=2)
-                src = back[:].rearrange("p (s u q) -> p s q u", s=2, u=2)
-                if h == 0:
+            pieces = ((0, 2), (2, 2)) if c + 1 < CHUNKS else ((0, 2), (2, 1), (3, 1))
+            for i, (first, count) in enumerate(pieces):
+                back = bank((2 * c + i) % 8, "back_bank")
+                for j in range(2 * count):
+                    nc.tensor.transpose(back[:, cols(j, P)], z_t[c // 2][:, 8 * (c % 2) + 2 * first + j, :], ident[:])
+                z = ring.tile([P, count * P * 4], BF16, name="z", tag="z%d" % (i % 2), align_bytes=64)
+                z_words = z[:].bitcast(F32).rearrange("p (s q u) -> p s q u", s=count, u=2)
+                src = back[:, 0 : 2 * count * P].rearrange("p (s u q) -> p s q u", s=count, u=2)
+                if i + 1 == len(pieces) and c % 2 == 1:
                     nc.vector.tensor_copy(z_words, src)
                 else:
                     nc.scalar.copy(z_words, src)
-                nc.vector.quantize_mx(out=codes[:, cols(h, 2 * P)].bitcast(FP8X4), scales=scales[:, cols(h, 2 * P)], in_=z[:])
+                span = slice(first * P, (first + count) * P)
+                nc.vector.quantize_mx(out=codes[:, span].bitcast(FP8X4), scales=scales[:, span], in_=z[:])
             z_q.append((codes, scales))
-            if c + 1 < CHUNKS:
-                product(0, c * CHUNK, CHUNK, 4 + c, nc.scalar.copy)
-        product(0, T2 - CHUNK, 2 * P, 7, nc.scalar.copy)
-        product(0, T2 - 2 * P, 2 * P, 4, nc.vector.tensor_copy)
+        for c in range(CHUNKS - 1):
+            product(0, c * CHUNK, CHUNK, 1 + c, nc.scalar.copy)
+        product(0, T2 - CHUNK, 2 * P, 4, nc.vector.tensor_copy)
+        product(0, T2 - 2 * P, P, 5, nc.vector.tensor_copy)
+        product(0, T2 - P, P, 6, nc.vector.tensor_copy)
         for n in range(1, OUT_TILES):
             for c in range(CHUNKS):
-                product(n, c * CHUNK, CHUNK, c, nc.scalar.copy)
+                product(n, c * CHUNK, CHUNK, (4 * n + 3 + c) % 8, nc.scalar.copy)
 
         picked = []
         for n in range(OUT_TILES):

@@ -30,6 +30,8 @@ SUBS = CHUNK // P
 QUADS = 4
 SHIFT_ROWS = 112
 SQUARE_SLOTS = (("slot_a", "slot_b"), ("slot_c", "slot_d"), ("slot_e", "slot_f"), ("slot_a", "slot_b"))
+BASE_KIB = (32, 40, 48, 92)
+LATE_KIB = 52
 WEIGHT_SLOTS = ("slot_e", "slot_a", "slot_c", "slot_e")
 
 
@@ -40,7 +42,11 @@ def tile_list_pump_dock_check_kernel(tc, tab_words, tab_scales, offs, w1_words, 
         lists = ctx.enter_context(tc.tile_pool(name="lists", bufs=1))
         keep = ctx.enter_context(tc.tile_pool(name="keep", bufs=1))
         ring = ctx.enter_context(tc.tile_pool(name="ring", bufs=2))
+        arena = ctx.enter_context(tc.tile_pool(name="arena", bufs=1))
         psum = ctx.enter_context(tc.psum_pool(name="psum", bufs=1))
+
+        def placed(shape, dtype, name, kib, extra=0):
+            return arena.tile(shape, dtype, name=name, offset=kib * 1024 + extra, align_bytes=64)
 
         def bank(i, name):
             return psum.tile([P, 512], F32, name=name, tag="bank%d" % i)
@@ -57,73 +63,76 @@ def tile_list_pump_dock_check_kernel(tc, tab_words, tab_scales, offs, w1_words, 
             return slice(i * width, (i + 1) * width)
 
         def load_table(a):
-            tile = keep.tile([P, T], U32, name="table%d" % a, tag="big%d" % a, align_bytes=64)
+            tile = placed([P, T], U32, "table%d" % a, 16 * a)
             nc.sync.dma_start(tile[:].bitcast(I32), tab_words[a].rearrange("p t i -> p (t i)").bitcast(I32))
             return tile
 
         def load_w2(first, count):
             tiles = []
             for a in range(PASSES):
-                tile = keep.tile([P, 4, count * P], F32, name="w2_raw%d_%d" % (first, a), align_bytes=64)
+                if first == 0:
+                    tile = keep.tile([P, 4, count * P], F32, name="w2_raw0_%d" % a, align_bytes=64)
+                else:
+                    tile = placed([P, 4, count * P], F32, "w2_raw%d_%d" % (first, a), 54 + 6 * first + 2 * a)
                 nc.sync.dma_start(tile[:], w2[cols(a, 512), first * P : (first + count) * P].rearrange("(p j) c -> p j c", j=4))
                 tiles.append(tile)
             return [[tile[:, :, cols(i, P)] for tile in tiles] for i in range(count)]
 
         def load_base(t):
-            tile = keep.tile([P, T2], F32, name="base%d" % t, tag="big%d" % t, align_bytes=64)
+            tile = placed([P, T2], F32, "base%d" % t, BASE_KIB[t])
             nc.sync.dma_start(tile[:], base[cols(t, P), :])
             return tile
 
-        tab_scale_rows = keep.tile([P, T], U8, name="tab_scale_rows", tag="words1", align_bytes=64)
-        nc.gpsimd.memset(tab_scale_rows[:].bitcast(I32), 0)
+        late_area = placed([P, LATE_KIB * 1024], U8, "late_area", 48)
+        tab_scale_rows = late_area[:, 0:T]
+        nc.gpsimd.memset(tab_scale_rows.bitcast(I32), 0)
+        vec_rows = keep.tile([P, P], F32, name="vec_rows")
+        nc.vector.memset(vec_rows[:], 0.0)
+        w1_sc = keep.tile([P, PASSES, H], U8, name="w1_sc", align_bytes=64)
+        nc.vector.memset(w1_sc[:].rearrange("p a c -> p (a c)").bitcast(I32), 0)
         for q in range(QUADS):
-            nc.gpsimd.dma_start(tab_scale_rows[32 * q : 32 * q + 4 * PASSES, :].bitcast(I32),
+            nc.gpsimd.dma_start(late_area[32 * q : 32 * q + 4 * PASSES, 0:T].bitcast(I32),
                                 tab_scales[:, 4 * q : 4 * q + 4, :].bitcast(I32))
-        v_sc = [keep.tile([P, S], U8, name="v_sc%d" % a, align_bytes=64) for a in range(PASSES)]
-        for a in range(1, PASSES):
-            nc.vector.memset(v_sc[a][:].bitcast(I32), 0)
-        w3_sc = keep.tile([P, N], U8, name="w3_sc", align_bytes=64)
-        nc.vector.memset(w3_sc[:].bitcast(I32), 0)
+        moved_sc = [keep.tile([P, S], U8, name="v_sc%d" % a, align_bytes=64) for a in range(1, PASSES)]
+        for tile in moved_sc:
+            nc.vector.memset(tile[:].bitcast(I32), 0)
 
         ident = keep.tile([P, P], F32, name="ident")
         make_identity(nc, ident[:])
-        vec_rows = keep.tile([P, P], F32, name="vec_rows")
-        nc.vector.memset(vec_rows[:], 0.0)
-        limit_rows = keep.tile([P, P], F32, name="limit_rows")
-        nc.vector.memset(limit_rows[:], 0.0)
-        w1_sc = keep.tile([P, PASSES, H], U8, name="w1_sc", align_bytes=64)
-        nc.vector.memset(w1_sc[:].rearrange("p a c -> p (a c)").bitcast(I32), 0)
 
         offs_sb = load_list(offs, "offs_sb")
         table = [load_table(0)]
-        table.append(load_table(1))
         nc.sync.dma_start(vec_rows[0:4, :], curve.rearrange("(t p) -> t p", p=P))
         nc.sync.dma_start(vec_rows[4:8, :], gain.rearrange("(t p) -> t p", p=P))
-        w2_raw = load_w2(0, 2)
-        w1_view = w1_words.rearrange("a p c -> p a c")
-        w1_first = keep.tile([P, PASSES, 2 * P], U8, name="w1_first", align_bytes=64)
-        nc.sync.dma_start(w1_first[:].bitcast(I32), w1_view[:, :, 0 : 2 * P].bitcast(I32))
         for q in range(QUADS):
             nc.sync.dma_start(w1_sc[32 * q : 32 * q + 4, :, :].bitcast(I32),
                               w1_scales[:, 4 * q : 4 * q + 4, :].rearrange("a r c -> r a c").bitcast(I32))
+        table.append(load_table(1))
+        w2_raw = load_w2(0, 1)
+        w1_view = w1_words.rearrange("a p c -> p a c")
+        w1_first = keep.tile([P, PASSES, 2 * P], U8, name="w1_first", align_bytes=64)
+        nc.sync.dma_start(w1_first[:].bitcast(I32), w1_view[:, :, 0 : 2 * P].bitcast(I32))
+        offs2_sb = load_list(offs2, "offs2_sb")
+        offs3_sb = load_list(offs3, "offs3_sb")
+        offs4_sb = load_list(offs4, "offs4_sb")
         table.append(load_table(2))
 
-        v = [keep.tile([P, S], U32, name="v0", tag="words0", align_bytes=64)]
-        nc.vector.tensor_copy(v[0][:], table[0][:].indirect(offs_sb[:]))
-        nc.vector.tensor_copy(v_sc[0][:], tab_scale_rows[:].indirect(offs_sb[:]))
+        v = [keep.tile([P, S], U32, name="v%d" % a, tag="words%d" % a, align_bytes=64) for a in range(2)]
+        for a in range(2):
+            nc.vector.tensor_copy(v[a][:], table[a][:].indirect(offs_sb[:]))
+        v_sc = [placed([P, S], U8, "v_sc0", 16)] + moved_sc
+        nc.vector.tensor_copy(v_sc[0][:], tab_scale_rows.indirect(offs_sb[:]))
         for a in range(1, PASSES):
             nc.sync.dma_start(v_sc[a][0:SHIFT_ROWS, :].bitcast(I32),
                               v_sc[0][4 * a : 4 * a + SHIFT_ROWS, :].bitcast(I32))
-        v.extend(keep.tile([P, S], U32, name="v%d" % a, tag="words%d" % a, align_bytes=64) for a in range(1, PASSES))
-        nc.vector.tensor_copy(v[1][:], table[1][:].indirect(offs_sb[:]))
 
-        wgs_sb = keep.tile([P, S], F32, name="wgs_sb")
+        wgs_sb = placed([P, S], F32, "wgs_sb", 56)
         nc.sync.dma_start(wgs_sb[:, cols(0, HALF)], wgs[:, cols(0, HALF)])
-        offs2_sb = load_list(offs2, "offs2_sb")
-        w2_raw.extend(load_w2(2, 1))
-        w1_rest = keep.tile([P, PASSES, 2 * (H - P)], U8, name="w1_rest", align_bytes=64)
+        w2_raw.extend(load_w2(1, 1))
+        w1_rest = placed([P, PASSES, 2 * (H - P)], U8, "w1_rest", 78)
         nc.sync.dma_start(w1_rest[:].bitcast(I32), w1_view[:, :, 2 * P : 2 * H].bitcast(I32))
         nc.sync.dma_start(wgs_sb[:, cols(1, HALF)], wgs[:, cols(1, HALF)])
+        w2_raw.extend(load_w2(2, 1))
         w2_raw.extend(load_w2(3, 1))
 
         vec_bank = bank(7, "vec_bank")
@@ -154,24 +163,25 @@ def tile_list_pump_dock_check_kernel(tc, tab_words, tab_scales, offs, w1_words, 
                 nc.vector.quantize_mx(out=codes[:, lo:hi].bitcast(FP8X4), scales=scales[:, lo:hi], in_=flat[:, 4 * lo : 4 * hi])
             w2_q.append((codes, scales))
 
-        first_codes = keep.tile([P, 2 * PASSES * P], U32, name="first_codes", tag="big1", align_bytes=64)
-        for t, slot in enumerate(("slot_f", "slot_d")):
-            round_w2(t, slot)
-            quantize_w2(t, first_codes[:, cols(t, PASSES * P)])
+        round_w2(0, "words2")
+        quantize_w2(0, placed([P, PASSES * P], U32, "first_codes", 86))
         base_sb = [load_base(t) for t in range(ROW_TILES)]
-        w3_sb = keep.tile([P, N], U32, name="w3_sb", align_bytes=64)
+        w3_sb = placed([P, N], U32, "w3_sb", 88)
+        w3_sc = placed([P, N], U8, "w3_sc", 90)
+        nc.vector.memset(w3_sc[:].bitcast(I32), 0)
+        limit_rows = placed([P, P], F32, "limit_rows", 91)
+        nc.vector.memset(limit_rows[:], 0.0)
         nc.sync.dma_start(w3_sb[:].bitcast(I32), w3_words[0].rearrange("p c i -> p (c i)").bitcast(I32))
         for q in range(QUADS):
             nc.sync.dma_start(w3_sc[32 * q : 32 * q + 4, :].bitcast(I32), w3_scales[0, 4 * q : 4 * q + 4, :].bitcast(I32))
         nc.sync.dma_start(limit_rows[0:OUT_TILES, :], limit.rearrange("(t p) -> t p", p=P))
-        offs3_sb = load_list(offs3, "offs3_sb")
-        offs4_sb = load_list(offs4, "offs4_sb")
-        wgo_sb = keep.tile([P, S], F32, name="wgo_sb")
+        wgo_sb = placed([P, S], F32, "wgo_sb", 82)
         nc.sync.dma_start(wgo_sb[:], wgo)
 
         outs = [keep.tile([P, T2], F32, name="out_page%d" % i) for i in range(2)]
         for tile in outs:
             nc.vector.memset(tile[:], 0.0)
+        v.append(keep.tile([P, S], U32, name="v2", tag="words2", align_bytes=64))
         for h in range(HALVES):
             nc.vector.tensor_copy(v[2][:, cols(h, HALF)], table[2][:].indirect(half_of(offs_sb, h)))
 
@@ -179,26 +189,34 @@ def tile_list_pump_dock_check_kernel(tc, tab_words, tab_scales, offs, w1_words, 
         th = {}
         neg_limit = []
 
+        def pass_a(t, h, a, a_bank):
+            w1_cols = w1_first[:, a, :] if t == 0 else w1_rest[:, a, cols(t - 1, 2 * P)]
+            nc.tensor.matmul_mx(out=a_bank[:], lhsT=w1_cols.bitcast(FP4X4), lhsT_scale=w1_sc[:, a, cols(t, P)],
+                                rhs=v[a][:, cols(h, HALF)].bitcast(FP8X4), rhs_scale=v_sc[a][:, cols(h, HALF)],
+                                start=(a == 0), stop=(a == PASSES - 1))
+
+        def pass_b(t, h, a, b_bank):
+            codes, scales = w2_q[t]
+            nc.tensor.matmul_mx(out=b_bank[:], lhsT=codes[:, cols(a, P)].bitcast(FP8X4), lhsT_scale=scales[:, cols(a, P)],
+                                rhs=v[a][:, cols(h, HALF)].bitcast(FP8X4), rhs_scale=v_sc[0][4 * a : P, cols(h, HALF)],
+                                start=(a == 0), stop=(a == PASSES - 1))
+
         def product_a(t, h):
             a_bank = bank(HALVES * ((t + 1) % 2) + h, "a_bank")
             for a in range(PASSES):
-                w1_cols = w1_first[:, a, :] if t == 0 else w1_rest[:, a, cols(t - 1, 2 * P)]
-                nc.tensor.matmul_mx(out=a_bank[:], lhsT=w1_cols.bitcast(FP4X4), lhsT_scale=w1_sc[:, a, cols(t, P)],
-                                    rhs=v[a][:, cols(h, HALF)].bitcast(FP8X4), rhs_scale=v_sc[a][:, cols(h, HALF)],
-                                    start=(a == 0), stop=(a == PASSES - 1))
+                pass_a(t, h, a, a_bank)
             return a_bank
 
-        def square_of_b(t, h):
-            codes, scales = w2_q[t]
-            b_bank = bank(HALVES * (t % 2) + h, "b_bank")
-            for a in range(PASSES):
-                nc.tensor.matmul_mx(out=b_bank[:], lhsT=codes[:, cols(a, P)].bitcast(FP8X4), lhsT_scale=scales[:, cols(a, P)],
-                                    rhs=v[a][:, cols(h, HALF)].bitcast(FP8X4), rhs_scale=v_sc[0][4 * a : P, cols(h, HALF)],
-                                    start=(a == 0), stop=(a == PASSES - 1))
-            slot = SQUARE_SLOTS[t][h]
-            sq = keep.tile([P, HALF], F32, name="sq%d_%d" % (t, h), tag=slot, align_bytes=64)
+        def square(t, h, b_bank):
+            sq = keep.tile([P, HALF], F32, name="sq%d_%d" % (t, h), tag=SQUARE_SLOTS[t][h], align_bytes=64)
             nc.scalar.activation(sq[:], b_bank[:], ACT.Square)
             return sq
+
+        def square_of_b(t, h):
+            b_bank = bank(HALVES * (t % 2) + h, "b_bank")
+            for a in range(PASSES):
+                pass_b(t, h, a, b_bank)
+            return square(t, h, b_bank)
 
         def runs(ap):
             return ap.rearrange("p (g w) -> p g w", w=32)
@@ -211,7 +229,10 @@ def tile_list_pump_dock_check_kernel(tc, tab_words, tab_scales, offs, w1_words, 
             th[h] = tile
 
         def weigh(t, lo, hi, slot):
-            gw = keep.tile([P, (hi - lo) * HALF], F32, name="gw%d_%d" % (t, lo), tag=slot, align_bytes=64)
+            if slot is None:
+                gw = placed([P, HALF], F32, "gw_second", 64)
+            else:
+                gw = keep.tile([P, (hi - lo) * HALF], F32, name="gw%d_%d" % (t, lo), tag=slot, align_bytes=64)
             nc.scalar.mul(gw[:], wgs_sb[:, lo * HALF : hi * HALF], vecs[:, 4 + t : 5 + t])
             return gw
 
@@ -219,13 +240,13 @@ def tile_list_pump_dock_check_kernel(tc, tab_words, tab_scales, offs, w1_words, 
             nc.vector.tensor_tensor(pages[t % 2][:].indirect(half_of(offs2_sb, h)), th[h][:], gw, ALU.mult)
 
         def negate_limits():
-            limit_bank = bank(7, "limit_bank")
+            limit_bank = bank(0, "limit_bank")
             nc.tensor.transpose(limit_bank[:, 0:P], limit_rows[:], ident[:])
             tile = keep.tile([P, OUT_TILES], F32, name="neg_limit")
             nc.scalar.mul(tile[:], limit_bank[:, 0:OUT_TILES], -1.0)
             neg_limit.append(tile)
 
-        def add_transposed(banks, src, first):
+        def add_transposed(banks, src, first, ident):
             for c in range(CHUNKS):
                 for s in range(SUBS):
                     nc.tensor.matmul(banks[c][:, cols(s, P)], src[:, cols(c * SUBS + s, P)], ident[:], is_transpose=True,
@@ -239,20 +260,32 @@ def tile_list_pump_dock_check_kernel(tc, tab_words, tab_scales, offs, w1_words, 
 
         def add_base(t):
             banks = [bank(4 + c, "sum_bank") for c in range(CHUNKS)]
-            add_transposed(banks, base_sb[t], True)
-            add_transposed(banks, pages[t % 2], False)
+            add_transposed(banks, base_sb[t], True, ident)
+            late = ident
+            if t == ROW_TILES - 1:
+                late = placed([P, P], F32, "late_ident", BASE_KIB[t])
+                nc.scalar.copy(late[:], ident[:])
+            add_transposed(banks, pages[t % 2], False, late)
             return banks
 
-        sq = square_of_b(0, 0)
+        a_banks = [bank(HALVES + h, "a_bank") for h in range(HALVES)]
+        b_banks = [bank(h, "b_bank") for h in range(HALVES)]
+        for h in range(HALVES):
+            pass_a(0, h, 0, a_banks[h])
+            for a in range(PASSES - 1):
+                pass_b(0, h, a, b_banks[h])
         gw = weigh(0, 0, 1, WEIGHT_SLOTS[0])
-        tanh_of_sum(0, 0, product_a(0, 0), sq)
-        sq = square_of_b(0, 1)
-        tanh_of_sum(0, 1, product_a(0, 1), sq)
+        for h in range(HALVES):
+            pass_a(0, h, 1, a_banks[h])
+            pass_b(0, h, PASSES - 1, b_banks[h])
+            pass_a(0, h, PASSES - 1, a_banks[h])
+            tanh_of_sum(0, h, a_banks[h], square(0, h, b_banks[h]))
         place(0, 0, gw[:])
-        place(0, 1, weigh(0, 1, 2, "slot_g")[:])
+        round_w2(1, "slot_a")
+        quantize_w2(1, keep.tile([P, PASSES * P], U32, name="w2_codes1", align_bytes=64))
+        place(0, 1, weigh(0, 1, 2, None)[:])
         round_w2(2, "slot_b")
         gw = weigh(1, 0, 2, WEIGHT_SLOTS[1])
-        round_w2(3, "slot_h")
         for t in range(1, ROW_TILES):
             a_banks = [product_a(t, h) for h in range(HALVES)]
             squares = [square_of_b(t, h) for h in range(HALVES)]
@@ -261,6 +294,8 @@ def tile_list_pump_dock_check_kernel(tc, tab_words, tab_scales, offs, w1_words, 
                 tanh_of_sum(t, h, a_banks[h], squares[h])
             if t + 1 < ROW_TILES:
                 quantize_w2(t + 1, keep.tile([P, PASSES * P], U32, name="w2_codes%d" % (t + 1), tag=SQUARE_SLOTS[t][1], align_bytes=64))
+            if t == 1:
+                round_w2(3, "slot_b")
             place(t, 0, gw[:, cols(0, HALF)])
             if t + 1 < ROW_TILES:
                 place(t, 1, gw[:, cols(1, HALF)])
@@ -271,7 +306,7 @@ def tile_list_pump_dock_check_kernel(tc, tab_words, tab_scales, offs, w1_words, 
         place(ROW_TILES - 1, 1, gw[:, cols(1, HALF)])
         sum_banks = add_base(ROW_TILES - 1)
 
-        y = [keep.tile([P, T2], F32, name="y%d" % n, tag="big%d" % n, align_bytes=64) for n in range(OUT_TILES)]
+        y = [placed([P, T2], F32, "y%d" % n, 8 * n) for n in range(OUT_TILES)]
         z_q = []
 
         def product(n, lo, width, bank_no, engine_copy):

@@ -32,6 +32,7 @@ SHIFT_ROWS = 112
 SQUARE_SLOTS = (("slot_a", "slot_b"), ("slot_c", "slot_d"), ("slot_e", "slot_f"), ("slot_a", "slot_b"))
 BASE_KIB = (32, 40, 48, 92)
 LATE_KIB = 52
+WARM_PASSES = 6
 WEIGHT_SLOTS = ("slot_e", "slot_a", "slot_c", "slot_e")
 
 
@@ -101,20 +102,24 @@ def tile_list_pump_dock_check_kernel(tc, tab_words, tab_scales, offs, w1_words, 
         make_identity(nc, ident[:])
 
         offs_sb = load_list(offs, "offs_sb")
-        table = [load_table(0)]
-        nc.sync.dma_start(vec_rows[0:4, :], curve.rearrange("(t p) -> t p", p=P))
-        nc.sync.dma_start(vec_rows[4:8, :], gain.rearrange("(t p) -> t p", p=P))
-        for q in range(QUADS):
+        def load_w1_scales(q):
             nc.sync.dma_start(w1_sc[32 * q : 32 * q + 4, :, :].bitcast(I32),
                               w1_scales[:, 4 * q : 4 * q + 4, :].rearrange("a r c -> r a c").bitcast(I32))
+
+        table = [load_table(0)]
+        offs2_sb = load_list(offs2, "offs2_sb")
+        offs3_sb = load_list(offs3, "offs3_sb")
+        offs4_sb = load_list(offs4, "offs4_sb")
+        nc.sync.dma_start(vec_rows[0:4, :], curve.rearrange("(t p) -> t p", p=P))
+        nc.sync.dma_start(vec_rows[4:8, :], gain.rearrange("(t p) -> t p", p=P))
+        load_w1_scales(0)
         table.append(load_table(1))
+        for q in range(1, QUADS):
+            load_w1_scales(q)
         w2_raw = load_w2(0, 1)
         w1_view = w1_words.rearrange("a p c -> p a c")
         w1_first = keep.tile([P, PASSES, 2 * P], U8, name="w1_first", align_bytes=64)
         nc.sync.dma_start(w1_first[:].bitcast(I32), w1_view[:, :, 0 : 2 * P].bitcast(I32))
-        offs2_sb = load_list(offs2, "offs2_sb")
-        offs3_sb = load_list(offs3, "offs3_sb")
-        offs4_sb = load_list(offs4, "offs4_sb")
         table.append(load_table(2))
 
         v = [keep.tile([P, S], U32, name="v%d" % a, tag="words%d" % a, align_bytes=64) for a in range(2)]
@@ -259,6 +264,12 @@ def tile_list_pump_dock_check_kernel(tc, tab_words, tab_scales, offs, w1_words, 
                         sum_bank[:].rearrange("q (s p u e) -> q s u p e", s=SUBS, u=2, e=2))
 
         def add_base(t):
+            if t == ROW_TILES - 1:
+                warm_bank = bank(7, "warm_bank")
+                codes, scales = w2_q[t]
+                for i in range(WARM_PASSES):
+                    nc.tensor.matmul_mx(out=warm_bank[:], lhsT=codes[:, 0:P].bitcast(FP8X4), lhsT_scale=scales[:, 0:P],
+                                        rhs=v[0][:, 0:HALF].bitcast(FP8X4), rhs_scale=v_sc[0][:, 0:HALF], start=True, stop=True)
             banks = [bank(4 + c, "sum_bank") for c in range(CHUNKS)]
             add_transposed(banks, base_sb[t], True, ident)
             late = ident

@@ -29,11 +29,24 @@ CHUNKS = T2 // CHUNK
 SUBS = CHUNK // P
 QUADS = 4
 SHIFT_ROWS = 112
+BANKS = 8
+SUM_BANK = 4
+
 SQUARE_SLOTS = (("slot_a", "slot_b"), ("slot_c", "slot_d"), ("slot_e", "slot_f"), ("slot_a", "slot_b"))
-BASE_KIB = (32, 40, 48, 92)
-LATE_KIB = 52
-WARM_PASSES = 6
 WEIGHT_SLOTS = ("slot_e", "slot_a", "slot_c", "slot_e")
+
+TABLE_KIB = 16
+PAGE_KIB = 8
+LATE_AT, LATE_KIB = 48, 52
+GATHERED_SCALES_AT = 16
+BASE_AT = (32, 40, 48, 92)
+WGS_AT = 56
+W2_RAW_AT = 60
+SECOND_WEIGHTS_AT = 64
+W1_REST_AT = 78
+WGO_AT = 82
+FIRST_CODES_AT = 86
+W3_AT, W3_SCALES_AT, LIMIT_AT = 88, 90, 91
 
 
 def tile_list_pump_dock_check_kernel(tc, tab_words, tab_scales, offs, w1_words, w1_scales, w2, curve, gain,
@@ -46,8 +59,8 @@ def tile_list_pump_dock_check_kernel(tc, tab_words, tab_scales, offs, w1_words, 
         arena = ctx.enter_context(tc.tile_pool(name="arena", bufs=1))
         psum = ctx.enter_context(tc.psum_pool(name="psum", bufs=1))
 
-        def placed(shape, dtype, name, kib, extra=0):
-            return arena.tile(shape, dtype, name=name, offset=kib * 1024 + extra, align_bytes=64)
+        def placed(shape, dtype, name, kib):
+            return arena.tile(shape, dtype, name=name, offset=kib * 1024, align_bytes=64)
 
         def bank(i, name):
             return psum.tile([P, 512], F32, name=name, tag="bank%d" % i)
@@ -64,27 +77,27 @@ def tile_list_pump_dock_check_kernel(tc, tab_words, tab_scales, offs, w1_words, 
             return slice(i * width, (i + 1) * width)
 
         def load_table(a):
-            tile = placed([P, T], U32, "table%d" % a, 16 * a)
+            tile = placed([P, T], U32, "table%d" % a, TABLE_KIB * a)
             nc.sync.dma_start(tile[:].bitcast(I32), tab_words[a].rearrange("p t i -> p (t i)").bitcast(I32))
             return tile
 
-        def load_w2(first, count):
+        def load_w2(t):
             tiles = []
             for a in range(PASSES):
-                if first == 0:
-                    tile = keep.tile([P, 4, count * P], F32, name="w2_raw0_%d" % a, align_bytes=64)
+                if t == 0:
+                    tile = keep.tile([P, 4, P], F32, name="w2_raw0_%d" % a, align_bytes=64)
                 else:
-                    tile = placed([P, 4, count * P], F32, "w2_raw%d_%d" % (first, a), 54 + 6 * first + 2 * a)
-                nc.sync.dma_start(tile[:], w2[cols(a, 512), first * P : (first + count) * P].rearrange("(p j) c -> p j c", j=4))
+                    tile = placed([P, 4, P], F32, "w2_raw%d_%d" % (t, a), W2_RAW_AT + 2 * (PASSES * (t - 1) + a))
+                nc.sync.dma_start(tile[:], w2[cols(a, 512), cols(t, P)].rearrange("(p j) c -> p j c", j=4))
                 tiles.append(tile)
-            return [[tile[:, :, cols(i, P)] for tile in tiles] for i in range(count)]
+            return tiles
 
         def load_base(t):
-            tile = placed([P, T2], F32, "base%d" % t, BASE_KIB[t])
+            tile = placed([P, T2], F32, "base%d" % t, BASE_AT[t])
             nc.sync.dma_start(tile[:], base[cols(t, P), :])
             return tile
 
-        late_area = placed([P, LATE_KIB * 1024], U8, "late_area", 48)
+        late_area = placed([P, LATE_KIB * 1024], U8, "late_area", LATE_AT)
         tab_scale_rows = late_area[:, 0:T]
         nc.gpsimd.memset(tab_scale_rows.bitcast(I32), 0)
         vec_rows = keep.tile([P, P], F32, name="vec_rows")
@@ -101,11 +114,11 @@ def tile_list_pump_dock_check_kernel(tc, tab_words, tab_scales, offs, w1_words, 
         ident = keep.tile([P, P], F32, name="ident")
         make_identity(nc, ident[:])
 
-        offs_sb = load_list(offs, "offs_sb")
         def load_w1_scales(q):
             nc.sync.dma_start(w1_sc[32 * q : 32 * q + 4, :, :].bitcast(I32),
                               w1_scales[:, 4 * q : 4 * q + 4, :].rearrange("a r c -> r a c").bitcast(I32))
 
+        offs_sb = load_list(offs, "offs_sb")
         table = [load_table(0)]
         offs2_sb = load_list(offs2, "offs2_sb")
         offs3_sb = load_list(offs3, "offs3_sb")
@@ -116,40 +129,39 @@ def tile_list_pump_dock_check_kernel(tc, tab_words, tab_scales, offs, w1_words, 
         table.append(load_table(1))
         for q in range(1, QUADS):
             load_w1_scales(q)
-        w2_raw = load_w2(0, 1)
+        w2_raw = [load_w2(0)]
         w1_view = w1_words.rearrange("a p c -> p a c")
         w1_first = keep.tile([P, PASSES, 2 * P], U8, name="w1_first", align_bytes=64)
         nc.sync.dma_start(w1_first[:].bitcast(I32), w1_view[:, :, 0 : 2 * P].bitcast(I32))
         table.append(load_table(2))
 
-        v = [keep.tile([P, S], U32, name="v%d" % a, tag="words%d" % a, align_bytes=64) for a in range(2)]
-        for a in range(2):
+        v = [keep.tile([P, S], U32, name="v%d" % a, tag="words%d" % a, align_bytes=64) for a in range(PASSES - 1)]
+        for a in range(PASSES - 1):
             nc.vector.tensor_copy(v[a][:], table[a][:].indirect(offs_sb[:]))
-        v_sc = [placed([P, S], U8, "v_sc0", 16)] + moved_sc
+        v_sc = [placed([P, S], U8, "v_sc0", GATHERED_SCALES_AT)] + moved_sc
         nc.vector.tensor_copy(v_sc[0][:], tab_scale_rows.indirect(offs_sb[:]))
         for a in range(1, PASSES):
             nc.sync.dma_start(v_sc[a][0:SHIFT_ROWS, :].bitcast(I32),
                               v_sc[0][4 * a : 4 * a + SHIFT_ROWS, :].bitcast(I32))
 
-        wgs_sb = placed([P, S], F32, "wgs_sb", 56)
+        wgs_sb = placed([P, S], F32, "wgs_sb", WGS_AT)
         nc.sync.dma_start(wgs_sb[:, cols(0, HALF)], wgs[:, cols(0, HALF)])
-        w2_raw.extend(load_w2(1, 1))
-        w1_rest = placed([P, PASSES, 2 * (H - P)], U8, "w1_rest", 78)
+        w2_raw.append(load_w2(1))
+        w1_rest = placed([P, PASSES, 2 * (H - P)], U8, "w1_rest", W1_REST_AT)
         nc.sync.dma_start(w1_rest[:].bitcast(I32), w1_view[:, :, 2 * P : 2 * H].bitcast(I32))
         nc.sync.dma_start(wgs_sb[:, cols(1, HALF)], wgs[:, cols(1, HALF)])
-        w2_raw.extend(load_w2(2, 1))
-        w2_raw.extend(load_w2(3, 1))
+        w2_raw.extend(load_w2(t) for t in range(2, ROW_TILES))
 
-        vec_bank = bank(7, "vec_bank")
+        vec_bank = bank(BANKS - 1, "vec_bank")
         nc.tensor.transpose(vec_bank[:, 0:P], vec_rows[:], ident[:])
-        vecs = keep.tile([P, 8], F32, name="vecs")
-        nc.scalar.copy(vecs[:], vec_bank[:, 0:8])
+        vecs = keep.tile([P, 2 * ROW_TILES], F32, name="vecs")
+        nc.scalar.copy(vecs[:], vec_bank[:, 0 : 2 * ROW_TILES])
 
         pages = [keep.tile([P, T2], F32, name="page%d" % i) for i in range(2)]
         for tile in pages:
             nc.vector.memset(tile[:], 0.0)
-        warm = keep.tile([P, 1], F32, name="warm")
-        nc.scalar.activation(warm[:], pages[0][:, 0:1], ACT.Tanh)
+        table_preload = keep.tile([P, 1], F32, name="warm")
+        nc.scalar.activation(table_preload[:], pages[0][:, 0:1], ACT.Tanh)
 
         w2_q = []
         w2_grouped = []
@@ -158,7 +170,7 @@ def tile_list_pump_dock_check_kernel(tc, tab_words, tab_scales, offs, w1_words, 
             grouped = keep.tile([P, PASSES, P, 4], BF16, name="w2_grouped%d" % t, tag=slot, align_bytes=64)
             for a in range(PASSES):
                 nc.scalar.copy(grouped[:, a, :, :].rearrange("p (c i) j -> p c j i", i=4),
-                               w2_raw[t][a].rearrange("p j (c i) -> p c j i", i=4))
+                               w2_raw[t][a][:].rearrange("p j (c i) -> p c j i", i=4))
             w2_grouped.append(grouped)
 
         def quantize_w2(t, codes):
@@ -169,18 +181,18 @@ def tile_list_pump_dock_check_kernel(tc, tab_words, tab_scales, offs, w1_words, 
             w2_q.append((codes, scales))
 
         round_w2(0, "words2")
-        quantize_w2(0, placed([P, PASSES * P], U32, "first_codes", 86))
+        quantize_w2(0, placed([P, PASSES * P], U32, "first_codes", FIRST_CODES_AT))
         base_sb = [load_base(t) for t in range(ROW_TILES)]
-        w3_sb = placed([P, N], U32, "w3_sb", 88)
-        w3_sc = placed([P, N], U8, "w3_sc", 90)
+        w3_sb = placed([P, N], U32, "w3_sb", W3_AT)
+        w3_sc = placed([P, N], U8, "w3_sc", W3_SCALES_AT)
         nc.vector.memset(w3_sc[:].bitcast(I32), 0)
-        limit_rows = placed([P, P], F32, "limit_rows", 91)
+        limit_rows = placed([P, P], F32, "limit_rows", LIMIT_AT)
         nc.vector.memset(limit_rows[:], 0.0)
         nc.sync.dma_start(w3_sb[:].bitcast(I32), w3_words[0].rearrange("p c i -> p (c i)").bitcast(I32))
         for q in range(QUADS):
             nc.sync.dma_start(w3_sc[32 * q : 32 * q + 4, :].bitcast(I32), w3_scales[0, 4 * q : 4 * q + 4, :].bitcast(I32))
         nc.sync.dma_start(limit_rows[0:OUT_TILES, :], limit.rearrange("(t p) -> t p", p=P))
-        wgo_sb = placed([P, S], F32, "wgo_sb", 82)
+        wgo_sb = placed([P, S], F32, "wgo_sb", WGO_AT)
         nc.sync.dma_start(wgo_sb[:], wgo)
 
         outs = [keep.tile([P, T2], F32, name="out_page%d" % i) for i in range(2)]
@@ -227,19 +239,18 @@ def tile_list_pump_dock_check_kernel(tc, tab_words, tab_scales, offs, w1_words, 
             return ap.rearrange("p (g w) -> p g w", w=32)
 
         def tanh_of_sum(t, h, a_bank, sq):
-            u = z_t[h][:, :, cols((t - 1) % ROW_TILES, 32)]
-            nc.vector.scalar_tensor_tensor(u, runs(sq[:]), vecs[:, t : t + 1], runs(a_bank[:]), ALU.mult, ALU.add)
+            total = z_t[h][:, :, cols((t - 1) % ROW_TILES, 32)]
+            nc.vector.scalar_tensor_tensor(total, runs(sq[:]), vecs[:, t : t + 1], runs(a_bank[:]), ALU.mult, ALU.add)
             tile = keep.tile([P, HALF], F32, name="th%d_%d" % (t, h), tag="th%d" % h)
-            nc.scalar.activation(runs(tile[:]), u, ACT.Tanh)
+            nc.scalar.activation(runs(tile[:]), total, ACT.Tanh)
             th[h] = tile
 
-        def weigh(t, lo, hi, slot):
-            if slot is None:
-                gw = placed([P, HALF], F32, "gw_second", 64)
-            else:
-                gw = keep.tile([P, (hi - lo) * HALF], F32, name="gw%d_%d" % (t, lo), tag=slot, align_bytes=64)
-            nc.scalar.mul(gw[:], wgs_sb[:, lo * HALF : hi * HALF], vecs[:, 4 + t : 5 + t])
+        def weigh(t, gw, span):
+            nc.scalar.mul(gw[:], wgs_sb[:, span], vecs[:, ROW_TILES + t : ROW_TILES + t + 1])
             return gw
+
+        def weight_tile(t, width):
+            return keep.tile([P, width], F32, name="gw%d_0" % t, tag=WEIGHT_SLOTS[t], align_bytes=64)
 
         def place(t, h, gw):
             nc.vector.tensor_tensor(pages[t % 2][:].indirect(half_of(offs2_sb, h)), th[h][:], gw, ALU.mult)
@@ -251,10 +262,10 @@ def tile_list_pump_dock_check_kernel(tc, tab_words, tab_scales, offs, w1_words, 
             nc.scalar.mul(tile[:], limit_bank[:, 0:OUT_TILES], -1.0)
             neg_limit.append(tile)
 
-        def add_transposed(banks, src, first, ident):
+        def add_transposed(banks, src, first, identity):
             for c in range(CHUNKS):
                 for s in range(SUBS):
-                    nc.tensor.matmul(banks[c][:, cols(s, P)], src[:, cols(c * SUBS + s, P)], ident[:], is_transpose=True,
+                    nc.tensor.matmul(banks[c][:, cols(s, P)], src[:, cols(c * SUBS + s, P)], identity[:], is_transpose=True,
                                      start=(s == 0 and first), stop=(s == SUBS - 1 and not first))
 
         def round_sum(t, c, sum_bank, engine_copy):
@@ -264,19 +275,13 @@ def tile_list_pump_dock_check_kernel(tc, tab_words, tab_scales, offs, w1_words, 
                         sum_bank[:].rearrange("q (s p u e) -> q s u p e", s=SUBS, u=2, e=2))
 
         def add_base(t):
-            if t == ROW_TILES - 1:
-                warm_bank = bank(7, "warm_bank")
-                codes, scales = w2_q[t]
-                for i in range(WARM_PASSES):
-                    nc.tensor.matmul_mx(out=warm_bank[:], lhsT=codes[:, 0:P].bitcast(FP8X4), lhsT_scale=scales[:, 0:P],
-                                        rhs=v[0][:, 0:HALF].bitcast(FP8X4), rhs_scale=v_sc[0][:, 0:HALF], start=True, stop=True)
-            banks = [bank(4 + c, "sum_bank") for c in range(CHUNKS)]
+            banks = [bank(SUM_BANK + c, "sum_bank") for c in range(CHUNKS)]
             add_transposed(banks, base_sb[t], True, ident)
-            late = ident
+            page_ident = ident
             if t == ROW_TILES - 1:
-                late = placed([P, P], F32, "late_ident", BASE_KIB[t])
-                nc.scalar.copy(late[:], ident[:])
-            add_transposed(banks, pages[t % 2], False, late)
+                page_ident = placed([P, P], F32, "late_ident", BASE_AT[t])
+                nc.scalar.copy(page_ident[:], ident[:])
+            add_transposed(banks, pages[t % 2], False, page_ident)
             return banks
 
         a_banks = [bank(HALVES + h, "a_bank") for h in range(HALVES)]
@@ -285,18 +290,18 @@ def tile_list_pump_dock_check_kernel(tc, tab_words, tab_scales, offs, w1_words, 
             pass_a(0, h, 0, a_banks[h])
             for a in range(PASSES - 1):
                 pass_b(0, h, a, b_banks[h])
-        gw = weigh(0, 0, 1, WEIGHT_SLOTS[0])
+        gw = weigh(0, weight_tile(0, HALF), cols(0, HALF))
         for h in range(HALVES):
             pass_a(0, h, 1, a_banks[h])
             pass_b(0, h, PASSES - 1, b_banks[h])
             pass_a(0, h, PASSES - 1, a_banks[h])
             tanh_of_sum(0, h, a_banks[h], square(0, h, b_banks[h]))
         place(0, 0, gw[:])
-        round_w2(1, "slot_a")
+        round_w2(1, SQUARE_SLOTS[0][0])
         quantize_w2(1, keep.tile([P, PASSES * P], U32, name="w2_codes1", align_bytes=64))
-        place(0, 1, weigh(0, 1, 2, None)[:])
-        round_w2(2, "slot_b")
-        gw = weigh(1, 0, 2, WEIGHT_SLOTS[1])
+        place(0, 1, weigh(0, placed([P, HALF], F32, "gw_second", SECOND_WEIGHTS_AT), cols(1, HALF))[:])
+        round_w2(2, SQUARE_SLOTS[0][1])
+        gw = weigh(1, weight_tile(1, S), cols(0, S))
         for t in range(1, ROW_TILES):
             a_banks = [product_a(t, h) for h in range(HALVES)]
             squares = [square_of_b(t, h) for h in range(HALVES)]
@@ -305,19 +310,19 @@ def tile_list_pump_dock_check_kernel(tc, tab_words, tab_scales, offs, w1_words, 
                 tanh_of_sum(t, h, a_banks[h], squares[h])
             if t + 1 < ROW_TILES:
                 quantize_w2(t + 1, keep.tile([P, PASSES * P], U32, name="w2_codes%d" % (t + 1), tag=SQUARE_SLOTS[t][1], align_bytes=64))
-            if t == 1:
-                round_w2(3, "slot_b")
+            if t + 2 < ROW_TILES:
+                round_w2(t + 2, SQUARE_SLOTS[0][1])
             place(t, 0, gw[:, cols(0, HALF)])
             if t + 1 < ROW_TILES:
                 place(t, 1, gw[:, cols(1, HALF)])
-                gw = weigh(t + 1, 0, 2, WEIGHT_SLOTS[t + 1])
+                gw = weigh(t + 1, weight_tile(t + 1, S), cols(0, S))
             for c in range(CHUNKS):
                 round_sum(t - 1, c, sum_banks[c], nc.scalar.copy)
         negate_limits()
         place(ROW_TILES - 1, 1, gw[:, cols(1, HALF)])
         sum_banks = add_base(ROW_TILES - 1)
 
-        y = [placed([P, T2], F32, "y%d" % n, 8 * n) for n in range(OUT_TILES)]
+        y = [placed([P, T2], F32, "y%d" % n, PAGE_KIB * n) for n in range(OUT_TILES)]
         z_q = []
 
         def product(n, lo, width, bank_no, engine_copy):
@@ -336,27 +341,27 @@ def tile_list_pump_dock_check_kernel(tc, tab_words, tab_scales, offs, w1_words, 
             scales = keep.tile([P, CHUNK], U8, name="z_scales%d" % c, align_bytes=64)
             pieces = ((0, 2), (2, 2)) if c + 1 < CHUNKS else ((0, 2), (2, 1), (3, 1))
             for i, (first, count) in enumerate(pieces):
-                back = bank((2 * c + i) % 8, "back_bank")
+                back = bank((2 * c + i) % BANKS, "back_bank")
                 for j in range(2 * count):
-                    nc.tensor.transpose(back[:, cols(j, P)], z_t[c // 2][:, 8 * (c % 2) + 2 * first + j, :], ident[:])
+                    nc.tensor.transpose(back[:, cols(j, P)], z_t[c // 2][:, 2 * SUBS * (c % 2) + 2 * first + j, :], ident[:])
                 z = ring.tile([P, count * P * 4], BF16, name="z", tag="z%d" % (i % 2), align_bytes=64)
-                z_words = z[:].bitcast(F32).rearrange("p (s q u) -> p s q u", s=count, u=2)
+                z_pairs = z[:].bitcast(F32).rearrange("p (s q u) -> p s q u", s=count, u=2)
                 src = back[:, 0 : 2 * count * P].rearrange("p (s u q) -> p s q u", s=count, u=2)
                 if i + 1 == len(pieces) and c % 2 == 1:
-                    nc.vector.tensor_copy(z_words, src)
+                    nc.vector.tensor_copy(z_pairs, src)
                 else:
-                    nc.scalar.copy(z_words, src)
+                    nc.scalar.copy(z_pairs, src)
                 span = slice(first * P, (first + count) * P)
                 nc.vector.quantize_mx(out=codes[:, span].bitcast(FP8X4), scales=scales[:, span], in_=z[:])
             z_q.append((codes, scales))
         for c in range(CHUNKS - 1):
             product(0, c * CHUNK, CHUNK, 1 + c, nc.scalar.copy)
-        product(0, T2 - CHUNK, 2 * P, 4, nc.vector.tensor_copy)
-        product(0, T2 - 2 * P, P, 5, nc.vector.tensor_copy)
-        product(0, T2 - P, P, 6, nc.vector.tensor_copy)
+        product(0, T2 - CHUNK, 2 * P, CHUNKS, nc.vector.tensor_copy)
+        product(0, T2 - 2 * P, P, CHUNKS + 1, nc.vector.tensor_copy)
+        product(0, T2 - P, P, CHUNKS + 2, nc.vector.tensor_copy)
         for n in range(1, OUT_TILES):
             for c in range(CHUNKS):
-                product(n, c * CHUNK, CHUNK, (4 * n + 3 + c) % 8, nc.scalar.copy)
+                product(n, c * CHUNK, CHUNK, (CHUNKS * n + 3 + c) % BANKS, nc.scalar.copy)
 
         picked = []
         for n in range(OUT_TILES):

@@ -160,8 +160,6 @@ def tile_list_pump_dock_check_kernel(tc, tab_words, tab_scales, offs, w1_words, 
         pages = [keep.tile([P, T2], F32, name="page%d" % i) for i in range(2)]
         for tile in pages:
             nc.vector.memset(tile[:], 0.0)
-        table_preload = keep.tile([P, 1], F32, name="warm")
-        nc.scalar.activation(table_preload[:], pages[0][:, 0:1], ACT.Tanh)
 
         w2_q = []
         w2_grouped = []

@@ -28,7 +28,7 @@ CHUNK = 512
 CHUNKS = T2 // CHUNK
 SUBS = CHUNK // P
 QUADS = 4
-SHIFT_ROWS = 112
+SHIFT_ROWS = 100
 BANKS = 8
 SUM_BANK = 4
 

from contextlib import ExitStack

import concourse.mybir as mybir
from concourse.masks import make_identity

K, T, S, H, N, T2 = 1536, 4096, 1024, 512, 384, 2048
FLOPS = 2 * 2 * K * H * S + 2 * H * N * T2

F32 = mybir.dt.float32
BF16 = mybir.dt.bfloat16
I32 = mybir.dt.int32
U32 = mybir.dt.uint32
U16 = mybir.dt.uint16
U8 = mybir.dt.uint8
FP8X4 = mybir.dt.float8_e4m3fn_x4
FP4X4 = mybir.dt.float4_e2m1fn_x4
ACT = mybir.ActivationFunctionType
ALU = mybir.AluOpType

P = 128
PASSES = K // 512
ROW_TILES = H // P
OUT_TILES = N // P
HALF = 512
HALVES = S // HALF
LIST_COLS = HALF // 16
CHUNK = 512
CHUNKS = T2 // CHUNK
SUBS = CHUNK // P
QUADS = 4
SHIFT_ROWS = 100
BANKS = 8
SUM_BANK = 4

SQUARE_SLOTS = (("slot_a", "slot_b"), ("slot_c", "slot_d"), ("slot_e", "slot_f"), ("slot_a", "slot_b"))
WEIGHT_SLOTS = ("slot_e", "slot_a", "slot_c", "slot_e")

TABLE_KIB = 16
PAGE_KIB = 8
LATE_AT, LATE_KIB = 48, 52
GATHERED_SCALES_AT = 16
BASE_AT = (32, 40, 48, 92)
WGS_AT = 56
W2_RAW_AT = 60
SECOND_WEIGHTS_AT = 64
W1_REST_AT = 78
WGO_AT = 82
FIRST_CODES_AT = 86
W3_AT, W3_SCALES_AT, LIMIT_AT = 88, 90, 91


def tile_list_pump_dock_check_kernel(tc, tab_words, tab_scales, offs, w1_words, w1_scales, w2, curve, gain,
                                               offs2, wgs, base, w3_words, w3_scales, offs3, limit, offs4, wgo, out):
    nc = tc.nc
    with ExitStack() as ctx:
        lists = ctx.enter_context(tc.tile_pool(name="lists", bufs=1))
        keep = ctx.enter_context(tc.tile_pool(name="keep", bufs=1))
        ring = ctx.enter_context(tc.tile_pool(name="ring", bufs=2))
        arena = ctx.enter_context(tc.tile_pool(name="arena", bufs=1))
        psum = ctx.enter_context(tc.psum_pool(name="psum", bufs=1))

        def placed(shape, dtype, name, kib):
            return arena.tile(shape, dtype, name=name, offset=kib * 1024, align_bytes=64)

        def bank(i, name):
            return psum.tile([P, 512], F32, name=name, tag="bank%d" % i)

        def load_list(src, name):
            tile = lists.tile([P, S // 16], U16, name=name)
            nc.sync.dma_start(tile[:], src)
            return tile

        def half_of(tile, h):
            return tile[:, h * LIST_COLS : (h + 1) * LIST_COLS]

        def cols(i, width):
            return slice(i * width, (i + 1) * width)

        def load_table(a):
            tile = placed([P, T], U32, "table%d" % a, TABLE_KIB * a)
            nc.sync.dma_start(tile[:].bitcast(I32), tab_words[a].rearrange("p t i -> p (t i)").bitcast(I32))
            return tile

        def load_w2(t):
            tiles = []
            for a in range(PASSES):
                if t == 0:
                    tile = keep.tile([P, 4, P], F32, name="w2_raw0_%d" % a, align_bytes=64)
                else:
                    tile = placed([P, 4, P], F32, "w2_raw%d_%d" % (t, a), W2_RAW_AT + 2 * (PASSES * (t - 1) + a))
                nc.sync.dma_start(tile[:], w2[cols(a, 512), cols(t, P)].rearrange("(p j) c -> p j c", j=4))
                tiles.append(tile)
            return tiles

        def load_base(t):
            tile = placed([P, T2], F32, "base%d" % t, BASE_AT[t])
            nc.sync.dma_start(tile[:], base[cols(t, P), :])
            return tile

        late_area = placed([P, LATE_KIB * 1024], U8, "late_area", LATE_AT)
        tab_scale_rows = late_area[:, 0:T]
        nc.gpsimd.memset(tab_scale_rows.bitcast(I32), 0)
        vec_rows = keep.tile([P, P], F32, name="vec_rows")
        nc.vector.memset(vec_rows[:], 0.0)
        w1_sc = keep.tile([P, PASSES, H], U8, name="w1_sc", align_bytes=64)
        nc.vector.memset(w1_sc[:].rearrange("p a c -> p (a c)").bitcast(I32), 0)
        for q in range(QUADS):
            nc.gpsimd.dma_start(late_area[32 * q : 32 * q + 4 * PASSES, 0:T].bitcast(I32),
                                tab_scales[:, 4 * q : 4 * q + 4, :].bitcast(I32))
        moved_sc = [keep.tile([P, S], U8, name="v_sc%d" % a, align_bytes=64) for a in range(1, PASSES)]
        for tile in moved_sc:
            nc.vector.memset(tile[:].bitcast(I32), 0)

        ident = keep.tile([P, P], F32, name="ident")
        make_identity(nc, ident[:])

        def load_w1_scales(q):
            nc.sync.dma_start(w1_sc[32 * q : 32 * q + 4, :, :].bitcast(I32),
                              w1_scales[:, 4 * q : 4 * q + 4, :].rearrange("a r c -> r a c").bitcast(I32))

        offs_sb = load_list(offs, "offs_sb")
        table = [load_table(0)]
        offs2_sb = load_list(offs2, "offs2_sb")
        offs3_sb = load_list(offs3, "offs3_sb")
        offs4_sb = load_list(offs4, "offs4_sb")
        nc.sync.dma_start(vec_rows[0:4, :], curve.rearrange("(t p) -> t p", p=P))
        nc.sync.dma_start(vec_rows[4:8, :], gain.rearrange("(t p) -> t p", p=P))
        load_w1_scales(0)
        table.append(load_table(1))
        for q in range(1, QUADS):
            load_w1_scales(q)
        w2_raw = [load_w2(0)]
        w1_view = w1_words.rearrange("a p c -> p a c")
        w1_first = keep.tile([P, PASSES, 2 * P], U8, name="w1_first", align_bytes=64)
        nc.sync.dma_start(w1_first[:].bitcast(I32), w1_view[:, :, 0 : 2 * P].bitcast(I32))
        table.append(load_table(2))

        v = [keep.tile([P, S], U32, name="v%d" % a, tag="words%d" % a, align_bytes=64) for a in range(PASSES - 1)]
        for a in range(PASSES - 1):
            nc.vector.tensor_copy(v[a][:], table[a][:].indirect(offs_sb[:]))
        v_sc = [placed([P, S], U8, "v_sc0", GATHERED_SCALES_AT)] + moved_sc
        nc.vector.tensor_copy(v_sc[0][:], tab_scale_rows.indirect(offs_sb[:]))
        for a in range(1, PASSES):
            nc.sync.dma_start(v_sc[a][0:SHIFT_ROWS, :].bitcast(I32),
                              v_sc[0][4 * a : 4 * a + SHIFT_ROWS, :].bitcast(I32))

        wgs_sb = placed([P, S], F32, "wgs_sb", WGS_AT)
        nc.sync.dma_start(wgs_sb[:, cols(0, HALF)], wgs[:, cols(0, HALF)])
        w2_raw.append(load_w2(1))
        w1_rest = placed([P, PASSES, 2 * (H - P)], U8, "w1_rest", W1_REST_AT)
        nc.sync.dma_start(w1_rest[:].bitcast(I32), w1_view[:, :, 2 * P : 2 * H].bitcast(I32))
        nc.sync.dma_start(wgs_sb[:, cols(1, HALF)], wgs[:, cols(1, HALF)])
        w2_raw.extend(load_w2(t) for t in range(2, ROW_TILES))

        vec_bank = bank(BANKS - 1, "vec_bank")
        nc.tensor.transpose(vec_bank[:, 0:P], vec_rows[:], ident[:])
        vecs = keep.tile([P, 2 * ROW_TILES], F32, name="vecs")
        nc.scalar.copy(vecs[:], vec_bank[:, 0 : 2 * ROW_TILES])

        pages = [keep.tile([P, T2], F32, name="page%d" % i) for i in range(2)]
        for tile in pages:
            nc.vector.memset(tile[:], 0.0)

        w2_q = []
        w2_grouped = []

        def round_w2(t, slot):
            grouped = keep.tile([P, PASSES, P, 4], BF16, name="w2_grouped%d" % t, tag=slot, align_bytes=64)
            for a in range(PASSES):
                nc.scalar.copy(grouped[:, a, :, :].rearrange("p (c i) j -> p c j i", i=4),
                               w2_raw[t][a][:].rearrange("p j (c i) -> p c j i", i=4))
            w2_grouped.append(grouped)

        def quantize_w2(t, codes):
            scales = keep.tile([P, PASSES * P], U8, name="w2_scales%d" % t, align_bytes=64)
            flat = w2_grouped[t][:].rearrange("p a c j -> p (a c j)")
            for lo, hi in ((0, 2 * P), (2 * P, 3 * P)):
                nc.vector.quantize_mx(out=codes[:, lo:hi].bitcast(FP8X4), scales=scales[:, lo:hi], in_=flat[:, 4 * lo : 4 * hi])
            w2_q.append((codes, scales))

        round_w2(0, "words2")
        quantize_w2(0, placed([P, PASSES * P], U32, "first_codes", FIRST_CODES_AT))
        base_sb = [load_base(t) for t in range(ROW_TILES)]
        w3_sb = placed([P, N], U32, "w3_sb", W3_AT)
        w3_sc = placed([P, N], U8, "w3_sc", W3_SCALES_AT)
        nc.vector.memset(w3_sc[:].bitcast(I32), 0)
        limit_rows = placed([P, P], F32, "limit_rows", LIMIT_AT)
        nc.vector.memset(limit_rows[:], 0.0)
        nc.sync.dma_start(w3_sb[:].bitcast(I32), w3_words[0].rearrange("p c i -> p (c i)").bitcast(I32))
        for q in range(QUADS):
            nc.sync.dma_start(w3_sc[32 * q : 32 * q + 4, :].bitcast(I32), w3_scales[0, 4 * q : 4 * q + 4, :].bitcast(I32))
        nc.sync.dma_start(limit_rows[0:OUT_TILES, :], limit.rearrange("(t p) -> t p", p=P))
        wgo_sb = placed([P, S], F32, "wgo_sb", WGO_AT)
        nc.sync.dma_start(wgo_sb[:], wgo)

        outs = [keep.tile([P, T2], F32, name="out_page%d" % i) for i in range(2)]
        for tile in outs:
            nc.vector.memset(tile[:], 0.0)
        v.append(keep.tile([P, S], U32, name="v2", tag="words2", align_bytes=64))
        for h in range(HALVES):
            nc.vector.tensor_copy(v[2][:, cols(h, HALF)], table[2][:].indirect(half_of(offs_sb, h)))

        z_t = [keep.tile([P, 2 * SUBS * 2, P], F32, name="z_t%d" % i, align_bytes=64) for i in range(2)]
        th = {}
        neg_limit = []

        def pass_a(t, h, a, a_bank):
            w1_cols = w1_first[:, a, :] if t == 0 else w1_rest[:, a, cols(t - 1, 2 * P)]
            nc.tensor.matmul_mx(out=a_bank[:], lhsT=w1_cols.bitcast(FP4X4), lhsT_scale=w1_sc[:, a, cols(t, P)],
                                rhs=v[a][:, cols(h, HALF)].bitcast(FP8X4), rhs_scale=v_sc[a][:, cols(h, HALF)],
                                start=(a == 0), stop=(a == PASSES - 1))

        def pass_b(t, h, a, b_bank):
            codes, scales = w2_q[t]
            nc.tensor.matmul_mx(out=b_bank[:], lhsT=codes[:, cols(a, P)].bitcast(FP8X4), lhsT_scale=scales[:, cols(a, P)],
                                rhs=v[a][:, cols(h, HALF)].bitcast(FP8X4), rhs_scale=v_sc[0][4 * a : P, cols(h, HALF)],
                                start=(a == 0), stop=(a == PASSES - 1))

        def product_a(t, h):
            a_bank = bank(HALVES * ((t + 1) % 2) + h, "a_bank")
            for a in range(PASSES):
                pass_a(t, h, a, a_bank)
            return a_bank

        def square(t, h, b_bank):
            sq = keep.tile([P, HALF], F32, name="sq%d_%d" % (t, h), tag=SQUARE_SLOTS[t][h], align_bytes=64)
            nc.scalar.activation(sq[:], b_bank[:], ACT.Square)
            return sq

        def square_of_b(t, h):
            b_bank = bank(HALVES * (t % 2) + h, "b_bank")
            for a in range(PASSES):
                pass_b(t, h, a, b_bank)
            return square(t, h, b_bank)

        def runs(ap):
            return ap.rearrange("p (g w) -> p g w", w=32)

        def tanh_of_sum(t, h, a_bank, sq):
            total = z_t[h][:, :, cols((t - 1) % ROW_TILES, 32)]
            nc.vector.scalar_tensor_tensor(total, runs(sq[:]), vecs[:, t : t + 1], runs(a_bank[:]), ALU.mult, ALU.add)
            tile = keep.tile([P, HALF], F32, name="th%d_%d" % (t, h), tag="th%d" % h)
            nc.scalar.activation(runs(tile[:]), total, ACT.Tanh)
            th[h] = tile

        def weigh(t, gw, span):
            nc.scalar.mul(gw[:], wgs_sb[:, span], vecs[:, ROW_TILES + t : ROW_TILES + t + 1])
            return gw

        def weight_tile(t, width):
            return keep.tile([P, width], F32, name="gw%d_0" % t, tag=WEIGHT_SLOTS[t], align_bytes=64)

        def place(t, h, gw):
            nc.vector.tensor_tensor(pages[t % 2][:].indirect(half_of(offs2_sb, h)), th[h][:], gw, ALU.mult)

        def negate_limits():
            limit_bank = bank(0, "limit_bank")
            nc.tensor.transpose(limit_bank[:, 0:P], limit_rows[:], ident[:])
            tile = keep.tile([P, OUT_TILES], F32, name="neg_limit")
            nc.scalar.mul(tile[:], limit_bank[:, 0:OUT_TILES], -1.0)
            neg_limit.append(tile)

        def add_transposed(banks, src, first, identity):
            for c in range(CHUNKS):
                for s in range(SUBS):
                    nc.tensor.matmul(banks[c][:, cols(s, P)], src[:, cols(c * SUBS + s, P)], identity[:], is_transpose=True,
                                     start=(s == 0 and first), stop=(s == SUBS - 1 and not first))

        def round_sum(t, c, sum_bank, engine_copy):
            halves = z_t[c // 2][:].rearrange("q g w -> q (g w)").bitcast(BF16).rearrange(
                "q (c s u p e) -> q c s u p e", c=2, s=SUBS, u=2, e=2)
            engine_copy(halves[:, c % 2, :, :, cols(t, 32), :],
                        sum_bank[:].rearrange("q (s p u e) -> q s u p e", s=SUBS, u=2, e=2))

        def add_base(t):
            banks = [bank(SUM_BANK + c, "sum_bank") for c in range(CHUNKS)]
            add_transposed(banks, base_sb[t], True, ident)
            page_ident = ident
            if t == ROW_TILES - 1:
                page_ident = placed([P, P], F32, "late_ident", BASE_AT[t])
                nc.scalar.copy(page_ident[:], ident[:])
            add_transposed(banks, pages[t % 2], False, page_ident)
            return banks

        a_banks = [bank(HALVES + h, "a_bank") for h in range(HALVES)]
        b_banks = [bank(h, "b_bank") for h in range(HALVES)]
        for h in range(HALVES):
            pass_a(0, h, 0, a_banks[h])
            for a in range(PASSES - 1):
                pass_b(0, h, a, b_banks[h])
        gw = weigh(0, weight_tile(0, HALF), cols(0, HALF))
        for h in range(HALVES):
            pass_a(0, h, 1, a_banks[h])
            pass_b(0, h, PASSES - 1, b_banks[h])
            pass_a(0, h, PASSES - 1, a_banks[h])
            tanh_of_sum(0, h, a_banks[h], square(0, h, b_banks[h]))
        place(0, 0, gw[:])
        round_w2(1, SQUARE_SLOTS[0][0])
        quantize_w2(1, keep.tile([P, PASSES * P], U32, name="w2_codes1", align_bytes=64))
        place(0, 1, weigh(0, placed([P, HALF], F32, "gw_second", SECOND_WEIGHTS_AT), cols(1, HALF))[:])
        round_w2(2, SQUARE_SLOTS[0][1])
        gw = weigh(1, weight_tile(1, S), cols(0, S))
        for t in range(1, ROW_TILES):
            a_banks = [product_a(t, h) for h in range(HALVES)]
            squares = [square_of_b(t, h) for h in range(HALVES)]
            sum_banks = add_base(t - 1)
            for h in range(HALVES):
                tanh_of_sum(t, h, a_banks[h], squares[h])
            if t + 1 < ROW_TILES:
                quantize_w2(t + 1, keep.tile([P, PASSES * P], U32, name="w2_codes%d" % (t + 1), tag=SQUARE_SLOTS[t][1], align_bytes=64))
            if t + 2 < ROW_TILES:
                round_w2(t + 2, SQUARE_SLOTS[0][1])
            place(t, 0, gw[:, cols(0, HALF)])
            if t + 1 < ROW_TILES:
                place(t, 1, gw[:, cols(1, HALF)])
                gw = weigh(t + 1, weight_tile(t + 1, S), cols(0, S))
            for c in range(CHUNKS):
                round_sum(t - 1, c, sum_banks[c], nc.scalar.copy)
        negate_limits()
        place(ROW_TILES - 1, 1, gw[:, cols(1, HALF)])
        sum_banks = add_base(ROW_TILES - 1)

        y = [placed([P, T2], F32, "y%d" % n, PAGE_KIB * n) for n in range(OUT_TILES)]
        z_q = []

        def product(n, lo, width, bank_no, engine_copy):
            c, first = divmod(lo, CHUNK)
            codes, scales = z_q[c]
            y_bank = bank(bank_no, "y_bank")
            nc.tensor.matmul_mx(out=y_bank[:, 0:width], lhsT=w3_sb[:, cols(n, P)].bitcast(FP8X4), lhsT_scale=w3_sc[:, cols(n, P)],
                                rhs=codes[:, first : first + width].bitcast(FP8X4), rhs_scale=scales[:, first : first + width],
                                start=True, stop=True)
            engine_copy(y[n][:, lo : lo + width], y_bank[:, 0:width])

        for c in range(CHUNKS):
            round_sum(ROW_TILES - 1, c, sum_banks[c], nc.vector.tensor_copy if c % 2 == 1 else nc.scalar.copy)
        for c in range(CHUNKS):
            codes = keep.tile([P, CHUNK], U32, name="z_codes%d" % c, align_bytes=64)
            scales = keep.tile([P, CHUNK], U8, name="z_scales%d" % c, align_bytes=64)
            pieces = ((0, 2), (2, 2)) if c + 1 < CHUNKS else ((0, 2), (2, 1), (3, 1))
            for i, (first, count) in enumerate(pieces):
                back = bank((2 * c + i) % BANKS, "back_bank")
                for j in range(2 * count):
                    nc.tensor.transpose(back[:, cols(j, P)], z_t[c // 2][:, 2 * SUBS * (c % 2) + 2 * first + j, :], ident[:])
                z = ring.tile([P, count * P * 4], BF16, name="z", tag="z%d" % (i % 2), align_bytes=64)
                z_pairs = z[:].bitcast(F32).rearrange("p (s q u) -> p s q u", s=count, u=2)
                src = back[:, 0 : 2 * count * P].rearrange("p (s u q) -> p s q u", s=count, u=2)
                if i + 1 == len(pieces) and c % 2 == 1:
                    nc.vector.tensor_copy(z_pairs, src)
                else:
                    nc.scalar.copy(z_pairs, src)
                span = slice(first * P, (first + count) * P)
                nc.vector.quantize_mx(out=codes[:, span].bitcast(FP8X4), scales=scales[:, span], in_=z[:])
            z_q.append((codes, scales))
        for c in range(CHUNKS - 1):
            product(0, c * CHUNK, CHUNK, 1 + c, nc.scalar.copy)
        product(0, T2 - CHUNK, 2 * P, CHUNKS, nc.vector.tensor_copy)
        product(0, T2 - 2 * P, P, CHUNKS + 1, nc.vector.tensor_copy)
        product(0, T2 - P, P, CHUNKS + 2, nc.vector.tensor_copy)
        for n in range(1, OUT_TILES):
            for c in range(CHUNKS):
                product(n, c * CHUNK, CHUNK, (CHUNKS * n + 3 + c) % BANKS, nc.scalar.copy)

        picked = []
        for n in range(OUT_TILES):
            tile = keep.tile([P, S], F32, name="picked%d" % n, tag="words%d" % n, align_bytes=64)
            nc.vector.tensor_copy(tile[:], y[n][:].indirect(offs3_sb[:]))
            picked.append(tile)
        for n in range(OUT_TILES):
            size = keep.tile([P, S], F32, name="size", tag="size")
            nc.scalar.activation(size[:], picked[n][:], ACT.Abs)
            nc.scalar.activation(picked[n][:], size[:], ACT.Identity, bias=neg_limit[0][:, n : n + 1])
            nc.vector.tensor_tensor(outs[n % 2][:].indirect(offs4_sb[:]), picked[n][:], wgo_sb[:], ALU.mult)
            nc.sync.dma_start(out[cols(n, P), :], outs[n % 2][:])
